import numpy as np, ml_dtypes
CORES = [16,18,20,22]
N = 4
import mx_ref
BF = ml_dtypes.bfloat16
def gentries(a):
    return np.ascontiguousarray(a.reshape(8, 16, -1).transpose(0, 2, 1)).reshape(8, -1)
def gtable(e):
    e = np.asarray(e); return np.ascontiguousarray(e.reshape(8, -1, 16).transpose(0, 2, 1)).reshape(128, -1).astype(np.int32)
def gcols(t, e):
    v = np.concatenate([t.reshape(8, 16, -1, 4), np.zeros((8, 16, 1, 4), BF)], axis=2)
    return np.ascontiguousarray(np.stack([v[g][:, e[g]] for g in range(8)])).reshape(128, -1)
def tile(rs):
    return np.stack(rs, axis=2).reshape(128, -1).astype(BF)
def cut(t, i, w=512):
    return t[:, w * i:w * i + w]
def pick(q, e):
    c = np.concatenate([q[0].reshape(128, -1, 4), np.zeros((128, 1, 4), np.uint8)], axis=1); s = np.concatenate([q[1], np.ones((16, 1), np.uint8)], axis=1)
    return (np.ascontiguousarray(c[:, e].reshape(128, -1)), np.ascontiguousarray(s[:, e]))
def join(*qs):
    return (np.concatenate([q[0] for q in qs], axis=1), np.concatenate([q[1] for q in qs], axis=1))
def put(q, e, v):
    c, s = q[0].reshape(128, -1, 4).copy(), q[1].copy(); c[:, e] = v[0].reshape(128, -1, 4); s[:, e] = v[1]
    return (c.reshape(128, -1), s)
def pk(c, s):
    return (np.ascontiguousarray(c), mx_ref.live(s))
def emit(q):
    return q[0], q[1]
def packed(v, rng):
    q = [mx_ref.quantize(np.ascontiguousarray(v[r])) for r in range(N)]
    return np.stack([a for a, b in q]), np.stack([mx_ref.plane(b, rng) for a, b in q])
def values_of_codes():
    e, c = np.zeros((128, 128, 4), np.float32), np.zeros((128, 2, 4), np.uint8)
    e[np.arange(128), np.arange(128), 0] = 1
    c[:127, :, 0] = np.arange(256).reshape(2, 128).T[:127]
    return mx_ref.matmul(mx_ref.quantize(e.reshape(128, 512).astype(BF)), (c.reshape(128, 8), np.full((16, 2), 127, np.uint8))).T.reshape(-1).astype(np.float64)
CODE_VALUE, SCALE_VALUE = values_of_codes(), 2.0 ** (np.arange(256) - 127.0)
def decode(q):
    return (CODE_VALUE[q[0]].reshape(16, 8, -1, 4) * SCALE_VALUE[q[1]][:, None, :, None] + 0.0).reshape(128, -1).astype(np.float32)
def f(rng, *shape):
    return mx_ref.flush((rng.standard_normal(shape, dtype=np.float32) * np.exp2(rng.integers(-2, 3, shape[:-1] + (1,)))).astype(BF))
def wide(rng, *shape, cols=0):
    v = rng.standard_normal(shape, dtype=np.float32) * np.exp2(rng.integers(-12, 13, shape)).astype(np.float32)
    if cols: v *= np.repeat(np.exp2(rng.integers(-cols, cols + 1, shape[:-2] + (1, shape[-1] // 4))) * (rng.random(shape[:-2] + (1, shape[-1] // 4)) > 0.0625), 4, axis=-1).astype(np.float32)
    return mx_ref.flush(v.astype(BF))
C, P, E, T, R = 320, 48, 2, 96, 3
STEP = [1, 2, 1]
OPPOSITE = np.array([E * (P - 1 - q) + i for q in range(P) for i in range(E)])
def sow(n, s):
    o, m = np.zeros((8, C), int), np.zeros((8, P), int)
    for g in range(8):
        end = np.cumsum(n[g])
        mark = np.where(n[g] > 0, s[g][np.maximum(end - 1, 0)] + np.float32(0.0), np.float32(-np.inf))
        chosen = 4 * np.arange(P // 4) + np.argmax(mark.reshape(-1, 4), axis=1)
        pit = np.repeat(np.arange(P), n[g])
        k = np.arange(C) - (end - n[g])[pit]
        moved = np.isin(pit, chosen)
        to = np.where(moved, (pit + 1 + k) % P, pit)
        o[g] = np.lexsort((k, moved, to))
        m[g] = np.bincount(to, minlength=P)
    return o, m
def ends(n):
    i = np.arange(E)
    return np.where(i < n[:, :, None], np.cumsum(n, axis=1)[:, :, None] - 1 - i, -1).reshape(8, T)
def gput(t, e, h):
    a, b = t.reshape(8, 16, -1, 4).copy(), h.reshape(8, 16, -1, 4)
    for g in range(8):
        j = np.flatnonzero(e[g] >= 0)
        a[g][:, e[g][j]] = b[g][:, j]
    return a.reshape(128, -1)
def big(v):
    v = v.astype(np.float32)
    v[np.abs(v) < np.float32(2.0 ** -16)] = 0
    return v.astype(BF)
def numbers_of(rng):
    return {"x": big(f(rng, N, 128, 4 * C)), "u": np.array(f(rng, N, 128, 512)), "v": np.array(f(rng, N, 128, 512))}
def weights(rng, still=[]):
    w = big(f(rng, N, 128, 2048)).reshape(N, 8, 16, 4, 8, 16, 4)
    for i in still:
        w[:, :, i] = 0
        w[:, :, :, :, :, i] = 0
    c, p = packed(w.reshape(N, 128, 2048), rng)
    return {"wc": c, "ws": p}
def sizes(rng):
    n = np.zeros((N, 8, P), int)
    for r in range(N):
        for g in range(8):
            m = rng.integers(0, P, P)
            n[r, g] = np.bincount(m[rng.integers(0, P, C)], minlength=P)
    return n
def stored(n):
    return np.stack([gtable(a) for a in n])
def signs(rng):
    return np.stack([rng.permutation(8) % 2 * 2.0 - 1.0 for r in range(N)])
def setup_inputs(rng):
    return {**numbers_of(rng), **weights(rng), "sz": stored(sizes(rng))}
def setup_inputs_ties(rng):
    d = numbers_of(rng)
    e = rng.permutation(N)
    x = d["x"].reshape(N, 8, 16, C, 4)
    for r in range(N):
        k = np.zeros(C, int) if r == e[0] else rng.permutation(C) % 3
        a = x[r][:, :8, :3].copy()
        a[:, :, 2] = 0
        x[r][:, :8] = a[:, :, k]
    x[e[1]] = 0
    u = d["u"].reshape(N, 8, 16, 8, 16, 4)
    k = u.copy()
    u[:, :, :, :, 0] = 0
    for g in range(8): u[:, g, :8, g, 0] = k[:, g, :8, g, 0]
    return {"x": x.reshape(N, 128, 4 * C), "u": u.reshape(N, 128, 512), "v": d["v"], **weights(rng, range(8)), "sz": stored(sizes(rng))}
def setup_inputs_near(rng):
    d = numbers_of(rng)
    n = sizes(rng)
    x = d["x"].astype(np.float32).reshape(N, 8, 16, C, 4)
    x[:, :, 0] = 0
    x[:, :, 8:] = 0
    u = d["u"].reshape(N, 128, 128, 4)
    u[:, :, ::16] = 0
    o, c = rng.permutation(N) % 4, signs(rng)
    for r in range(N):
        if o[r] == 3:
            x[r, :, 9:] = rng.integers(8, 16, (8, 7, C, 4)) * 2.0 ** -30
            x[r, :, 9] = 0
            stays = rng.permutation(8) < 4
            for g in range(8):
                h, m = int(rng.integers(1, 5)), 4 * int(rng.integers(0, P // 4))
                if stays[g]: h = 1
                n[r, g] = 0
                n[r, g, m] = h
                n[r, g, m + 1 if stays[g] else m + 3] = C - h
                s = rng.integers(8, 10, C)
                s[h - 1], s[C - 1] = (9, 8) if stays[g] else (8, 9)
                x[r, g, 8, :, 0] = s * 2.0 ** -30
        else:
            size = 1.0 if o[r] < 2 else 2.0 ** -4
            s = (np.arange(C) + rng.integers(0, C, (8, 1))) % C // 8
            z = ((s[:, :, None] >> np.arange(8)) & 1) * np.exp2(np.arange(8) - 23.0) * size
            if o[r] < 2: x[r, :, 0, :, 0] = c[r][:, None]
            x[r, :, 8] = z[:, :, :4]
            x[r, :, 9] = z[:, :, 4:]
            x[r, :, 10:] = rng.integers(4, 8, (8, 6, C, 4)) * 2.0 ** -20 * size
        k = 1.0 if o[r] == 0 else 2.0 ** -30
        for h in range(0, 128, 16):
            u[r, h, h, 0] = k
            u[r, h + 8:h + 10, h] = k
    return {"x": x.reshape(N, 128, 4 * C).astype(BF), "u": u.reshape(N, 128, 512), "v": d["v"], **weights(rng, [0, 8, 9, 10, 11, 12, 13, 14, 15]), "sz": stored(n)}
def setup_inputs_huge(rng):
    d = numbers_of(rng)
    n = sizes(rng)
    c = np.stack([rng.permutation(C) % 2 * 2.0 - 1.0 for r in range(N)])
    r, z = np.arange(N), int(rng.integers(N))
    one = np.isin(r, [z] + [z ^ s for s in STEP])
    c[one] = ((r ^ (r >> 1) ^ (r >> 2)) % 2 * 2.0 - 1.0)[one][:, None]
    k = rng.random((N, 128, C, 4))
    x = 2.0 ** 30 * np.where(one[:, None, None, None], 0.75 + 0.125 * k, 0.08 + 0.01 * k) * c[:, None, :, None]
    x[z, :, C - 1] = 2.0 ** 30 * c[z, C - 1]
    for m in n[z]:
        m[P - 1] = np.sum(m[P - 4:])
        m[P - 4:P - 1] = 0
        m[np.argmax(m)] -= 1
        m[P - 1] += 1
    u = d["u"].reshape(N, 128, 128, 4)
    a = 2.0 ** 30 * (1 - 0.1 * rng.random((N, 128, 8, 4))) * signs(rng)[:, None, :, None]
    a[z] = 2.0 ** 30 * np.sign(a[z])
    u[:, :, ::16] = a.astype(np.float32).astype(BF)
    w = np.zeros((N, 128, 4, 128, 4), np.float32)
    i = np.arange(128)
    for b in range(4): w[:, i, b, i, b] = -1
    wc, ws = packed(w.reshape(N, 128, 2048).astype(BF), rng)
    return {"x": x.astype(np.float32).reshape(N, 128, 4 * C).astype(BF), "u": u.reshape(N, 128, 512), "v": d["v"], "wc": wc, "ws": ws, "sz": stored(n)}
def setup_inputs_pits(rng):
    d = setup_inputs(rng)
    n = np.zeros((N, 8, P), int)
    for r in range(N):
        k = rng.permutation(8)
        for g in range(8):
            m = n[r, g]
            q = 4 * rng.permutation(P // 4) + rng.integers(0, 4, P // 4)
            if k[g] == 0: m[q[0]] = C
            if k[g] == 1: m[P - 1] = C
            if k[g] == 2:
                m[q[:3]] = P - 1, P, P + 1
                m += np.bincount(4 * (q[3:] // 4)[rng.integers(0, P // 4 - 3, C - 3 * P)] + rng.integers(0, 4, C - 3 * P), minlength=P)
            if k[g] == 3 and r % 2 == 0: m += np.bincount(q[np.arange(C) % (P // 4)], minlength=P)
            if k[g] == 3 and r % 2 == 1:
                i = int(rng.integers(0, P // 4))
                m[3::4] = 4 * ((i - 1 - np.arange(P // 4)) % (P // 4)) + 1
                m[4 * (q[0] // 4) + 3] += C - np.sum(m)
            if k[g] == 4: m += np.bincount(np.arange(C) % P, minlength=P)
            if k[g] == 5:
                m[:] = rng.permutation(np.arange(P) % (E + 2))
                m[q[0]] += C - np.sum(m)
            if k[g] == 6: m[q[:2]] = C - 1, 1
            if k[g] == 7: m[q[:2]] = 2 * P, C - 2 * P
    d["sz"] = stored(n)
    return d
def setup_inputs_spread(rng):
    d = setup_inputs(rng)
    d["x"] = big(wide(rng, N, 128, 4 * C, cols=6))
    return d
def check_inputs(d):
    b = []
    for k in ("x", "u", "v"):
        a = np.abs(d[k].astype(np.float32))
        if not (np.isfinite(a).all() and ((a == 0) | (a >= 2.0 ** -30) & (a <= 2.0 ** 30)).all()): b.append("a value of " + k)
    if ((d["wc"] & 0x7F) == 0x7F).any(): b.append("a code of wc that is no number")
    z = np.zeros((128, 4, 4), np.float32)
    z[:, 1] = 2.0 ** -30
    z[:, 2] = 2.0 ** 30
    c, s = emit(mx_ref.quantize(z.reshape(128, 16).astype(BF)))
    for r in range(N):
        p = mx_ref.live(d["ws"][r])
        if not ((p == s[0, 0]) | (p >= s[0, 1]) & (p <= s[0, 2])).all(): b.append("a scale of ws")
        n = gentries(d["sz"][r]).astype(np.int64)
        if (n < 0).any(): b.append("a size of sz below 0")
        if (np.sum(n, axis=1) != C).any(): b.append("the sum of a group's sizes")
    return b
def reference(x, u, v, wc, ws, sz):
    qu = [mx_ref.quantize(u[r]) for r in range(N)]
    lay = [pk(wc[r], ws[r]) for r in range(N)]
    now = [x[r] for r in range(N)]
    n = [gentries(sz[r]) for r in range(N)]
    for t in range(R):
        own, sent = [], []
        for r in range(N):
            o, n[r] = sow(n[r], mx_ref.matmul(qu[r], mx_ref.quantize(now[r]))[::16])
            now[r] = gcols(now[r], o)
            own.append(gcols(now[r], ends(n[r])))
            sent.append(mx_ref.quantize(own[r]))
        came = decode(join(*sent))
        for r in range(N):
            c = cut(came, r ^ STEP[t], 4 * T).reshape(128, T, 4)[:, OPPOSITE].reshape(128, 4 * T)
            q = mx_ref.quantize((own[r].astype(np.float32) + c).astype(BF))
            h = tile([mx_ref.matmul(pick(lay[r], np.arange(128 * b, 128 * b + 128)), q) * np.float32(0.015625) + own[r][:, b::4].astype(np.float32) for b in range(4)])
            now[r] = gput(now[r], ends(n[r]), h)
    y, oz = np.zeros((N, 128, C), np.float32), np.zeros((N, 8, P), np.float32)
    oc, osc = np.zeros((N, 128, 4 * C), np.uint8), np.zeros((N, 16, C), np.uint8)
    for r in range(N):
        q = mx_ref.quantize(now[r])
        y[r] = mx_ref.matmul(mx_ref.quantize(v[r]), q)
        oz[r] = n[r]
        oc[r], osc[r] = emit(q)
    return {"y": y, "oz": oz, "oc": oc, "osc": osc}

@@ -1,0 +1,533 @@
+import numpy as np
+from concourse.mybir import dt, AluOpType as Op, ActivationFunctionType as Act
+
+C, P, NT, R = 320, 48, 96, 3
+STEP = [1, 2, 1]
+HB = 324
+XW = 4 * (HB + NT)
+OFF, BIG = 32768.0, 1048576.0
+FL = 336
+KEY = 4097.0
+LAP = KEY * P
+OW = 424
+HALF = 160
+XV = 144
+CYC, GATHER, SCATTER, WAKE, FAR, WIDE, NEAR, CALL = 0.00104, 1.56, 3.8, 0.1, 2.8, 4.3, 2.0, 0.3
+TRIES = 9000
+LANES = {"v": 8, "s": 8, "p": 4, "g": 4}
+N20 = "e1 e2 e3 e4 e5 e6 vj pit p512 p513 kk xx l48 k2 dq zero fst".split()
+N48 = "mask qd zg c15 hs hh lt gg aa ea j48".split()
+
+F, B16, I32, U16, Q4, U8 = "float32", "bfloat16", "int32", "uint16", "float8_e4m3fn_x4", "uint8"
+
+
+def _s(n, d=F):
+    return ("sbuf", [128, n], d)
+
+
+SCRATCH = {
+    "x0": _s(XW, B16), "x1": _s(XW, B16), "x2": _s(XW, B16), "x3": _s(4 * C, B16),
+    "ub": _s(512, B16), "vb": _s(512, B16), "szb": _s(4, I32),
+    "qu0": _s(128, Q4), "su0": _s(128, U8), "qu": _s(128, Q4), "su": _s(128, U8), "qv": _s(128, Q4), "sv": _s(128, U8),
+    "qw": _s(512, Q4), "sw": _s(512, U8), "qe": _s(512, Q4), "se": _s(512, U8),
+    "qx": _s(C, Q4), "sx": _s(C, U8), "qb": _s(128, Q4), "sb": _s(128, U8),
+    "ones": _s(528, B16), "eye": _s(528, B16), "dd": _s(4 * FL, B16),
+    "ta": _s(4 * NT, B16), "tb": _s(512, B16), "a64": _s(4 * NT), "tmp": _s(4 * NT),
+    "ps": ("psum", [128, 4096], F), "n20": _s(24 * len(N20)), "n48": _s(P * len(N48)),
+    "tm": _s(2 * FL), "tcf": _s(2 * FL, B16), "tf0": _s(2 * FL, B16), "tf1": _s(2 * FL, B16), "stp": _s(656, B16),
+    "ip": _s(8, I32), "col": _s(24), "v512": _s(144), "j20": _s(20), "jw": _s(20),
+    "p16": _s(16), "p4": _s(16), "t4": _s(16), "wp16": _s(C), "wpb": _s(C, B16), "wp4": _s(C), "rst": _s(C, B16), "rs2": _s(NT, B16),
+    "base": _s(24), "t1s": _s(80), "t1a": _s(32), "t1": _s(192), "th": _s(192),
+    "dum": _s(12), "hid": _s(NT), "so": _s(48, U16), "qc": _s(4),
+    "sw_": _s(376), "mk": _s(P), "rm": _s(P), "pc": _s(8), "pm": _s(24, U16),
+    "ga": _s(P, B16), "gs": _s(P), "idx": _s(4, U16), "pw": _s(192), "pww": _s(192), "en": _s(64),
+    "gt": _s(NT), "rj": _s(192), "nc": _s(4), "own": _s(8), "ei": _s(8, I32), "ek": _s(8, I32),
+    "l9": _s(12), "lo": _s(10, U16), "crp": _s(P, B16), "cg": _s(C, B16), "cw": _s(C, B16), "val": _s(C), "vw": _s(C),
+    "wg": _s(C, B16), "wr": _s(C, B16), "rr": _s(C, B16), "yg": _s(C), "s4": _s(16), "fo": _s(40, U16),
+    "vo": _s(20, U16), "do": _s(20, U16), "ow": _s(R * OW), "ao": _s(24, U16), "oww": _s(C), "xo": _s(80, U16),
+    "vq": _s(P), "mw": _s(472), "mr": _s(C), "mww": _s(C), "pib": _s(20, B16), "zs": _s(20), "lb": _s(20, B16), "po": _s(20, U16),
+    "es": _s(64), "sc": _s(4), "mz": _s(P), "yb": _s(C),
+}
+for _t in range(R):
+    SCRATCH["qx%d" % _t] = _s(C, Q4)
+    SCRATCH["sx%d" % _t] = _s(C, U8)
+    SCRATCH["ql%d" % _t] = _s(C, Q4)
+    SCRATCH["sl%d" % _t] = _s(C, U8)
+    SCRATCH["lm%d" % _t] = _s(8, U16)
+    SCRATCH["lp%d" % _t] = _s(8, U16)
+SEMAPHORES = (["sent", "arr0", "arr1", "arr2", "lis0", "lis1", "lis2"] + ["d%d" % i for i in range(24)]
+              + [e + str(i) for e in LANES for i in range(LANES[e])])
+ORDER = {}
+
+
+def depends(ops):
+    last_w, readers, deps = {}, {}, []
+    for n, (e, fn, rd, wr, kind, cost) in enumerate(ops):
+        d = set()
+        for k in rd:
+            if k in last_w: d.add(last_w[k])
+        for k in wr:
+            if k in last_w: d.add(last_w[k])
+            d.update(readers.get(k, []))
+        d.discard(n)
+        deps.append(d)
+        for k in rd: readers.setdefault(k, []).append(n)
+        for k in wr:
+            last_w[k] = n
+            readers[k] = []
+    return deps
+
+
+def arrange(ops, deps):
+    n = len(ops)
+    if n in ORDER: return ORDER[n]
+    eng, cost = [o[0] for o in ops], [o[5] for o in ops]
+    lat = [{"d": NEAR, "r": FAR, "R": WIDE}.get(o[4], 0.0) + WAKE for o in ops]
+    users = [[] for o in ops]
+    for i in range(n):
+        for d in deps[i]: users[d].append(i)
+    base = [0.0] * n
+    for i in range(n - 1, -1, -1):
+        base[i] = cost[i] + lat[i] + max([base[u] for u in users[i]] + [0.0])
+
+    def play(way, slack):
+        left, ready = [len(d) for d in deps], [0.0] * n
+        free, pool, cand = {e: 0.0 for e in "vspgy"}, {e: [] for e in "vspgy"}, {}
+        for i in range(n):
+            if not left[i]: pool[eng[i]].append(i)
+        order, end, tot, stale = [], 0.0, 0.0, "vspgy"
+        while len(order) < n:
+            for e in stale:
+                cand.pop(e, None)
+                if not pool[e]: continue
+                t = free[e]
+                c = top = max(pool[e], key=lambda i: way[i])
+                if ready[top] > t:
+                    lim = ready[top] + slack
+                    fit = [i for i in pool[e] if max(ready[i], t) + cost[i] <= lim]
+                    if fit: c = max(fit, key=lambda i: way[i] - max(0.0, ready[i] - t))
+                cand[e] = (max(t, ready[c]), c)
+            s, c = min(cand.values())
+            e = stale = eng[c]
+            pool[e].remove(c)
+            free[e] = s + cost[c]
+            end = max(end, free[e] + lat[c])
+            tot += free[e]
+            order.append(c)
+            for u in users[c]:
+                ready[u] = max(ready[u], free[e] + lat[c])
+                left[u] -= 1
+                if not left[u]:
+                    pool[eng[u]].append(u)
+                    if eng[u] not in stale: stale += eng[u]
+        return end + 3.0 * tot / n, order
+
+    rng = np.random.RandomState(1)
+    way, slack = list(base), 0.1
+    best, order = play(way, slack)
+    now = best
+    for k in range(TRIES):
+        w, s = list(way), slack
+        for i in rng.randint(0, n, 1 + k % 3): w[int(i)] += float(rng.normal()) * 1.5
+        if k % 16 == 0: s = float(rng.uniform(0.0, 0.4))
+        e, o = play(w, s)
+        if e <= now + 0.02 * (1 - k / TRIES): now, way, slack = e, w, s
+        if e < best: best, order = e, o
+    ORDER[n] = order
+    return order
+
+
+def emit(ops, g, T):
+    queue = {"v": g.vector, "s": g.scalar, "p": g.tensor, "g": g, "y": g.sync}
+    deps = depends(ops)
+    known = {e: 0 for e in queue}
+    after, sig, waited, place = {}, {}, set(), {}
+    lanes = {e: [] for e in LANES}
+    ndma = 0
+
+    def wait(e, d):
+        queue[e].wait_ge(T.sem[sig[d][0]], sig[d][1])
+        waited.add(d)
+        known[e] |= after[d]
+
+    for n in arrange(ops, deps):
+        e, fn, rd, wr, kind, cost = ops[n]
+        place[n] = len(place)
+        for d in sorted(deps[n], key=lambda d: -place[d]):
+            if ops[d][4] not in "rR" and not known[e] >> d & 1: wait(e, d)
+        if kind == "w":
+            fn()
+            known[e] |= 1 << n
+            after[n] = known[e]
+            continue
+        if kind == "c":
+            ls = lanes[e]
+            k = next((i for i in range(len(ls)) if known[e] >> ls[i][1] & 1), None)
+            if k is None and len(ls) < LANES[e]:
+                ls.append([0, n])
+                k = len(ls) - 1
+            elif k is None:
+                k = min(range(len(ls)), key=lambda i: place[ls[i][1]])
+                wait(e, ls[k][1])
+            ls[k][0] += 1
+            ls[k][1] = n
+            sig[n] = (e + str(k), ls[k][0])
+        elif kind == "d":
+            sig[n] = ("d%d" % ndma, 16)
+            ndma += 1
+        after[n] = known[e] | 1 << n
+        ins = fn()
+        if kind not in "rR": ins.then_inc(T.sem[sig[n][0]], 16 if kind == "d" else 1)
+    for e in lanes:
+        for ln in lanes[e]:
+            if ln[1] not in waited: wait(e, ln[1])
+    for n in sig:
+        if ops[n][4] == "d" and n not in waited: wait(ops[n][0], n)
+
+
+def rank_program(g, core, T, topo):
+    rank = T.rank_of(core)
+    if rank is None:
+        return
+    flip = (rank ^ (rank >> 1)) & 1
+    sg = -1.0 if flip else 1.0
+    V, S = g.vector, g.scalar
+    ops = []
+    nsent = [0]
+
+    def add(e, fn, rd, wr, cost, kind="c"):
+        ops.append((e, fn, rd.split(), wr.split(), kind, cost))
+
+    def cy(n): return max(64, n) * CYC
+
+    def ga(n): return 0.05 + n * GATHER * CYC
+
+    def ts(out, in0, s1, o0, s2, o1, rd, wr, c=0.067):
+        if o1 is None: add("v", lambda: V.tensor_scalar(out, in0, s1, None, o0), rd, wr, c)
+        else: add("v", lambda: V.tensor_scalar(out, in0, s1, s2, o0, o1), rd, wr, c)
+
+    def tt(out, a, b, o, rd, wr, c=0.067):
+        add("v", lambda: V.tensor_tensor(out, a, b, o), rd, wr, c)
+
+    def cp(out, a, rd, wr, c=0.067):
+        add("v", lambda: V.tensor_copy(out, a), rd, wr, c)
+
+    def scan(out, d0, d1, init, o0, o1, rd, wr, c=0.067):
+        add("v", lambda: V.tensor_tensor_scan(out, d0, d1, init, o0, o1), rd, wr, c)
+
+    def fill(ap, v, wr, c=0.067):
+        add("v", lambda: V.memset(ap, v), "", wr, c)
+
+    def act(out, a, rd, wr, scale=1.0, bias=None, c=0.067, f=None):
+        if bias is None: add("s", lambda: S.activation(out, a, Act.Copy, scale=scale), rd, wr, c)
+        else: add("s", lambda: S.activation(out, a, f or Act.Identity, bias=bias, scale=scale), rd, wr, c)
+
+    def sfill(out, v, wr, n):
+        act(out, T.tm[:, 0:n], "tm", wr, 0.0, v, cy(n))
+
+    def quant(q, s, a, rd, wr, n=128):
+        add("v", lambda: V.quantize_mx(q, s, a), rd, wr, 0.015 + 0.0011 * n)
+
+    def mm(bank, n, wq, ws, xq, xs, rd):
+        add("p", lambda: g.tensor.matmul_mx(T.ps[:, 512 * bank:512 * bank + n], wq, ws, xq, xs, True, True), rd, "ps%d" % bank, (n + 16) * 0.001)
+
+    def iota(out, pat, base, cm, wr, flt=True):
+        n = 1
+        for a in pat: n *= a[1]
+        if flt: add("g", lambda: g.iota(out, pat, base, cm, allow_small_or_imprecise_dtypes=True), "", wr, 0.13 + 2 * n * CYC)
+        else: add("g", lambda: g.iota(out, pat, base, cm), "", wr, 0.13 + 2 * n * CYC)
+
+    def dma(e, out, a, rd, wr):
+        q = {"y": g.sync, "s": S, "g": g}[e]
+        add(e, lambda: q.dma_start(out, a), rd, wr, 0.1, "d")
+
+    def send(dst, src, arr, t, part, rd, wr, kind):
+        mate = T.cores[rank ^ STEP[t]]
+        rid, pid = topo.addr(mate)[0:2]
+        eng = topo.engines(core, mate)
+        k = len(eng) // 2
+        eng = (eng[:k], eng[k:], eng)[part]
+        add("g", lambda: g.remote_dma(dst, src, arr, T.sem.sent, pid, rid, sum(1 << e for e in eng)), rd, wr, CALL, kind)
+        nsent[0] += len(eng)
+        return len(eng)
+
+    def pick(out, pat, src, rd, wr, c):
+        scan(out, pat, src, 0.0, Op.add, Op.min, rd, wr, c)
+
+    def rev(buf, a, on=True):
+        if not (flip and on): return buf[:, a:a + P]
+        return buf[:, a + P - 1:a - 1:-1] if a else buf[:, P - 1::-1]
+
+    X = [T.x0, T.x1, T.x2, T.x3]
+    col = T.col
+    ci, cr, ct, c16, c4, csp, c36, cd, c16b, c161, cf, cz, c4a, cq, co0, co1, cs = (col[:, k:k + 1] for k in range(17))
+    e1, e2, e3, e4, e5, e6, vj, pit, p512, p513, kk, xx, l48, k2, dq, zero, fst = (T.n20[:, 24 * k:24 * k + 20] for k in range(len(N20)))
+    mask, qd, zg, c15, hs, hh, lt, gg, aa, ea, j48 = (T.n48[:, P * k:P * k + P] for k in range(len(N48)))
+    repi, upk = T.so[:, 20:40], T.so[:, 40:48]
+
+    dma("y", T.szb[:, 0:3], T.sz[:], "", "szb")
+    dma("s", T.ub[:], T.u[:], "", "ub")
+    dma("y", T.x0[:, 0:4 * HALF], T.x[:, 0:4 * HALF], "", "x0a x0b")
+    dma("s", T.x0[:, 4 * HALF:4 * C], T.x[:, 4 * HALF:4 * C], "", "x0c")
+    dma("y", T.qw[:].bitcast(dt.uint8), T.wc[:], "", "qw")
+    dma("y", T.sw[:], T.ws[:], "", "sw")
+    dma("y", T.vb[:], T.v[:], "", "vb")
+
+    fill(T.ones[:], 1.0, "ones", cy(264))
+    iota(T.ip[:, 0:1], [[0, 1]], 0, 1, "ip", False)
+    iota(T.tm[:, 0:FL], [[1, FL]], 0, 0, "tm")
+    iota(j48, [[16, 3], [0, 16]], 0, 0, "j48")
+    iota(T.j20[:], [[16, 20]], 0, 0, "j20")
+    iota(T.v512[:], [[512, 144]], 0, 0, "v512")
+    if flip: iota(qd, [[-1, 12], [0, 4]], 11, 0, "qd")
+    else: iota(qd, [[1, 12], [0, 4]], 0, 0, "qd")
+    iota(T.t4[:], [[0, 4], [1, 4]], 0, 0, "t4")
+    iota(T.base[:, 20:24], [[64, 4]], 0, 0, "base1")
+    iota(T.hid[:], [[1, NT]], HB, 0, "hid")
+    iota(hs, [[int(KEY), P]], int(KEY), 0, "hs")
+    for t in range(R): iota(T.ow[:, OW * t + C:OW * t + OW], [[0, OW - C]], C, 0, "ow%d" % t)
+    iota(T.th[:], [[0, 192]], int(C + LAP), 0, "th")
+    add("g", lambda: g.affine_select(T.eye[:], T.ones[:], [[1, 528]], Op.is_equal, 0.0, -3, -4), "ones", "eye", 1.27)
+    fill(T.t1[:], 0.0, "t1", cy(192))
+    fill(T.ow[:, 0:R * OW:OW], 0.0, "owz")
+    fill(c15, 1.5, "c15")
+    fill(T.en[:, P:64], 4096.0, "en")
+    fill(T.en[:, 0:1], 0.0, "enz")
+    fill(T.sw_[:, C + 1:376], -1e29, "swz")
+    fill(T.sw_[:, 0:1], -1e29, "swy")
+    fill(T.rst[:], 1.0, "rst", cy(160))
+    fill(T.rst[:, 0:C:16], 0.0, "rst")
+    fill(T.rs2[:], 1.0, "rs2")
+    fill(T.rs2[:, 0:NT:32], 0.0, "rs2")
+    fill(T.es[:, P:64], -1.0 / 48, "esz")
+    fill(zero, 0.0, "zero")
+    fill(T.tf0[:], 0.0, "tf0", cy(FL))
+    fill(T.tf0[:, 0:2 * FL:FL], 1024.0, "tf0")
+    fill(T.tf1[:], -1.0, "tf1", cy(FL))
+    fill(T.tf1[:, 0:2], 1024.0, "tf1")
+    fill(T.tf1[:, FL:FL + 2], 1024.0, "tf1")
+    fill(T.t1s[:, 0:32], 0.0, "t1s0")
+    fill(T.t1s[:, P:80], -1.0, "t1s2")
+    for t in range(R): sfill(X[t][:, 4 * C:4 * HB], 0.0, "x%dz" % t, 16)
+    for b in range(4): sfill(T.dd[:, FL * b + C:FL * b + FL], 0.0, "ddz%d" % b, 16)
+    sfill(T.mw[:, 0:C], 0.0, "mw", C)
+    sfill(T.mw[:, C:472], 0.0, "mwz", 472 - C)
+    sfill(T.tb[:, 4 * NT:512], 0.0, "tbz", 128)
+    sfill(T.tcf[:, 0:FL], 0.0, "tcf", FL)
+    sfill(T.tcf[:, FL:2 * FL], 4096.0, "tcg", FL)
+    sfill(T.stp[:, 0:C], 1.0, "stp0", C)
+    sfill(T.stp[:, C + 16:656], 0.0, "stp2", C)
+    act(T.tm[:, FL:2 * FL], T.tm[:, 0:FL], "tm", "tm2", c=cy(FL))
+    ts(T.ip[:, 1:2], T.ip[:, 0:1], 15, Op.bitwise_and, None, None, "ip", "ip1")
+    ts(T.ip[:, 2:3], T.ip[:, 0:1], 2, Op.arith_shift_right, 3, Op.bitwise_and, "ip", "ip2")
+    ts(T.ip[:, 3:4], T.ip[:, 0:1], 3, Op.bitwise_and, None, None, "ip", "ip3")
+    cp(ci, T.ip[:, 1:2], "ip1", "ci")
+    cp(col[:, 1:3], T.ip[:, 2:4], "ip2 ip3", "cr")
+    act(c16, ci, "ci", "c16", -OFF, 15 * OFF)
+    act(c16b, ci, "ci", "c16b", -OFF / 4, 15 * OFF / 4)
+    act(c161, ci, "ci", "c161", -OFF, 15 * OFF + 1)
+    act(co0, ci, "ci", "co0", -OFF, 15 * OFF + 1023)
+    act(co1, ci, "ci", "co1", -OFF, 15 * OFF + 511)
+    act(cs, ci, "ci", "cs", -OFF, 15 * OFF + FL - 2.5)
+    act(c36, ci, "ci", "c36", 1.0, 36.0)
+    act(cd, ci, "ci", "cd", OFF + 1, C + 1 - 15 * OFF)
+    act(cf, ci, "ci", "cf", -OFF, 15 * OFF + C)
+    act(cz, ci, "ci", "cz", sg / 48, (23.5 + 47 * flip) / 48 - 192)
+    act(cq, ci, "ci", "cq", sg, 15.0 * flip)
+    act(c4a, cr, "cr", "c4a", -4 * OFF, 12 * OFF)
+    act(c4, ct, "cr c4a", "c4", 1.0, c4a)
+    ts(csp, ci, 12.0, Op.is_ge, c36, Op.mult, "ci c36", "csp")
+    ts(repi, zero, ci, Op.add, None, None, "ci zero", "repi")
+    ts(T.p16[:], T.tm[:, 0:16], ci, Op.is_equal, BIG + OFF, Op.mult, "tm ci", "p16")
+    ts(T.p4[:], T.t4[:], cr, Op.is_equal, BIG + OFF, Op.mult, "t4 cr", "p4")
+    ts(T.stp[:, C:C + 16], T.tm[:, 0:16], ci, Op.is_le, None, None, "tm ci", "stp1")
+    ts(T.t1a[:, 0:16], T.tm[:, 0:16], cq, Op.is_equal, 4097.0, Op.mult, "tm cq", "t1a")
+    ts(T.t1a[:, 16:32], T.tm[:, 0:16], cq, Op.is_ge, None, None, "tm cq", "t1b")
+    tt(T.t1s[:, 32:P], T.t1a[:, 0:16], T.t1a[:, 16:32], Op.subtract, "t1a t1b", "t1s1")
+    act(T.wp16[:, 0:192], T.p16[:].indirect(T.so[:, 20:32]), "p16 repi", "wp16", bias=-OFF, c=ga(192))
+    act(T.wp16[:, 192:C], T.wp16[:, 0:128], "wp16", "wp16x", c=cy(128))
+    act(T.wpb[:], T.wp16[:], "wp16 wp16x", "wpb", 0.25, c=cy(C))
+    act(T.wp4[:], T.p4[:].indirect(repi), "p4 repi", "wp4", bias=-OFF, c=ga(C))
+    cp(upk, T.j20[:, 0:8], "j20", "upk")
+    act(T.base[:, 0:20], zero, "zero csp", "base0", 1.0, csp)
+    act(T.base[:, 20:24], T.base[:, 20:24], "base1 csp", "base1", 1.0, csp)
+    act(T.dum[:, 0:9], T.j20[:, 0:9], "j20 cd", "dum", 1.0, cd)
+    act(T.jw[:], T.j20[:], "j20 ci", "jw", 1.0, ci)
+    act(T.qc[:, 0:3], T.jw[:, 0:3], "jw", "qc", sg * KEY, 2048 + 47 * KEY * flip)
+    act(fst, T.j20[:], "j20 cf", "fst", -1.0, cf)
+    act(zg, j48, "j48 cz", "zg", sg / 48, cz)
+    quant(T.qu0[:], T.su0[:], T.ub[:], "ub", "qu0")
+    add("s", lambda: S.activation(T.su[:], T.su0[:].indirect(upk), Act.Copy), "qu0 upk", "su", ga(128))
+    cp(T.qu[:].bitcast(dt.uint32), T.qu0[:].bitcast(dt.uint32).indirect(upk), "qu0 upk", "qu", ga(128))
+    ts(mask, qd, ci, Op.is_equal, 3e29, Op.mult, "qd ci", "mask")
+    act(mask, mask, "mask", "mask", 1.0, -2e29)
+    for b in range(4):
+        quant(T.qe[:, 128 * b:128 * b + 128], T.se[:, 128 * b:128 * b + 128], T.eye[:, 3 - b:515 - b], "eye", "qe%d" % b)
+    quant(T.qv[:], T.sv[:], T.vb[:], "vb", "qv")
+    cp(T.idx[:, 0:3], T.szb[:, 0:3], "szb", "idx")
+
+    idx = T.idx[:, 0:3]
+    un = rev(T.pw, 144)
+
+    def sizes(first):
+        win = T.tm[:, 0:FL] if first else T.tm[:]
+        act(rev(T.pw, 144, first), win.indirect(idx), "tm idx" if first else "tm tm2 idx", "un", -1.0, 1.5, ga(P))
+        scan(T.en[:, 1:P + 1], c15, un, 0.0, Op.add, Op.subtract, "c15 un", "en")
+
+    def places(first, last):
+        tt(rev(T.pw, 0, first), T.tf0[:].indirect(idx), rev(T.en, 1, not first), Op.add, "tf0 idx en", "pw0", ga(P))
+        tt(rev(T.pw, P, first), T.tf1[:].indirect(idx), rev(T.en, 1, not first), Op.add, "tf1 idx en", "pw1", ga(P))
+        n, k = (NT, 6) if last else (192, 9)
+        if not last: tt(rev(T.pw, 96, first), T.tf0[:].indirect(idx), rev(T.en, 0, not first), Op.add, "tf0 idx en enz", "pw2", ga(P))
+        pick(T.pww[:, 0:n], T.wp16[:, 0:n], T.pw[:, 0:n], "wp16 pw0 pw1 pw2 un", "pww", cy(n))
+        tt(T.l9[:, 0:k], T.pww[:, 15:16 * k:16], T.dum[:, 0:k], Op.min, "pww dum", "l9")
+        ts(T.lo[:, 0:k], T.l9[:, 0:k], c16, Op.add, None, None, "l9 c16", "lo")
+
+    def tables():
+        tt(ea, T.tm[:, 0:P], un, Op.subtract, "tm un", "ea", cy(96))
+        act(T.es[:, 0:P], ea, "ea", "es", 1.0 / 48, 1.5 / 48)
+        act(T.sc[:, 0:3], T.pww[:, 159:192:16], "pww cs", "sc", 1.0, cs)
+        act(T.t1[:, P:192:64], T.sc[:, 0:3], "sc t1", "t1n", -11.0, 1.0 - FL)
+        tt(hh, T.en[:, 0:P], hs, Op.subtract, "en enz hs", "hh", cy(96))
+        for c in range(3):
+            a = 16 * c if flip else 32 - 16 * c
+            act(T.t1[:, 64 * c:64 * c + P], T.t1s[:, a:a + P], "sc t1s0 t1s1 t1s2 t1", "t1%d" % c, -1.0, T.sc[:, c:c + 1], f=Act.Relu)
+            act(T.th[:, 64 * c:64 * c + P], hh, "hh qc th", "th%d" % c, 1.0, T.qc[:, c:c + 1])
+        ts(T.own[:, 0:3], T.pww[:, 15:48:16], co0, Op.add, 1024.0 + C, Op.min, "pww co0", "own0")
+        ts(T.own[:, 3:6], T.pww[:, 63:96:16], co1, Op.add, 512.0 + C, Op.min, "pww co1", "own1")
+
+    def labels(v):
+        tt(T.vq[:], rev(T.v512, P * v), rev(T.en, 0), Op.add, "v512 en enz", "vq", cy(96))
+        cp(T.mw[:].indirect(T.lo[:, 6:9]), T.vq[:], "vq lo mw mwz", "mw", 0.05 + P * SCATTER * CYC)
+        scan(T.mr[:], T.mw[:, 0:C], T.mw[:, 0:C], 0.0, Op.max, Op.max, "mw", "mr", cy(C))
+        pick(T.mww[:], T.wp16[:], T.mr[:], "wp16 wp16x mr", "mww", cy(C))
+        act(vj, T.mww[:, 15:C:16], "mww c16", "vj", 1.0, c16)
+        act(T.pib[:], vj, "vj", "pib", 1.0 / 512, 192 - 0.31 - P * v)
+        act(pit, T.pib[:], "pib", "pit", 1.0, -192.0)
+        act(p512, T.pib[:], "pib", "p512", 512.0, 512.0 * (P * v - 192))
+        act(p513, T.pib[:], "pib", "p513", 513.0, 512.0 * P * v - 513.0 * 192)
+        cp(T.po[:], pit, "pit", "po")
+        tt(e5, T.jw[:], vj, Op.subtract, "vj jw", "e5")
+        tt(kk, e5, p512, Op.add, "e5 p512", "kk")
+        tt(xx, e5, p513, Op.add, "e5 p513", "xx")
+        act(T.zs[:], xx, "xx", "zs", 1.0 / 48, 24.5 / 48 - 192)
+        act(T.lb[:], xx, "xx", "lb", 1.0 / 48, 192 - 22.5 / 48)
+        act(l48, T.lb[:], "lb", "l48", 48.0 / 4096, -(192 * 48.0 + 2) / 4096)
+        act(k2, kk, "kk", "k2", 1.0 / 4096)
+        tt(dq, k2, l48, Op.subtract, "k2 l48", "dq")
+
+    def grid():
+        pick(T.s4[:], T.wp16[:, 0:16], T.en[:, 0:64:4], "wp16 en enz", "s4", cy(16))
+        ts(T.fo[:, 0:40:2], fst, T.s4[:, 15:16], Op.add, 655.0, Op.min, "fst s4", "fo")
+        for c in range(20):
+            act(T.yg[:, 16 * c:16 * c + 16], T.stp[:].indirect(T.fo[:, 2 * c:2 * c + 1]), "stp0 stp1 stp2 fo zs", "yg%d" % c,
+                -1.0, T.zs[:, c:c + 1], 0.1)
+
+    def pack(t, wq, ws, wk, out, ok):
+        qx, sx = (T["qx%d" % t], T["sx%d" % t]) if t < R else (T.qx, T.sx)
+        for h, a, n, rd in ((0, 0, HALF, "x%da x%db" % (t, t)), (1, HALF, C - HALF, "x%dc" % t)):
+            nm = "ab"[h]
+            quant(qx[:, a:a + n], sx[:, a:a + n], X[t][:, 4 * a:4 * a + 4 * n], rd, "qx%s%d" % (nm, t), n)
+            mm(h, n, wq, ws, qx[:, a:a + n], sx[:, a:a + n], wk + " qx%s%d" % (nm, t))
+            act(out(a, n), T.ps[:, 512 * h:512 * h + n], "ps%d" % h, ok + nm + " ps%d" % h, c=cy(n))
+
+    sizes(True)
+    places(True, False)
+    tables()
+    labels(0)
+    grid()
+    ygk = " ".join("yg%d" % c for c in range(20))
+    for t in range(R):
+        xk = "x%da x%db x%dc x%dz" % (t, t, t, t)
+        ow = T.ow[:, OW * t:OW * t + OW]
+        ok = "ow%d" % t
+        pack(t, T.qu[:], T.su[:], "qu su", lambda a, n: T.sw_[:, 1 + a:1 + a + n], "sw")
+        qx, sx, ql, sl, arr = T["qx%d" % t], T["sx%d" % t], T["ql%d" % t], T["sl%d" % t], T.sem["arr%d" % t]
+        na = send(ql[:, 0:HALF].bitcast(dt.uint8), qx[:, 0:HALF].bitcast(dt.uint8), arr, t, 0, "qxa%d" % t, "r0", "R")
+        na += send(ql[:, HALF:C].bitcast(dt.uint8), qx[:, HALF:C].bitcast(dt.uint8), arr, t, 1, "qxb%d" % t, "r1", "R")
+        na += send(sl[:], sx[:], arr, t, 0, "qxa%d qxb%d" % (t, t), "r2", "R")
+        add("p", lambda arr=arr, n=na: g.tensor.wait_ge(arr, n), "r0 r1 r2", "ql%d" % t, 0.0, "w")
+        for b in range(4):
+            mm(4 + b, C, T.qe[:, 128 * b:128 * b + 128], T.se[:, 128 * b:128 * b + 128], ql[:], sl[:], "qe%d ql%d" % (b, t))
+            act(T.dd[:, FL * b:FL * b + C], T.ps[:, 512 * (4 + b):512 * (4 + b) + C], "ps%d" % (4 + b), "dd%d ps%d" % (b, 4 + b), c=cy(C))
+        tt(T.mk[:], T.sw_[:].indirect(T.lo[:, 0:3]), mask, Op.min, "swa swb swz swy lo mask", "mk", ga(P))
+        scan(T.rm[:], rev(T.mk, 0), rev(T.mk, 0), -3e29, Op.max, Op.max, "mk", "rm")
+        add("s", lambda: S.activation(lt, T.rm[:], Act.Sign, bias=T.rm[:, P - 1:P], scale=-1.0, accum_out=T.pc[:, 0:1]), "rm", "lt pc", 0.09)
+        ts(T.pm[:], T.base[:], T.pc[:, 0:1], Op.add, None, None, "pc base0 base1", "pm")
+        pm3, pm64 = T.pm[:, 0:3], T.pm[:, 20:23]
+        tt(T.ga[:], T.es[:].indirect(pm3), zg, Op.subtract, "es esz pm zg", "ga", ga(P))
+        tt(gg, T.t1[:].indirect(pm64), T.ga[:], Op.subtract, "t1 t1n t10 t11 t12 pm ga", "gg", ga(P))
+        scan(T.gs[:], T.rst[:, 0:P], gg, 0.0, Op.mult, Op.add, "rst gg", "gs")
+        ts(idx, T.gs[:, 15:P:16], -1.0, Op.mult, -191.0 * 16, Op.add, "gs", "idx")
+        ts(aa, T.ga[:], -192.0, Op.add, LAP, Op.mult, "ga", "aa")
+        tt(T.gt[:, 1:NT:2], T.th[:].indirect(pm64), aa, Op.add, "th th0 th1 th2 pm aa", "g1", ga(P))
+        ts(T.gt[:, 0:NT:2], T.gt[:, 1:NT:2], -LAP, Op.add, None, None, "g1", "g2")
+        ts(T.nc[:, 0:3], T.gs[:, 15:P:16], 0.5 - 191 * 16 - FL, Op.is_gt, 4096.0, Op.mult, "gs", "nc")
+        tt(T.gt[:, 25:NT:32], T.nc[:, 0:3], T.own[:, 0:3], Op.min, "nc own0 g1 g2", "g3")
+        tt(T.gt[:, 27:NT:32], T.nc[:, 0:3], T.own[:, 3:6], Op.min, "nc own1 g1 g2", "g4")
+        scan(T.rj[:, NT - 1::-1], T.rs2[:], T.gt[:, NT - 1::-1], 0.0, Op.mult, Op.max, "rs2 g1 g2 g3 g4", "rj0", cy(NT))
+        scan(T.rj[:, 2 * NT - 2:NT - 1:-1], T.gt[:, NT - 2::-1], T.rj[:, NT - 1:0:-1], float(C), Op.max, Op.min, "rj0 g1 g2 g3 g4", "rj1", cy(NT))
+        cp(T.ei[:, 0:6], T.rj[:, 0:2 * NT:32], "rj0 rj1", "ei")
+        ts(T.ek[:, 0:6], T.ei[:, 0:6], 511, Op.bitwise_and, None, None, "ei", "ek")
+        lm, lp, lis = T["lm%d" % t], T["lp%d" % t], T.sem["lis%d" % t]
+        cp(lm[:, 0:6], T.ek[:, 0:6], "ek", "lm%d" % t)
+        nl = send(lp[:, 0:6], lm[:, 0:6], lis, t, 2, "lm%d" % t, "r3", "r")
+        win = X[t][:, 0:4 * HB]
+        for b in range(4):
+            ts(T.ao[:, 6 * b:6 * b + 6], T.ek[:, 0:6], 4.0, Op.mult, float(b), Op.add, "ek", "ao%d" % b)
+            act(T.ta[:, b:4 * NT:4], win.indirect(T.ao[:, 6 * b:6 * b + 6]), "ao%d %s" % (b, xk), "ta%d" % b, c=ga(NT))
+        act(T.a64[:], T.ta[:], "ta0 ta1 ta2 ta3", "a64", 64.0, c=cy(384))
+        sizes(False)
+        act(rev(T.crp, 0), T.tcf[:].indirect(idx), "tcf tcg idx", "crp", c=ga(P))
+        act(T.cg[:], T.crp[:].indirect(T.po[:]), "crp po c16b", "cg", 1.0, c16b, ga(C))
+        pick(T.cw[:], T.wpb[:], T.cg[:], "wpb cg", "cw", cy(160))
+        mv = T.cw[:, 15:C:16]
+        tt(e1, mv, dq, Op.mult, "cw dq", "e1")
+        tt(e2, e1, pit, Op.add, "e1 pit", "e2")
+        cp(T.vo[:], e2, "e2", "vo")
+        act(T.val[:], T.en[:].indirect(T.vo[:]), "en enz vo c161", "val", 1.0, c161, ga(C))
+        pick(T.vw[:], T.wp16[:], T.val[:], "wp16 wp16x val", "vw", cy(C))
+        tt(T.wg[:], T.es[:].indirect(T.pm[:, 0:20]), T.yg[:], Op.subtract, "es esz pm " + ygk, "wg", ga(C))
+        ts(T.wr[:], T.wg[:], -192.0, Op.add, 0.0, Op.max, "wg", "wr", cy(160))
+        scan(T.rr[:], T.rst[:], T.wr[:], 0.0, Op.mult, Op.add, "rst wr", "rr", cy(160))
+        tt(e3, mv, kk, Op.subtract, "cw kk", "e3")
+        tt(e4, e3, T.rr[:, 15:C:16], Op.min, "e3 rr", "e4")
+        tt(e6, T.vw[:, 15:C:16], e4, Op.subtract, "vw e4", "e6")
+        cp(T.do[:], e6, "e6", "do")
+        cp(ow.indirect(T.do[:]), T.tm[:, 0:C], "do tm owz " + ok, ok, 0.05 + C * SCATTER * CYC)
+        places(False, t == R - 1)
+        cp(ow.indirect(T.lo[:, 0:6]), T.hid[:], "lo hid " + ok, ok, 0.05 + NT * SCATTER * CYC)
+        pick(T.oww[:], T.wp4[:], T.ow[:, OW * t + 1:OW * t + C + 1], "wp4 " + ok, "oww", cy(C))
+        ts(T.xo[:], T.oww[:, 3:C:4], 4.0, Op.mult, c4, Op.add, "oww c4", "xo", cy(80))
+        if t < R - 1:
+            labels(t + 1)
+            tables()
+            grid()
+        else:
+            act(T.mz[:], un, "un", "mz", -1.0, 1.5)
+            dma("y", T.oz[:], T.mz[0:128:16, :], "mz", "oz")
+        add("v", lambda lis=lis, n=nl: V.wait_ge(lis, n), "r3", "lp%d" % t, 0.0, "w")
+        for b in range(4):
+            tt(T.tb[:, b:4 * NT:4], T.dd[:, FL * b:FL * b + FL].indirect(lp[:, 0:6]), T.ta[:, b:4 * NT:4], Op.add,
+               "ta%d dd%d ddz%d lp%d" % (b, b, b, t), "tb%d" % b, ga(NT))
+        quant(T.qb[:], T.sb[:], T.tb[:], "tb0 tb1 tb2 tb3 tbz", "qb")
+        for b in range(4):
+            mm(b, 128, T.qw[:, 128 * b:128 * b + 128], T.sw[:, 128 * b:128 * b + 128], T.qb[:], T.sb[:], "qw sw qb")
+        for b in range(4):
+            tt(T.tmp[:, NT * b:NT * b + NT], T.ps[:, 512 * b:512 * b + NT], T.a64[:, b:4 * NT:4], Op.add, "a64 ps%d" % b, "tmp%d ps%d" % (b, b), cy(NT))
+            act(X[t][:, 4 * HB + b:XW:4], T.tmp[:, NT * b:NT * b + NT], "tmp%d" % b, "h%d%d" % (t, b), 0.015625, c=cy(NT))
+        hk = xk + " xo h%d0 h%d1 h%d2 h%d3" % (t, t, t, t)
+        a, b = XV // 4, HALF // 4
+        cp(X[t + 1][:, 0:4 * XV], X[t][:].indirect(T.xo[:, 0:a]), hk, "x%da" % (t + 1), ga(4 * XV))
+        if b > a: act(X[t + 1][:, 4 * XV:4 * HALF], X[t][:].indirect(T.xo[:, a:b]), hk, "x%db" % (t + 1), c=ga(4 * (HALF - XV)))
+        act(X[t + 1][:, 4 * HALF:4 * C], X[t][:].indirect(T.xo[:, b:80]), hk, "x%dc" % (t + 1), c=ga(4 * (C - HALF)))
+
+    pack(R, T.qv[:], T.sv[:], "qv", lambda a, n: T.yb[:, a:a + n], "yb")
+    dma("y", T.oc[:, 0:4 * HALF], T.qx[:, 0:HALF].bitcast(dt.uint8), "qxa3", "oca")
+    dma("y", T.oc[:, 4 * HALF:4 * C], T.qx[:, HALF:C].bitcast(dt.uint8), "qxb3", "ocb")
+    for k in range(4):
+        dma("y", T.osc[4 * k:4 * k + 4, :], T.sx[32 * k:32 * k + 4, :], "qxa3 qxb3", "osc%d" % k)
+    dma("s", T.y[:, 0:HALF], T.yb[:, 0:HALF], "yba", "ya")
+    dma("s", T.y[:, HALF:C], T.yb[:, HALF:C], "ybb", "yb")
+    add("g", lambda: g.wait_ge(T.sem.sent, nsent[0]), "r0 r1 r2 r3", "", 0.0, "w")
+    emit(ops, g, T)

@@ -12,8 +12,9 @@ LAP = KEY * P
 OW = 424
 HALF = 160
 XV = 144
-CYC, GATHER, SCATTER, WAKE, FAR, WIDE, NEAR, CALL = 0.00104, 1.56, 3.8, 0.1, 2.8, 4.3, 2.0, 0.3
-TRIES = 9000
+CYC, GATHER, SCATTER, WAKE, FAR, WIDE, NEAR, CALL = 0.00104, 1.56, 3.8, 0.15, 3.3, 5.2, 2.0, 0.5
+OTHER = [(0.1, 2.6, 4.3, 0.3), (0.2, 4.2, 6.5, 0.9)]
+TRIES = 12000
 LANES = {"v": 8, "s": 8, "p": 4, "g": 4}
 N20 = "e1 e2 e3 e4 e5 e6 vj pit p512 p513 kk xx l48 k2 dq zero fst".split()
 N48 = "mask qd zg c15 hs hh lt gg aa ea j48".split()
@@ -34,15 +35,15 @@ SCRATCH = {
     "ones": _s(528, B16), "eye": _s(528, B16), "dd": _s(4 * FL, B16),
     "ta": _s(4 * NT, B16), "tb": _s(512, B16), "a64": _s(4 * NT), "tmp": _s(4 * NT),
     "ps": ("psum", [128, 4096], F), "n20": _s(24 * len(N20)), "n48": _s(P * len(N48)),
-    "tm": _s(2 * FL), "tcf": _s(2 * FL, B16), "tf0": _s(2 * FL, B16), "tf1": _s(2 * FL, B16), "stp": _s(656, B16),
+    "tm": _s(2 * FL), "tf0": _s(2 * FL, B16), "tf1": _s(2 * FL, B16), "stp": _s(656, B16),
     "ip": _s(8, I32), "col": _s(24), "v512": _s(144), "j20": _s(20), "jw": _s(20),
     "p16": _s(16), "p4": _s(16), "t4": _s(16), "wp16": _s(C), "wpb": _s(C, B16), "wp4": _s(C), "rst": _s(C, B16), "rs2": _s(NT, B16),
     "base": _s(24), "t1s": _s(80), "t1a": _s(32), "t1": _s(192), "th": _s(192),
     "dum": _s(12), "hid": _s(NT), "so": _s(48, U16), "qc": _s(4),
     "sw_": _s(376), "mk": _s(P), "rm": _s(P), "pc": _s(8), "pm": _s(24, U16),
     "ga": _s(P, B16), "gs": _s(P), "idx": _s(4, U16), "pw": _s(192), "pww": _s(192), "en": _s(64),
-    "gt": _s(NT), "rj": _s(192), "nc": _s(4), "own": _s(8), "ei": _s(8, I32), "ek": _s(8, I32),
-    "l9": _s(12), "lo": _s(10, U16), "crp": _s(P, B16), "cg": _s(C, B16), "cw": _s(C, B16), "val": _s(C), "vw": _s(C),
+    "gt": _s(NT), "rj": _s(192), "own": _s(8), "ei": _s(8, I32), "ek": _s(8, I32),
+    "l9": _s(12), "lo": _s(10, U16), "crp": _s(R * 64 + 16, B16), "nf": _s(P, B16), "cg": _s(C, B16), "cw": _s(C, B16), "val": _s(C), "vw": _s(C),
     "wg": _s(C, B16), "wr": _s(C, B16), "rr": _s(C, B16), "yg": _s(C), "s4": _s(16), "fo": _s(40, U16),
     "vo": _s(20, U16), "do": _s(20, U16), "ow": _s(R * OW), "ao": _s(24, U16), "oww": _s(C), "xo": _s(80, U16),
     "vq": _s(P), "mw": _s(472), "mr": _s(C), "mww": _s(C), "pib": _s(20, B16), "zs": _s(20), "lb": _s(20, B16), "po": _s(20, U16),
@@ -90,6 +91,18 @@ def arrange(ops, deps):
     for i in range(n - 1, -1, -1):
         base[i] = cost[i] + lat[i] + max([base[u] for u in users[i]] + [0.0])
 
+    def again(order, wake, far, wide, call):
+        free, fin = {e: 0.0 for e in "vspgy"}, [0.0] * n
+        late = {"d": NEAR + wake, "r": far + wake, "R": wide + wake, "c": wake, "w": wake}
+        for c in order:
+            s = free[eng[c]]
+            for d in deps[c]:
+                if fin[d] > s: s = fin[d]
+            s += call if ops[c][4] in "rR" else cost[c]
+            free[eng[c]] = s
+            fin[c] = s + late[ops[c][4]]
+        return max(fin)
+
     def play(way, slack):
         left, ready = [len(d) for d in deps], [0.0] * n
         free, pool, cand = {e: 0.0 for e in "vspgy"}, {e: [] for e in "vspgy"}, {}
@@ -120,7 +133,7 @@ def arrange(ops, deps):
                 if not left[u]:
                     pool[eng[u]].append(u)
                     if eng[u] not in stale: stale += eng[u]
-        return end + 3.0 * tot / n, order
+        return end + 8.0 * tot / n + sum(again(order, *a) for a in OTHER), order
 
     rng = np.random.RandomState(1)
     way, slack = list(base), 0.1
@@ -131,7 +144,7 @@ def arrange(ops, deps):
         for i in rng.randint(0, n, 1 + k % 3): w[int(i)] += float(rng.normal()) * 1.5
         if k % 16 == 0: s = float(rng.uniform(0.0, 0.4))
         e, o = play(w, s)
-        if e <= now + 0.02 * (1 - k / TRIES): now, way, slack = e, w, s
+        if e <= now + 0.05 * (1 - k / TRIES): now, way, slack = e, w, s
         if e < best: best, order = e, o
     ORDER[n] = order
     return order
@@ -313,8 +326,6 @@ def rank_program(g, core, T, topo):
     sfill(T.mw[:, 0:C], 0.0, "mw", C)
     sfill(T.mw[:, C:472], 0.0, "mwz", 472 - C)
     sfill(T.tb[:, 4 * NT:512], 0.0, "tbz", 128)
-    sfill(T.tcf[:, 0:FL], 0.0, "tcf", FL)
-    sfill(T.tcf[:, FL:2 * FL], 4096.0, "tcg", FL)
     sfill(T.stp[:, 0:C], 1.0, "stp0", C)
     sfill(T.stp[:, C + 16:656], 0.0, "stp2", C)
     act(T.tm[:, FL:2 * FL], T.tm[:, 0:FL], "tm", "tm2", c=cy(FL))
@@ -349,6 +360,8 @@ def rank_program(g, core, T, topo):
     act(T.wpb[:], T.wp16[:], "wp16 wp16x", "wpb", 0.25, c=cy(C))
     act(T.wp4[:], T.p4[:].indirect(repi), "p4 repi", "wp4", bias=-OFF, c=ga(C))
     cp(upk, T.j20[:, 0:8], "j20", "upk")
+    act(T.crp[:, 0:R * 64], T.tm[:, 0:R * 64], "tm c16b", "crp0 crp1 crp2", 0.0, c16b, cy(R * 64))
+    act(T.crp[:, R * 64:R * 64 + 16], T.crp[:, 0:16], "crp0", "crs", 1.0, 4096.0)
     act(T.base[:, 0:20], zero, "zero csp", "base0", 1.0, csp)
     act(T.base[:, 20:24], T.base[:, 20:24], "base1 csp", "base1", 1.0, csp)
     act(T.dum[:, 0:9], T.j20[:, 0:9], "j20 cd", "dum", 1.0, cd)
@@ -454,6 +467,9 @@ def rank_program(g, core, T, topo):
         scan(T.rm[:], rev(T.mk, 0), rev(T.mk, 0), -3e29, Op.max, Op.max, "mk", "rm")
         add("s", lambda: S.activation(lt, T.rm[:], Act.Sign, bias=T.rm[:, P - 1:P], scale=-1.0, accum_out=T.pc[:, 0:1]), "rm", "lt pc", 0.09)
         ts(T.pm[:], T.base[:], T.pc[:, 0:1], Op.add, None, None, "pc base0 base1", "pm")
+        crp = T.crp[:, 64 * t:64 * t + 64]
+        cp(crp.indirect(T.pm[:, 0:1]), T.crp[:, R * 64:R * 64 + 16], "pm crs crp%d" % t, "crp%d" % t, 0.05 + 16 * SCATTER * CYC)
+        pick(T.nf[:], T.wpb[:, 0:P], rev(T.crp, 64 * t), "wpb crp%d" % t, "nc", cy(24))
         pm3, pm64 = T.pm[:, 0:3], T.pm[:, 20:23]
         tt(T.ga[:], T.es[:].indirect(pm3), zg, Op.subtract, "es esz pm zg", "ga", ga(P))
         tt(gg, T.t1[:].indirect(pm64), T.ga[:], Op.subtract, "t1 t1n t10 t11 t12 pm ga", "gg", ga(P))
@@ -462,9 +478,8 @@ def rank_program(g, core, T, topo):
         ts(aa, T.ga[:], -192.0, Op.add, LAP, Op.mult, "ga", "aa")
         tt(T.gt[:, 1:NT:2], T.th[:].indirect(pm64), aa, Op.add, "th th0 th1 th2 pm aa", "g1", ga(P))
         ts(T.gt[:, 0:NT:2], T.gt[:, 1:NT:2], -LAP, Op.add, None, None, "g1", "g2")
-        ts(T.nc[:, 0:3], T.gs[:, 15:P:16], 0.5 - 191 * 16 - FL, Op.is_gt, 4096.0, Op.mult, "gs", "nc")
-        tt(T.gt[:, 25:NT:32], T.nc[:, 0:3], T.own[:, 0:3], Op.min, "nc own0 g1 g2", "g3")
-        tt(T.gt[:, 27:NT:32], T.nc[:, 0:3], T.own[:, 3:6], Op.min, "nc own1 g1 g2", "g4")
+        tt(T.gt[:, 25:NT:32], T.own[:, 0:3], T.nf[:, 15:P:16], Op.subtract, "nc own0 g1 g2", "g3")
+        tt(T.gt[:, 27:NT:32], T.own[:, 3:6], T.nf[:, 15:P:16], Op.subtract, "nc own1 g1 g2", "g4")
         scan(T.rj[:, NT - 1::-1], T.rs2[:], T.gt[:, NT - 1::-1], 0.0, Op.mult, Op.max, "rs2 g1 g2 g3 g4", "rj0", cy(NT))
         scan(T.rj[:, 2 * NT - 2:NT - 1:-1], T.gt[:, NT - 2::-1], T.rj[:, NT - 1:0:-1], float(C), Op.max, Op.min, "rj0 g1 g2 g3 g4", "rj1", cy(NT))
         cp(T.ei[:, 0:6], T.rj[:, 0:2 * NT:32], "rj0 rj1", "ei")
@@ -478,8 +493,7 @@ def rank_program(g, core, T, topo):
             act(T.ta[:, b:4 * NT:4], win.indirect(T.ao[:, 6 * b:6 * b + 6]), "ao%d %s" % (b, xk), "ta%d" % b, c=ga(NT))
         act(T.a64[:], T.ta[:], "ta0 ta1 ta2 ta3", "a64", 64.0, c=cy(384))
         sizes(False)
-        act(rev(T.crp, 0), T.tcf[:].indirect(idx), "tcf tcg idx", "crp", c=ga(P))
-        act(T.cg[:], T.crp[:].indirect(T.po[:]), "crp po c16b", "cg", 1.0, c16b, ga(C))
+        act(T.cg[:], crp.indirect(T.po[:]), "crp%d po" % t, "cg", c=ga(C))
         pick(T.cw[:], T.wpb[:], T.cg[:], "wpb cg", "cw", cy(160))
         mv = T.cw[:, 15:C:16]
         tt(e1, mv, dq, Op.mult, "cw dq", "e1")
@@ -526,8 +540,8 @@ def rank_program(g, core, T, topo):
     dma("y", T.oc[:, 0:4 * HALF], T.qx[:, 0:HALF].bitcast(dt.uint8), "qxa3", "oca")
     dma("y", T.oc[:, 4 * HALF:4 * C], T.qx[:, HALF:C].bitcast(dt.uint8), "qxb3", "ocb")
     for k in range(4):
-        dma("y", T.osc[4 * k:4 * k + 4, :], T.sx[32 * k:32 * k + 4, :], "qxa3 qxb3", "osc%d" % k)
-    dma("s", T.y[:, 0:HALF], T.yb[:, 0:HALF], "yba", "ya")
+        dma("ys"[k % 2], T.osc[4 * k:4 * k + 4, :], T.sx[32 * k:32 * k + 4, :], "qxa3 qxb3", "osc%d" % k)
+    dma("y", T.y[:, 0:HALF], T.yb[:, 0:HALF], "yba", "ya")
     dma("s", T.y[:, HALF:C], T.yb[:, HALF:C], "ybb", "yb")
     add("g", lambda: g.wait_ge(T.sem.sent, nsent[0]), "r0 r1 r2 r3", "", 0.0, "w")
     emit(ops, g, T)

@@ -4,20 +4,27 @@ from concourse.mybir import dt, AluOpType as Op, ActivationFunctionType as Act
 C, P, NT, R = 320, 48, 96, 3
 STEP = [1, 2, 1]
 HB = 324
-XW = 4 * (HB + NT)
-OFF, BIG = 32768.0, 1048576.0
-FL = 336
+PW = 4 * (C + R * NT)
+OFF, BIG = 1024.0, 1048576.0
+FL = 1024
+DW = 336
+GS = 724.0
 KEY = 4097.0
 LAP = KEY * P
+NONE = C + 1 - 512.0
+EPS = 1.0 / 1024
+MV = 512.0
+RND = 12582912.0
 OW = 424
+M, GW = 12, 240
 HALF = 160
 XV = 144
-CYC, GATHER, SCATTER, WAKE, FAR, WIDE, NEAR, CALL = 0.00104, 1.56, 3.8, 0.15, 3.3, 5.2, 2.0, 0.5
-OTHER = [(0.1, 2.6, 4.3, 0.3), (0.2, 4.2, 6.5, 0.9)]
-TRIES = 12000
-LANES = {"v": 8, "s": 8, "p": 4, "g": 4}
-N20 = "e1 e2 e3 e4 e5 e6 vj pit p512 p513 kk xx l48 k2 dq zero fst".split()
-N48 = "mask qd zg c15 hs hh lt gg aa ea j48".split()
+CYC, GATHER, SCATTER, CALL = 0.00104, 1.56, 3.8, 0.5
+CASES = [(0.15, 2.0, 3.0, 4.5, 0.5, 1.0), (0.1, 1.6, 2.2, 3.8, 0.3, 1.1), (0.2, 2.2, 3.8, 5.5, 0.7, 0.9)]
+TRIES = 120000
+LANES = {"v": 32, "s": 32, "p": 8, "g": 8}
+N20 = "e1 e2 e3 e4 e6 pit kk zz l48 k2 dq ra rd rv fr nk".split()
+N48 = "qd hh lt gg aa ab2 ea n32 c16s vq".split()
 
 F, B16, I32, U16, Q4, U8 = "float32", "bfloat16", "int32", "uint16", "float8_e4m3fn_x4", "uint8"
 
@@ -27,26 +34,27 @@ def _s(n, d=F):
 
 
 SCRATCH = {
-    "x0": _s(XW, B16), "x1": _s(XW, B16), "x2": _s(XW, B16), "x3": _s(4 * C, B16),
+    "pool": _s(PW, B16), "x0": _s(4 * HB, B16), "x1": _s(4 * HB, B16), "x2": _s(4 * HB, B16), "x3": _s(4 * C, B16),
     "ub": _s(512, B16), "vb": _s(512, B16), "szb": _s(4, I32),
     "qu0": _s(128, Q4), "su0": _s(128, U8), "qu": _s(128, Q4), "su": _s(128, U8), "qv": _s(128, Q4), "sv": _s(128, U8),
     "qw": _s(512, Q4), "sw": _s(512, U8), "qe": _s(512, Q4), "se": _s(512, U8),
     "qx": _s(C, Q4), "sx": _s(C, U8), "qb": _s(128, Q4), "sb": _s(128, U8),
-    "ones": _s(528, B16), "eye": _s(528, B16), "dd": _s(4 * FL, B16),
-    "ta": _s(4 * NT, B16), "tb": _s(512, B16), "a64": _s(4 * NT), "tmp": _s(4 * NT),
+    "ones": _s(528, B16), "eye": _s(528, B16), "dd": _s(4 * DW, B16),
+    "ta": _s(4 * NT, B16), "tb": _s(512, B16), "a64": _s(4 * NT),
     "ps": ("psum", [128, 4096], F), "n20": _s(24 * len(N20)), "n48": _s(P * len(N48)),
-    "tm": _s(2 * FL), "tf0": _s(2 * FL, B16), "tf1": _s(2 * FL, B16), "stp": _s(656, B16),
-    "ip": _s(8, I32), "col": _s(24), "v512": _s(144), "j20": _s(20), "jw": _s(20),
-    "p16": _s(16), "p4": _s(16), "t4": _s(16), "wp16": _s(C), "wpb": _s(C, B16), "wp4": _s(C), "rst": _s(C, B16), "rs2": _s(NT, B16),
-    "base": _s(24), "t1s": _s(80), "t1a": _s(32), "t1": _s(192), "th": _s(192),
-    "dum": _s(12), "hid": _s(NT), "so": _s(48, U16), "qc": _s(4),
-    "sw_": _s(376), "mk": _s(P), "rm": _s(P), "pc": _s(8), "pm": _s(24, U16),
-    "ga": _s(P, B16), "gs": _s(P), "idx": _s(4, U16), "pw": _s(192), "pww": _s(192), "en": _s(64),
+    "tm": _s(FL + DW), "ip": _s(8, I32), "col": _s(24), "j20": _s(20), "jw": _s(20),
+    "jm": _s(C, B16), "wpa": _s(C, B16), "wp4": _s(C, B16), "j4": _s(C, B16), "rst": _s(P, B16), "r12": _s(GW, B16),
+    "base": _s(8), "t1": _s(192), "th": _s(192),
+    "dum": _s(8), "upk": _s(8, U16), "qc": _s(4),
+    "sw_": _s(376), "mk": _s(P), "rm": _s(P), "pc": _s(8), "pm": _s(8, U16),
+    "ga": _s(P, B16), "gs": _s(P), "idx": _s(4, U16), "tu": _s(104), "ub2": _s(56), "pww": _s(NT),
     "gt": _s(NT), "rj": _s(192), "own": _s(8), "ei": _s(8, I32), "ek": _s(8, I32),
-    "l9": _s(12), "lo": _s(10, U16), "crp": _s(R * 64 + 16, B16), "nf": _s(P, B16), "cg": _s(C, B16), "cw": _s(C, B16), "val": _s(C), "vw": _s(C),
-    "wg": _s(C, B16), "wr": _s(C, B16), "rr": _s(C, B16), "yg": _s(C), "s4": _s(16), "fo": _s(40, U16),
-    "vo": _s(20, U16), "do": _s(20, U16), "ow": _s(R * OW), "ao": _s(24, U16), "oww": _s(C), "xo": _s(80, U16),
-    "vq": _s(P), "mw": _s(472), "mr": _s(C), "mww": _s(C), "pib": _s(20, B16), "zs": _s(20), "lb": _s(20, B16), "po": _s(20, U16),
+    "en6": _s(8), "f6": _s(8), "l6": _s(8), "l9": _s(8), "lo": _s(8, U16), "ls": _s(4, U16),
+    "crp": _s(R * 64 + 16, B16), "cg": _s(C, B16), "cw": _s(C, B16), "val": _s(C), "vw": _s(C),
+    "d1": _s(GW, B16), "v1": _s(GW, B16), "ab": _s(GW, B16), "inc": _s(GW), "yg": _s(GW), "e16": _s(16),
+    "wg": _s(GW, B16), "wr": _s(GW, B16), "rr": _s(GW, B16),
+    "vo": _s(20, U16), "do": _s(20, U16), "ow": _s(OW), "slw": _s(C), "ao": _s(24, U16), "oww": _s(C), "xo": _s(80, U16),
+    "mw": _s(376), "mr": _s(C), "mww": _s(C), "pib": _s(20, B16), "lb": _s(20, B16), "po": _s(20, U16),
     "es": _s(64), "sc": _s(4), "mz": _s(P), "yb": _s(C),
 }
 for _t in range(R):
@@ -82,72 +90,86 @@ def depends(ops):
 def arrange(ops, deps):
     n = len(ops)
     if n in ORDER: return ORDER[n]
-    eng, cost = [o[0] for o in ops], [o[5] for o in ops]
-    lat = [{"d": NEAR, "r": FAR, "R": WIDE}.get(o[4], 0.0) + WAKE for o in ops]
+    eng = ["vspgy".index(o[0]) for o in ops]
+    deps = [sorted(d) for d in deps]
     users = [[] for o in ops]
     for i in range(n):
         for d in deps[i]: users[d].append(i)
-    base = [0.0] * n
-    for i in range(n - 1, -1, -1):
-        base[i] = cost[i] + lat[i] + max([base[u] for u in users[i]] + [0.0])
+    costs = [[call if o[4] in "rR" else o[5] * (f if o[4] == "c" else 1.0) for o in ops] for wake, near, far, wide, call, f in CASES]
+    lates = [[{"d": near, "r": far, "R": wide}.get(o[4], 0.0) + wake for o in ops] for wake, near, far, wide, call, f in CASES]
 
-    def again(order, wake, far, wide, call):
-        free, fin = {e: 0.0 for e in "vspgy"}, [0.0] * n
-        late = {"d": NEAR + wake, "r": far + wake, "R": wide + wake, "c": wake, "w": wake}
+    def play(order, k):
+        cost, late = costs[k], lates[k]
+        free, last, fin, start, held = [0.0] * 5, [-1] * 5, [0.0] * n, [0.0] * n, [-1] * n
         for c in order:
-            s = free[eng[c]]
+            e = eng[c]
+            s, h = free[e], last[e]
             for d in deps[c]:
-                if fin[d] > s: s = fin[d]
-            s += call if ops[c][4] in "rR" else cost[c]
-            free[eng[c]] = s
-            fin[c] = s + late[ops[c][4]]
-        return max(fin)
+                if fin[d] > s: s, h = fin[d], d
+            start[c], held[c] = s, h
+            s += cost[c]
+            free[e], last[e], fin[c] = s, c, s + late[c]
+        return max(fin), start, held, fin
 
-    def play(way, slack):
-        left, ready = [len(d) for d in deps], [0.0] * n
-        free, pool, cand = {e: 0.0 for e in "vspgy"}, {e: [] for e in "vspgy"}, {}
-        for i in range(n):
-            if not left[i]: pool[eng[i]].append(i)
-        order, end, tot, stale = [], 0.0, 0.0, "vspgy"
-        while len(order) < n:
-            for e in stale:
-                cand.pop(e, None)
-                if not pool[e]: continue
-                t = free[e]
-                c = top = max(pool[e], key=lambda i: way[i])
-                if ready[top] > t:
-                    lim = ready[top] + slack
-                    fit = [i for i in pool[e] if max(ready[i], t) + cost[i] <= lim]
-                    if fit: c = max(fit, key=lambda i: way[i] - max(0.0, ready[i] - t))
-                cand[e] = (max(t, ready[c]), c)
-            s, c = min(cand.values())
-            e = stale = eng[c]
-            pool[e].remove(c)
-            free[e] = s + cost[c]
-            end = max(end, free[e] + lat[c])
-            tot += free[e]
-            order.append(c)
-            for u in users[c]:
-                ready[u] = max(ready[u], free[e] + lat[c])
-                left[u] -= 1
-                if not left[u]:
-                    pool[eng[u]].append(u)
-                    if eng[u] not in stale: stale += eng[u]
-        return end + 8.0 * tot / n + sum(again(order, *a) for a in OTHER), order
+    def value(order):
+        r = [play(order, k) for k in range(len(CASES))]
+        return sum(a[0] for a in r) + sum(r[0][3]) / n, r
 
+    way = [0.0] * n
+    for i in range(n - 1, -1, -1):
+        way[i] = costs[0][i] + lates[0][i] + max([way[u] for u in users[i]] + [0.0])
+    left, ready, free, order = [len(d) for d in deps], [0.0] * n, [0.0] * 5, []
+    pool = [i for i in range(n) if not left[i]]
+    while pool:
+        t = min(max(ready[i], free[eng[i]]) for i in pool)
+        c = max((i for i in pool if max(ready[i], free[eng[i]]) <= t + 0.1), key=lambda i: way[i])
+        pool.remove(c)
+        order.append(c)
+        free[eng[c]] = max(ready[c], free[eng[c]]) + costs[0][c]
+        for u in users[c]:
+            ready[u] = max(ready[u], free[eng[c]] + lates[0][c])
+            left[u] -= 1
+            if not left[u]: pool.append(u)
     rng = np.random.RandomState(1)
-    way, slack = list(base), 0.1
-    best, order = play(way, slack)
-    now = best
-    for k in range(TRIES):
-        w, s = list(way), slack
-        for i in rng.randint(0, n, 1 + k % 3): w[int(i)] += float(rng.normal()) * 1.5
-        if k % 16 == 0: s = float(rng.uniform(0.0, 0.4))
-        e, o = play(w, s)
-        if e <= now + 0.05 * (1 - k / TRIES): now, way, slack = e, w, s
-        if e < best: best, order = e, o
-    ORDER[n] = order
-    return order
+    now, runs = value(order)
+    best, kept = now, order
+    pos = {c: i for i, c in enumerate(order)}
+    for step in range(TRIES):
+        end, start, held, fin = runs[step % len(CASES)]
+        if step % 3:
+            c, path = fin.index(end), []
+            while c >= 0:
+                if held[c] >= 0 and held[c] not in deps[c]: path.append(c)
+                c = held[c]
+            if not path: continue
+            c = path[rng.randint(len(path))]
+            p = held[c]
+            if rng.rand() < 0.5:
+                lo = max([pos[d] for d in deps[c]] + [-1]) + 1
+                if lo > pos[p]: continue
+                mates = [i for i in range(lo, pos[p] + 1) if eng[order[i]] == eng[c]][-4:]
+                to = mates[rng.randint(len(mates))]
+                new = order[:to] + [c] + order[to:pos[c]] + order[pos[c] + 1:]
+            else:
+                hi = min([pos[u] for u in users[p]] + [n])
+                if hi <= pos[c]: continue
+                mates = [i for i in range(pos[c], hi) if eng[order[i]] == eng[c]][:6]
+                to = mates[rng.randint(len(mates))]
+                new = order[:pos[p]] + order[pos[p] + 1:to + 1] + [p] + order[to + 1:]
+        else:
+            c = rng.randint(n)
+            lo, hi = max([pos[d] for d in deps[c]] + [-1]) + 1, min([pos[u] for u in users[c]] + [n])
+            to = rng.randint(max(lo, pos[c] - 30), min(hi, pos[c] + 30))
+            new = order[:pos[c]] + order[pos[c] + 1:]
+            new.insert(to, c)
+        v, r = value(new)
+        if v <= now + 0.25 * (1 - step / TRIES) * rng.rand():
+            order = sorted(new, key=lambda i: r[0][1][i])
+            pos = {c: i for i, c in enumerate(order)}
+            now, runs = v, r
+            if v < best: best, kept = v, order
+    ORDER[n] = [int(c) for c in kept]
+    return ORDER[n]
 
 
 def emit(ops, g, T):
@@ -215,6 +237,8 @@ def rank_program(g, core, T, topo):
 
     def ga(n): return 0.05 + n * GATHER * CYC
 
+    def sca(n): return 0.05 + n * SCATTER * CYC
+
     def ts(out, in0, s1, o0, s2, o1, rd, wr, c=0.067):
         if o1 is None: add("v", lambda: V.tensor_scalar(out, in0, s1, None, o0), rd, wr, c)
         else: add("v", lambda: V.tensor_scalar(out, in0, s1, s2, o0, o1), rd, wr, c)
@@ -236,7 +260,7 @@ def rank_program(g, core, T, topo):
         else: add("s", lambda: S.activation(out, a, f or Act.Identity, bias=bias, scale=scale), rd, wr, c)
 
     def sfill(out, v, wr, n):
-        act(out, T.tm[:, 0:n], "tm", wr, 0.0, v, cy(n))
+        act(out, T.ones[:, 0:n], "ones", wr, 0.0, v, cy(n))
 
     def quant(q, s, a, rd, wr, n=128):
         add("v", lambda: V.quantize_mx(q, s, a), rd, wr, 0.015 + 0.0011 * n)
@@ -254,29 +278,30 @@ def rank_program(g, core, T, topo):
         q = {"y": g.sync, "s": S, "g": g}[e]
         add(e, lambda: q.dma_start(out, a), rd, wr, 0.1, "d")
 
-    def send(dst, src, arr, t, part, rd, wr, kind):
+    def send(dst, src, arr, t, rd, wr, kind):
         mate = T.cores[rank ^ STEP[t]]
         rid, pid = topo.addr(mate)[0:2]
-        eng = topo.engines(core, mate)
-        k = len(eng) // 2
-        eng = (eng[:k], eng[k:], eng)[part]
-        add("g", lambda: g.remote_dma(dst, src, arr, T.sem.sent, pid, rid, sum(1 << e for e in eng)), rd, wr, CALL, kind)
-        nsent[0] += len(eng)
-        return len(eng)
+        add("g", lambda: g.remote_dma(dst, src, arr, T.sem.sent, pid, rid, topo.mask(core, mate)), rd, wr, CALL, kind)
+        k = len(topo.engines(core, mate))
+        nsent[0] += k
+        return k
 
     def pick(out, pat, src, rd, wr, c):
         scan(out, pat, src, 0.0, Op.add, Op.min, rd, wr, c)
 
-    def rev(buf, a, on=True):
-        if not (flip and on): return buf[:, a:a + P]
-        return buf[:, a + P - 1:a - 1:-1] if a else buf[:, P - 1::-1]
+    def rev(buf, a, on=True, n=P):
+        if not (flip and on): return buf[:, a:a + n]
+        return buf[:, a + n - 1:a - 1:-1] if a else buf[:, n - 1::-1]
 
     X = [T.x0, T.x1, T.x2, T.x3]
     col = T.col
-    ci, cr, ct, c16, c4, csp, c36, cd, c16b, c161, cf, cz, c4a, cq, co0, co1, cs = (col[:, k:k + 1] for k in range(17))
-    e1, e2, e3, e4, e5, e6, vj, pit, p512, p513, kk, xx, l48, k2, dq, zero, fst = (T.n20[:, 24 * k:24 * k + 20] for k in range(len(N20)))
-    mask, qd, zg, c15, hs, hh, lt, gg, aa, ea, j48 = (T.n48[:, P * k:P * k + P] for k in range(len(N48)))
-    repi, upk = T.so[:, 20:40], T.so[:, 40:48]
+    ci, cr, ct, c16, c4, csp, c36, cd, c161, c16m, cz, c4a, cq, cs, cf0, cf1, cl, ck = (col[:, k:k + 1] for k in range(18))
+    e1, e2, e3, e4, e6, pit, kk, zz, l48, k2, dq, ra, rd2, rv, fr, nk = (T.n20[:, 24 * k:24 * k + 20] for k in range(len(N20)))
+    qd, hh, lt, gg, aa, ab2, ea, n32, c16s, vq = (T.n48[:, P * k:P * k + P] for k in range(len(N48)))
+    at = {k: P * i for i, k in enumerate(N48)}
+    HID, T1S, RS2, T1A = DW, DW + R * NT, DW + R * NT + 80, FL - 32
+    mask, zg, hs, j48 = (T.tm[:, RS2 + NT + P * k:RS2 + NT + P * k + P] for k in range(4))
+    tmk = "tm tm2 hid t1s0 t1s1 t1s2 rs2 mask zg hs j48 t1a t1b idx"
 
     dma("y", T.szb[:, 0:3], T.sz[:], "", "szb")
     dma("s", T.ub[:], T.u[:], "", "ub")
@@ -288,90 +313,76 @@ def rank_program(g, core, T, topo):
 
     fill(T.ones[:], 1.0, "ones", cy(264))
     iota(T.ip[:, 0:1], [[0, 1]], 0, 1, "ip", False)
-    iota(T.tm[:, 0:FL], [[1, FL]], 0, 0, "tm")
+    iota(T.tm[:, 0:DW], [[1, DW]], 0, 0, "tm")
     iota(j48, [[16, 3], [0, 16]], 0, 0, "j48")
     iota(T.j20[:], [[16, 20]], 0, 0, "j20")
-    iota(T.v512[:], [[512, 144]], 0, 0, "v512")
+    iota(T.jm[:, 0:NT], [[0, NT // 16], [1, 16]], 0, 0, "jm")
+    iota(T.j4[:], [[0, C // 4], [1, 4]], 0, 0, "j4")
     if flip: iota(qd, [[-1, 12], [0, 4]], 11, 0, "qd")
     else: iota(qd, [[1, 12], [0, 4]], 0, 0, "qd")
-    iota(T.t4[:], [[0, 4], [1, 4]], 0, 0, "t4")
-    iota(T.base[:, 20:24], [[64, 4]], 0, 0, "base1")
-    iota(T.hid[:], [[1, NT]], HB, 0, "hid")
+    fill(T.base[:, 0:4], 0.0, "base1")
+    iota(T.base[:, 4:8], [[64, 4]], 0, 0, "base0")
+    iota(T.tm[:, HID:HID + R * NT], [[1, R * NT]], C, 0, "hid")
     iota(hs, [[int(KEY), P]], int(KEY), 0, "hs")
-    for t in range(R): iota(T.ow[:, OW * t + C:OW * t + OW], [[0, OW - C]], C, 0, "ow%d" % t)
-    iota(T.th[:], [[0, 192]], int(C + LAP), 0, "th")
+    iota(T.ow[:], [[0, OW]], C, 0, "ow")
+    iota(T.th[:], [[0, 192]], int(NONE), 0, "th")
     add("g", lambda: g.affine_select(T.eye[:], T.ones[:], [[1, 528]], Op.is_equal, 0.0, -3, -4), "ones", "eye", 1.27)
+    add("g", lambda: g.affine_select(T.r12[:], T.ones[:, 0:GW], [[0, 20], [1, M]], Op.not_equal, 0.0, 0, 0), "ones", "r12", 0.67)
     fill(T.t1[:], 0.0, "t1", cy(192))
-    fill(T.ow[:, 0:R * OW:OW], 0.0, "owz")
-    fill(c15, 1.5, "c15")
-    fill(T.en[:, P:64], 4096.0, "en")
-    fill(T.en[:, 0:1], 0.0, "enz")
+    fill(T.tu[:, 0:1], 0.0, "enz")
+    fill(T.ub2[:, 0:1], 0.0, "ubz")
     fill(T.sw_[:, C + 1:376], -1e29, "swz")
     fill(T.sw_[:, 0:1], -1e29, "swy")
-    fill(T.rst[:], 1.0, "rst", cy(160))
-    fill(T.rst[:, 0:C:16], 0.0, "rst")
-    fill(T.rs2[:], 1.0, "rs2")
-    fill(T.rs2[:, 0:NT:32], 0.0, "rs2")
-    fill(T.es[:, P:64], -1.0 / 48, "esz")
-    fill(zero, 0.0, "zero")
-    fill(T.tf0[:], 0.0, "tf0", cy(FL))
-    fill(T.tf0[:, 0:2 * FL:FL], 1024.0, "tf0")
-    fill(T.tf1[:], -1.0, "tf1", cy(FL))
-    fill(T.tf1[:, 0:2], 1024.0, "tf1")
-    fill(T.tf1[:, FL:FL + 2], 1024.0, "tf1")
-    fill(T.t1s[:, 0:32], 0.0, "t1s0")
-    fill(T.t1s[:, P:80], -1.0, "t1s2")
+    fill(T.rst[:], 1.0, "rst")
+    fill(T.rst[:, 0:P:16], 0.0, "rst")
+    fill(T.tm[:, RS2:RS2 + NT], 0.0, "rs2", cy(NT))
+    fill(T.tm[:, RS2:RS2 + NT:32], -4 * BIG, "rs2")
+    fill(T.es[:, P:64], 192.49, "esz")
+    fill(c16s, 16.0, "c16s")
+    fill(T.d1[:], -1.0, "d1", cy(GW // 2))
+    fill(T.tm[:, T1S:T1S + 32], 0.0, "t1s0")
+    fill(T.tm[:, T1S + P:T1S + 80], -1.0, "t1s2")
     for t in range(R): sfill(X[t][:, 4 * C:4 * HB], 0.0, "x%dz" % t, 16)
-    for b in range(4): sfill(T.dd[:, FL * b + C:FL * b + FL], 0.0, "ddz%d" % b, 16)
-    sfill(T.mw[:, 0:C], 0.0, "mw", C)
-    sfill(T.mw[:, C:472], 0.0, "mwz", 472 - C)
+    sfill(T.dd[:, C:4 * DW:DW], 0.0, "ddz", 4)
+    sfill(T.mw[:], 0.0, "mw", 376)
     sfill(T.tb[:, 4 * NT:512], 0.0, "tbz", 128)
-    sfill(T.stp[:, 0:C], 1.0, "stp0", C)
-    sfill(T.stp[:, C + 16:656], 0.0, "stp2", C)
-    act(T.tm[:, FL:2 * FL], T.tm[:, 0:FL], "tm", "tm2", c=cy(FL))
+    act(T.tm[:, FL:FL + DW], T.tm[:, 0:DW], "tm", "tm2", c=cy(DW))
+    for k in range(4):
+        act(T.pool[:, C * k:C * k + C], T.x0[:, C * k:C * k + C], "x0a x0b x0c", "p%d" % k, 64.0, c=cy(C))
     ts(T.ip[:, 1:2], T.ip[:, 0:1], 15, Op.bitwise_and, None, None, "ip", "ip1")
     ts(T.ip[:, 2:3], T.ip[:, 0:1], 2, Op.arith_shift_right, 3, Op.bitwise_and, "ip", "ip2")
     ts(T.ip[:, 3:4], T.ip[:, 0:1], 3, Op.bitwise_and, None, None, "ip", "ip3")
     cp(ci, T.ip[:, 1:2], "ip1", "ci")
     cp(col[:, 1:3], T.ip[:, 2:4], "ip2 ip3", "cr")
-    act(c16, ci, "ci", "c16", -OFF, 15 * OFF)
-    act(c16b, ci, "ci", "c16b", -OFF / 4, 15 * OFF / 4)
-    act(c161, ci, "ci", "c161", -OFF, 15 * OFF + 1)
-    act(co0, ci, "ci", "co0", -OFF, 15 * OFF + 1023)
-    act(co1, ci, "ci", "co1", -OFF, 15 * OFF + 511)
-    act(cs, ci, "ci", "cs", -OFF, 15 * OFF + FL - 2.5)
-    act(c36, ci, "ci", "c36", 1.0, 36.0)
-    act(cd, ci, "ci", "cd", OFF + 1, C + 1 - 15 * OFF)
-    act(cf, ci, "ci", "cf", -OFF, 15 * OFF + C)
-    act(cz, ci, "ci", "cz", sg / 48, (23.5 + 47 * flip) / 48 - 192)
-    act(cq, ci, "ci", "cq", sg, 15.0 * flip)
+    for k, nm, a, b in ((c16, "c16", -OFF, 15 * OFF), (c161, "c161", -OFF, 15 * OFF + 1), (c16m, "c16m", -OFF, 15 * OFF - 1),
+                        (cs, "cs", OFF, FL - 1 - 15 * OFF), (cf0, "cf0", 4096 * OFF, 2048 - 4096 * 15 * OFF),
+                        (cf1, "cf1", 4096 * OFF, 6144 - 4096 * 15 * OFF), (c36, "c36", 1.0, 36.0), (cd, "cd", 1.0, C + 1.0),
+                        (cz, "cz", sg / 48, 47.0 * flip / 48), (cq, "cq", sg, 15.0 * flip),
+                        (cl, "cl", -OFF / 16, 15 * OFF / 16 + 192 - 0.31), (ck, "ck", 32 * OFF, -32 * 15 * OFF)):
+        act(k, ci, "ci", nm, a, b)
     act(c4a, cr, "cr", "c4a", -4 * OFF, 12 * OFF)
     act(c4, ct, "cr c4a", "c4", 1.0, c4a)
     ts(csp, ci, 12.0, Op.is_ge, c36, Op.mult, "ci c36", "csp")
-    ts(repi, zero, ci, Op.add, None, None, "ci zero", "repi")
-    ts(T.p16[:], T.tm[:, 0:16], ci, Op.is_equal, BIG + OFF, Op.mult, "tm ci", "p16")
-    ts(T.p4[:], T.t4[:], cr, Op.is_equal, BIG + OFF, Op.mult, "t4 cr", "p4")
-    ts(T.stp[:, C:C + 16], T.tm[:, 0:16], ci, Op.is_le, None, None, "tm ci", "stp1")
-    ts(T.t1a[:, 0:16], T.tm[:, 0:16], cq, Op.is_equal, 4097.0, Op.mult, "tm cq", "t1a")
-    ts(T.t1a[:, 16:32], T.tm[:, 0:16], cq, Op.is_ge, None, None, "tm cq", "t1b")
-    tt(T.t1s[:, 32:P], T.t1a[:, 0:16], T.t1a[:, 16:32], Op.subtract, "t1a t1b", "t1s1")
-    act(T.wp16[:, 0:192], T.p16[:].indirect(T.so[:, 20:32]), "p16 repi", "wp16", bias=-OFF, c=ga(192))
-    act(T.wp16[:, 192:C], T.wp16[:, 0:128], "wp16", "wp16x", c=cy(128))
-    act(T.wpb[:], T.wp16[:], "wp16 wp16x", "wpb", 0.25, c=cy(C))
-    act(T.wp4[:], T.p4[:].indirect(repi), "p4 repi", "wp4", bias=-OFF, c=ga(C))
-    cp(upk, T.j20[:, 0:8], "j20", "upk")
-    act(T.crp[:, 0:R * 64], T.tm[:, 0:R * 64], "tm c16b", "crp0 crp1 crp2", 0.0, c16b, cy(R * 64))
-    act(T.crp[:, R * 64:R * 64 + 16], T.crp[:, 0:16], "crp0", "crs", 1.0, 4096.0)
-    act(T.base[:, 0:20], zero, "zero csp", "base0", 1.0, csp)
-    act(T.base[:, 20:24], T.base[:, 20:24], "base1 csp", "base1", 1.0, csp)
-    act(T.dum[:, 0:9], T.j20[:, 0:9], "j20 cd", "dum", 1.0, cd)
+    ts(T.jm[:, 0:NT], T.jm[:, 0:NT], ci, Op.is_equal, BIG, Op.mult, "jm ci", "jm")
+    ts(T.wpa[:, 0:NT], T.jm[:, 0:NT], -OFF, Op.add, None, None, "jm", "wpa")
+    act(T.wpa[:, NT:2 * NT], T.wpa[:, 0:NT], "wpa", "wpb", c=cy(NT))
+    act(T.wpa[:, 2 * NT:C], T.wpa[:, 0:C - 2 * NT], "wpa wpb", "wpc", c=cy(C - 2 * NT))
+    ts(T.j4[:], T.j4[:], cr, Op.is_equal, BIG, Op.mult, "j4 cr", "j4", cy(C // 2))
+    act(T.wp4[:], T.j4[:], "j4", "wp4", 1.0, -OFF, cy(C))
+    ts(T.tm[:, T1A:T1A + 16], T.tm[:, 0:16], cq, Op.is_equal, 4097.0, Op.mult, "tm cq", "t1a")
+    ts(T.tm[:, T1A + 16:FL], T.tm[:, 0:16], cq, Op.is_ge, None, None, "tm cq", "t1b")
+    tt(T.tm[:, T1S + 32:T1S + P], T.tm[:, T1A:T1A + 16], T.tm[:, T1A + 16:FL], Op.subtract, "t1a t1b", "t1s1")
+    cp(T.upk[:], T.j20[:, 0:8], "j20", "upk")
+    act(T.crp[:, 0:R * 64], T.ones[:, 0:R * 64], "ones c16", "crp0 crp1 crp2", 0.0, c16, cy(R * 64))
+    act(T.crp[:, R * 64:R * 64 + 16], T.crp[:, 0:16], "crp0", "crs", 1.0, MV)
+    act(T.base[:], T.base[:], "base0 base1 csp", "base0 base1", 1.0, csp)
+    act(T.dum[:, 0:6], T.j20[:, 0:6], "j20 cd", "dum", 1.0, cd)
     act(T.jw[:], T.j20[:], "j20 ci", "jw", 1.0, ci)
-    act(T.qc[:, 0:3], T.jw[:, 0:3], "jw", "qc", sg * KEY, 2048 + 47 * KEY * flip)
-    act(fst, T.j20[:], "j20 cf", "fst", -1.0, cf)
+    act(T.qc[:, 0:3], T.jw[:, 0:3], "jw", "qc", sg * KEY, 2049 + 47 * KEY * flip)
     act(zg, j48, "j48 cz", "zg", sg / 48, cz)
     quant(T.qu0[:], T.su0[:], T.ub[:], "ub", "qu0")
-    add("s", lambda: S.activation(T.su[:], T.su0[:].indirect(upk), Act.Copy), "qu0 upk", "su", ga(128))
-    cp(T.qu[:].bitcast(dt.uint32), T.qu0[:].bitcast(dt.uint32).indirect(upk), "qu0 upk", "qu", ga(128))
+    add("s", lambda: S.activation(T.su[:], T.su0[:].indirect(T.upk[:]), Act.Copy), "qu0 upk", "su", ga(128))
+    cp(T.qu[:].bitcast(dt.uint32), T.qu0[:].bitcast(dt.uint32).indirect(T.upk[:]), "qu0 upk", "qu", ga(128))
     ts(mask, qd, ci, Op.is_equal, 3e29, Op.mult, "qd ci", "mask")
     act(mask, mask, "mask", "mask", 1.0, -2e29)
     for b in range(4):
@@ -380,61 +391,69 @@ def rank_program(g, core, T, topo):
     cp(T.idx[:, 0:3], T.szb[:, 0:3], "szb", "idx")
 
     idx = T.idx[:, 0:3]
-    un = rev(T.pw, 144)
+    un = T.tu[:, P + 1:2 * P + 1]
+    pe, pn = ((P + 15, 15) if flip else (15, P + 15))
+    endp, sizp = T.pww[:, pe:pe + 33:16], T.pww[:, pn:pn + 33:16]
 
     def sizes(first):
-        win = T.tm[:, 0:FL] if first else T.tm[:]
-        act(rev(T.pw, 144, first), win.indirect(idx), "tm idx" if first else "tm tm2 idx", "un", -1.0, 1.5, ga(P))
-        scan(T.en[:, 1:P + 1], c15, un, 0.0, Op.add, Op.subtract, "c15 un", "en")
+        win, wk = (T.tm[:, 0:DW], "tm idx") if first else (T.tm[:], tmk)
+        act(rev(T.tu, P + 1, not first), win.indirect(idx), wk, "un", 1.0 + EPS, c=ga(P))
+        act(rev(T.ub2, 1, not first), win.indirect(idx), wk, "ub2", -EPS, c=ga(P))
+        scan(T.tu[:, 1:P + 1], un, T.ub2[:, 0:P], 0.0, Op.add, Op.add, "un ub2 ubz", "en")
 
-    def places(first, last):
-        tt(rev(T.pw, 0, first), T.tf0[:].indirect(idx), rev(T.en, 1, not first), Op.add, "tf0 idx en", "pw0", ga(P))
-        tt(rev(T.pw, P, first), T.tf1[:].indirect(idx), rev(T.en, 1, not first), Op.add, "tf1 idx en", "pw1", ga(P))
-        n, k = (NT, 6) if last else (192, 9)
-        if not last: tt(rev(T.pw, 96, first), T.tf0[:].indirect(idx), rev(T.en, 0, not first), Op.add, "tf0 idx en enz", "pw2", ga(P))
-        pick(T.pww[:, 0:n], T.wp16[:, 0:n], T.pw[:, 0:n], "wp16 pw0 pw1 pw2 un", "pww", cy(n))
-        tt(T.l9[:, 0:k], T.pww[:, 15:16 * k:16], T.dum[:, 0:k], Op.min, "pww dum", "l9")
-        ts(T.lo[:, 0:k], T.l9[:, 0:k], c16, Op.add, None, None, "l9 c16", "lo")
+    def places(last):
+        pick(T.pww[:], T.wpa[:, 0:NT], rev(T.tu, 1, n=NT), "wpa en un", "pww", cy(NT))
+        act(T.en6[:, 0:3], endp, "pww c16", "en6a", 1.0, c16)
+        act(T.en6[:, 3:6], endp, "pww c16m", "en6b", 1.0, c16m)
+        act(T.f6[:, 0:3], sizp, "pww cf0", "f6a", -4096.0, cf0, f=Act.Relu)
+        act(T.f6[:, 3:6], sizp, "pww cf1", "f6b", -4096.0, cf1, f=Act.Relu)
+        tt(T.l6[:, 0:6], T.en6[:, 0:6], T.f6[:, 0:6], Op.add, "en6a en6b f6a f6b", "l6")
+        tt(T.l9[:, 0:6], T.l6[:, 0:6], T.dum[:, 0:6], Op.min, "l6 dum", "l9")
+        cp(T.lo[:, 0:6], T.l9[:, 0:6], "l9", "lo")
 
     def tables():
-        tt(ea, T.tm[:, 0:P], un, Op.subtract, "tm un", "ea", cy(96))
-        act(T.es[:, 0:P], ea, "ea", "es", 1.0 / 48, 1.5 / 48)
-        act(T.sc[:, 0:3], T.pww[:, 159:192:16], "pww cs", "sc", 1.0, cs)
-        act(T.t1[:, P:192:64], T.sc[:, 0:3], "sc t1", "t1n", -11.0, 1.0 - FL)
-        tt(hh, T.en[:, 0:P], hs, Op.subtract, "en enz hs", "hh", cy(96))
+        tt(ea, T.tm[:, 0:P], un, Op.add, "tm un", "ea", cy(96))
+        act(T.es[:, 0:P], ea, "ea", "es", 1.0 / 48, 191.5 + 0.3 / 48)
+        act(T.sc[:, 0:3], sizp, "pww cs", "sc", -1.0, cs)
+        act(T.t1[:, P:192:64], T.sc[:, 0:3], "sc t1", "t1n", -11.0, 3060 - (FL - 1) + GS)
+        tt(hh, T.tu[:, 0:P], hs, Op.subtract, "en enz hs", "hh", cy(96))
         for c in range(3):
-            a = 16 * c if flip else 32 - 16 * c
-            act(T.t1[:, 64 * c:64 * c + P], T.t1s[:, a:a + P], "sc t1s0 t1s1 t1s2 t1", "t1%d" % c, -1.0, T.sc[:, c:c + 1], f=Act.Relu)
+            a = T1S + (16 * c if flip else 32 - 16 * c)
+            act(T.t1[:, 64 * c:64 * c + P], T.tm[:, a:a + P], "sc t1s0 t1s1 t1s2 t1", "t1%d" % c, -1.0, T.sc[:, c:c + 1], f=Act.Relu)
             act(T.th[:, 64 * c:64 * c + P], hh, "hh qc th", "th%d" % c, 1.0, T.qc[:, c:c + 1])
-        ts(T.own[:, 0:3], T.pww[:, 15:48:16], co0, Op.add, 1024.0 + C, Op.min, "pww co0", "own0")
-        ts(T.own[:, 3:6], T.pww[:, 63:96:16], co1, Op.add, 512.0 + C, Op.min, "pww co1", "own1")
+        tt(T.own[:, 0:6], T.en6[:, 0:6], T.f6[:, 0:6], Op.subtract, "en6a en6b f6a f6b", "own")
 
-    def labels(v):
-        tt(T.vq[:], rev(T.v512, P * v), rev(T.en, 0), Op.add, "v512 en enz", "vq", cy(96))
-        cp(T.mw[:].indirect(T.lo[:, 6:9]), T.vq[:], "vq lo mw mwz", "mw", 0.05 + P * SCATTER * CYC)
+    def first_labels():
+        act(n32, T.tm[:, 0:DW].indirect(idx), "tm idx", "n32", 1.0 / 32, c=ga(P))
+        fill(vq[:, 0:1], 0.0, "vq0")
+        scan(vq[:, 1:P], n32[:, 0:P - 1], c16s[:, 1:P], 0.0, Op.add, Op.add, "n32 c16s", "vq")
+        tt(e1[:, 0:3], T.l6[:, 0:3], sizp, Op.subtract, "l6 pww", "e1")
+        ts(e2[:, 0:3], e1[:, 0:3], c16, Op.subtract, 0.4, Op.add, "e1 c16", "e2")
+        tt(e3[:, 0:3], e2[:, 0:3], T.dum[:, 0:3], Op.min, "e2 dum", "e3")
+        cp(T.ls[:, 0:3], e3[:, 0:3], "e3", "ls")
+        cp(T.mw[:].indirect(T.ls[:, 0:3]), rev(T.n48, at["vq"]), "vq vq0 ls mw", "mw", sca(P))
         scan(T.mr[:], T.mw[:, 0:C], T.mw[:, 0:C], 0.0, Op.max, Op.max, "mw", "mr", cy(C))
-        pick(T.mww[:], T.wp16[:], T.mr[:], "wp16 wp16x mr", "mww", cy(C))
-        act(vj, T.mww[:, 15:C:16], "mww c16", "vj", 1.0, c16)
-        act(T.pib[:], vj, "vj", "pib", 1.0 / 512, 192 - 0.31 - P * v)
-        act(pit, T.pib[:], "pib", "pit", 1.0, -192.0)
-        act(p512, T.pib[:], "pib", "p512", 512.0, 512.0 * (P * v - 192))
-        act(p513, T.pib[:], "pib", "p513", 513.0, 512.0 * P * v - 513.0 * 192)
-        cp(T.po[:], pit, "pit", "po")
-        tt(e5, T.jw[:], vj, Op.subtract, "vj jw", "e5")
-        tt(kk, e5, p512, Op.add, "e5 p512", "kk")
-        tt(xx, e5, p513, Op.add, "e5 p513", "xx")
-        act(T.zs[:], xx, "xx", "zs", 1.0 / 48, 24.5 / 48 - 192)
-        act(T.lb[:], xx, "xx", "lb", 1.0 / 48, 192 - 22.5 / 48)
-        act(l48, T.lb[:], "lb", "l48", 48.0 / 4096, -(192 * 48.0 + 2) / 4096)
-        act(k2, kk, "kk", "k2", 1.0 / 4096)
-        tt(dq, k2, l48, Op.subtract, "k2 l48", "dq")
+        pick(T.mww[:], T.wpa[:], T.mr[:], "wpa wpb wpc mr", "mww", cy(C))
+        act(T.pib[:], T.mww[:, 15:C:16], "mww cl", "pib", 1.0 / 16, cl)
+        act(ra, T.mww[:, 15:C:16], "mww ck", "ra", -32.0, ck)
+        act(rv, T.pib[:], "pib", "rv", 512.0, -512.0 * 192)
+        tt(fr, T.jw[:], ra, Op.add, "jw ra", "fr")
+        tt(kk, fr, rv, Op.add, "fr rv", "kk")
 
-    def grid():
-        pick(T.s4[:], T.wp16[:, 0:16], T.en[:, 0:64:4], "wp16 en enz", "s4", cy(16))
-        ts(T.fo[:, 0:40:2], fst, T.s4[:, 15:16], Op.add, 655.0, Op.min, "fst s4", "fo")
-        for c in range(20):
-            act(T.yg[:, 16 * c:16 * c + 16], T.stp[:].indirect(T.fo[:, 2 * c:2 * c + 1]), "stp0 stp1 stp2 fo zs", "yg%d" % c,
-                -1.0, T.zs[:, c:c + 1], 0.1)
+    def labels():
+        act(pit, T.pib[:], "pib", "pit", 1.0, -192.0)
+        act(T.d1[:, 0:GW:M], T.pib[:], "pib d1", "d1", 0.25, 144 - 0.375)
+        cp(T.po[:], pit, "pit", "po")
+        tt(zz, kk, pit, Op.add, "kk pit", "zz")
+        act(T.lb[:], zz, "zz", "lb", 1.0 / 48, 191.5 + 1.5 / 48)
+        act(l48, T.lb[:], "lb", "l48", 48.0 / MV, -(192 * 48.0 + 1.75) / MV)
+        act(k2, kk, "kk", "k2", 1.0 / MV)
+        tt(dq, k2, l48, Op.subtract, "k2 l48", "dq")
+        scan(T.v1[:], T.r12[:], T.d1[:], 0.0, Op.mult, Op.add, "r12 d1", "v1", cy(GW // 2))
+        act(T.ab[:], T.v1[:], "v1", "ab", 1.0, -191.0, cy(GW), Act.Abs)
+        act(T.inc[:], T.ab[:], "ab", "inc", -1.0, 1.0, cy(GW), Act.Relu)
+        act(T.inc[:, 0:GW:M], zz, "zz inc", "inc", 1.0 / 48, 1.0 / 48 - 1)
+        scan(T.yg[:], T.r12[:], T.inc[:], 0.0, Op.mult, Op.add, "r12 inc", "yg", cy(GW))
 
     def pack(t, wq, ws, wk, out, ok):
         qx, sx = (T["qx%d" % t], T["sx%d" % t]) if t < R else (T.qx, T.sx)
@@ -445,96 +464,105 @@ def rank_program(g, core, T, topo):
             act(out(a, n), T.ps[:, 512 * h:512 * h + n], "ps%d" % h, ok + nm + " ps%d" % h, c=cy(n))
 
     sizes(True)
-    places(True, False)
+    places(False)
     tables()
-    labels(0)
-    grid()
-    ygk = " ".join("yg%d" % c for c in range(20))
+    first_labels()
+    labels()
+    pool = "p0 p1 p2 p3"
     for t in range(R):
         xk = "x%da x%db x%dc x%dz" % (t, t, t, t)
-        ow = T.ow[:, OW * t:OW * t + OW]
-        ok = "ow%d" % t
         pack(t, T.qu[:], T.su[:], "qu su", lambda a, n: T.sw_[:, 1 + a:1 + a + n], "sw")
         qx, sx, ql, sl, arr = T["qx%d" % t], T["sx%d" % t], T["ql%d" % t], T["sl%d" % t], T.sem["arr%d" % t]
-        na = send(ql[:, 0:HALF].bitcast(dt.uint8), qx[:, 0:HALF].bitcast(dt.uint8), arr, t, 0, "qxa%d" % t, "r0", "R")
-        na += send(ql[:, HALF:C].bitcast(dt.uint8), qx[:, HALF:C].bitcast(dt.uint8), arr, t, 1, "qxb%d" % t, "r1", "R")
-        na += send(sl[:], sx[:], arr, t, 0, "qxa%d qxb%d" % (t, t), "r2", "R")
-        add("p", lambda arr=arr, n=na: g.tensor.wait_ge(arr, n), "r0 r1 r2", "ql%d" % t, 0.0, "w")
+        na = send(ql[:].bitcast(dt.uint8), qx[:].bitcast(dt.uint8), arr, t, "qxa%d qxb%d" % (t, t), "r0", "R")
+        na += send(sl[:], sx[:], arr, t, "qxa%d qxb%d" % (t, t), "r1", "R")
+        add("p", lambda arr=arr, n=na: g.tensor.wait_ge(arr, n), "r0 r1", "ql%d" % t, 0.0, "w")
         for b in range(4):
             mm(4 + b, C, T.qe[:, 128 * b:128 * b + 128], T.se[:, 128 * b:128 * b + 128], ql[:], sl[:], "qe%d ql%d" % (b, t))
-            act(T.dd[:, FL * b:FL * b + C], T.ps[:, 512 * (4 + b):512 * (4 + b) + C], "ps%d" % (4 + b), "dd%d ps%d" % (b, 4 + b), c=cy(C))
+            act(T.dd[:, DW * b:DW * b + C], T.ps[:, 512 * (4 + b):512 * (4 + b) + C], "ps%d" % (4 + b), "dd%d ps%d" % (b, 4 + b), c=cy(C))
         tt(T.mk[:], T.sw_[:].indirect(T.lo[:, 0:3]), mask, Op.min, "swa swb swz swy lo mask", "mk", ga(P))
         scan(T.rm[:], rev(T.mk, 0), rev(T.mk, 0), -3e29, Op.max, Op.max, "mk", "rm")
         add("s", lambda: S.activation(lt, T.rm[:], Act.Sign, bias=T.rm[:, P - 1:P], scale=-1.0, accum_out=T.pc[:, 0:1]), "rm", "lt pc", 0.09)
-        ts(T.pm[:], T.base[:], T.pc[:, 0:1], Op.add, None, None, "pc base0 base1", "pm")
+        ts(T.pm[:], T.base[:], T.pc[:, 0:1], Op.add, None, None, "pc base0", "pm")
         crp = T.crp[:, 64 * t:64 * t + 64]
-        cp(crp.indirect(T.pm[:, 0:1]), T.crp[:, R * 64:R * 64 + 16], "pm crs crp%d" % t, "crp%d" % t, 0.05 + 16 * SCATTER * CYC)
-        pick(T.nf[:], T.wpb[:, 0:P], rev(T.crp, 64 * t), "wpb crp%d" % t, "nc", cy(24))
-        pm3, pm64 = T.pm[:, 0:3], T.pm[:, 20:23]
+        cp(crp.indirect(T.pm[:, 0:1]), T.crp[:, R * 64:R * 64 + 16], "pm crs crp%d" % t, "crp%d" % t, sca(16))
+        pm3, pm64 = T.pm[:, 0:3], T.pm[:, 4:7]
         tt(T.ga[:], T.es[:].indirect(pm3), zg, Op.subtract, "es esz pm zg", "ga", ga(P))
         tt(gg, T.t1[:].indirect(pm64), T.ga[:], Op.subtract, "t1 t1n t10 t11 t12 pm ga", "gg", ga(P))
-        scan(T.gs[:], T.rst[:, 0:P], gg, 0.0, Op.mult, Op.add, "rst gg", "gs")
-        ts(idx, T.gs[:, 15:P:16], -1.0, Op.mult, -191.0 * 16, Op.add, "gs", "idx")
+        scan(T.gs[:], T.rst[:], gg, 0.0, Op.mult, Op.add, "rst gg", "gs")
+        ts(idx, T.gs[:, 15:P:16], -1.0, Op.mult, GS + 0.1, Op.add, "gs", "idx")
         ts(aa, T.ga[:], -192.0, Op.add, LAP, Op.mult, "ga", "aa")
-        tt(T.gt[:, 1:NT:2], T.th[:].indirect(pm64), aa, Op.add, "th th0 th1 th2 pm aa", "g1", ga(P))
-        ts(T.gt[:, 0:NT:2], T.gt[:, 1:NT:2], -LAP, Op.add, None, None, "g1", "g2")
-        tt(T.gt[:, 25:NT:32], T.own[:, 0:3], T.nf[:, 15:P:16], Op.subtract, "nc own0 g1 g2", "g3")
-        tt(T.gt[:, 27:NT:32], T.own[:, 3:6], T.nf[:, 15:P:16], Op.subtract, "nc own1 g1 g2", "g4")
-        scan(T.rj[:, NT - 1::-1], T.rs2[:], T.gt[:, NT - 1::-1], 0.0, Op.mult, Op.max, "rs2 g1 g2 g3 g4", "rj0", cy(NT))
-        scan(T.rj[:, 2 * NT - 2:NT - 1:-1], T.gt[:, NT - 2::-1], T.rj[:, NT - 1:0:-1], float(C), Op.max, Op.min, "rj0 g1 g2 g3 g4", "rj1", cy(NT))
+        act(ab2, T.ga[:], "ga", "ab2", LAP, -193 * LAP)
+        tt(T.gt[:, 1:NT:2], T.th[:].indirect(pm64), aa, Op.add, "th th0 th1 th2 pm aa", "g1 g3 g4", ga(P))
+        tt(T.gt[:, 0:NT:2], T.th[:].indirect(pm64), ab2, Op.add, "th th0 th1 th2 pm ab2", "g2", ga(P))
+        tt(T.gt[:, 25:NT:32], T.own[:, 0:3], T.gs[:, 15:P:16], Op.min, "gs own", "g3")
+        tt(T.gt[:, 27:NT:32], T.own[:, 3:6], T.gs[:, 15:P:16], Op.min, "gs own", "g4")
+        scan(T.rj[:, NT - 1::-1], T.tm[:, RS2:RS2 + NT], T.gt[:, NT - 1::-1], 0.0, Op.add, Op.max, "rs2 g1 g2 g3 g4", "rj0", cy(NT))
+        scan(T.rj[:, 2 * NT - 2:NT - 1:-1], T.gt[:, NT - 2::-1], T.rj[:, NT - 1:0:-1], NONE, Op.max, Op.min, "rj0 g1 g2 g3 g4", "rj1", cy(NT))
         cp(T.ei[:, 0:6], T.rj[:, 0:2 * NT:32], "rj0 rj1", "ei")
         ts(T.ek[:, 0:6], T.ei[:, 0:6], 511, Op.bitwise_and, None, None, "ei", "ek")
         lm, lp, lis = T["lm%d" % t], T["lp%d" % t], T.sem["lis%d" % t]
-        cp(lm[:, 0:6], T.ek[:, 0:6], "ek", "lm%d" % t)
-        nl = send(lp[:, 0:6], lm[:, 0:6], lis, t, 2, "lm%d" % t, "r3", "r")
+        ts(lm[:, 0:6], T.ek[:, 0:6], -1.0, Op.add, None, None, "ek", "lm%d" % t)
+        nl = send(lp[:, 0:6], lm[:, 0:6], lis, t, "lm%d" % t, "r3", "r")
         win = X[t][:, 0:4 * HB]
         for b in range(4):
-            ts(T.ao[:, 6 * b:6 * b + 6], T.ek[:, 0:6], 4.0, Op.mult, float(b), Op.add, "ek", "ao%d" % b)
+            ts(T.ao[:, 6 * b:6 * b + 6], T.ek[:, 0:6], 4.0, Op.mult, b - 4.0, Op.add, "ek", "ao%d" % b)
             act(T.ta[:, b:4 * NT:4], win.indirect(T.ao[:, 6 * b:6 * b + 6]), "ao%d %s" % (b, xk), "ta%d" % b, c=ga(NT))
         act(T.a64[:], T.ta[:], "ta0 ta1 ta2 ta3", "a64", 64.0, c=cy(384))
         sizes(False)
         act(T.cg[:], crp.indirect(T.po[:]), "crp%d po" % t, "cg", c=ga(C))
-        pick(T.cw[:], T.wpb[:], T.cg[:], "wpb cg", "cw", cy(160))
+        pick(T.cw[:], T.wpa[:], T.cg[:], "wpa wpb wpc cg", "cw", cy(C // 2))
         mv = T.cw[:, 15:C:16]
         tt(e1, mv, dq, Op.mult, "cw dq", "e1")
         tt(e2, e1, pit, Op.add, "e1 pit", "e2")
-        cp(T.vo[:], e2, "e2", "vo")
-        act(T.val[:], T.en[:].indirect(T.vo[:]), "en enz vo c161", "val", 1.0, c161, ga(C))
-        pick(T.vw[:], T.wp16[:], T.val[:], "wp16 wp16x val", "vw", cy(C))
-        tt(T.wg[:], T.es[:].indirect(T.pm[:, 0:20]), T.yg[:], Op.subtract, "es esz pm " + ygk, "wg", ga(C))
-        ts(T.wr[:], T.wg[:], -192.0, Op.add, 0.0, Op.max, "wg", "wr", cy(160))
-        scan(T.rr[:], T.rst[:], T.wr[:], 0.0, Op.mult, Op.add, "rst wr", "rr", cy(160))
+        ts(T.vo[:], e2, 0.25, Op.add, None, None, "e2", "vo")
+        act(T.val[:], T.tu[:, 0:P + 1].indirect(T.vo[:]), "en enz vo c161", "val", 1.0, c161, ga(C))
+        pick(T.vw[:], T.wpa[:], T.val[:], "wpa wpb wpc val", "vw", cy(C))
+        vw = T.vw[:, 15:C:16]
+        act(T.e16[:], T.es[:].indirect(T.pm[:, 0:1]), "es esz pm", "e16", c=0.09)
+        for m in range(M):
+            act(T.wg[:, m:GW:M], T.yg[:, m:GW:M], "yg e16", "wg%d" % m, -1.0, T.e16[:, m:m + 1])
+        ts(T.wr[:], T.wg[:], -192.0, Op.add, 0.0, Op.max, " ".join("wg%d" % m for m in range(M)), "wr", cy(GW // 2))
+        scan(T.rr[:], T.r12[:], T.wr[:], 0.0, Op.mult, Op.add, "r12 wr", "rr", cy(GW // 2))
         tt(e3, mv, kk, Op.subtract, "cw kk", "e3")
-        tt(e4, e3, T.rr[:, 15:C:16], Op.min, "e3 rr", "e4")
-        tt(e6, T.vw[:, 15:C:16], e4, Op.subtract, "vw e4", "e6")
+        tt(e4, e3, T.rr[:, M - 1:GW:M], Op.min, "e3 rr", "e4")
+        tt(e6, vw, e4, Op.subtract, "vw e4", "e6")
         cp(T.do[:], e6, "e6", "do")
-        cp(ow.indirect(T.do[:]), T.tm[:, 0:C], "do tm owz " + ok, ok, 0.05 + C * SCATTER * CYC)
-        places(False, t == R - 1)
-        cp(ow.indirect(T.lo[:, 0:6]), T.hid[:], "lo hid " + ok, ok, 0.05 + NT * SCATTER * CYC)
-        pick(T.oww[:], T.wp4[:], T.ow[:, OW * t + 1:OW * t + C + 1], "wp4 " + ok, "oww", cy(C))
+        if t == 0: cp(T.ow[:].indirect(T.do[:]), T.tm[:, 0:C], "do tm ow", "ow", sca(C))
+        else: cp(T.ow[:].indirect(T.do[:]), T.slw[:], "do slw ow", "ow", sca(C))
+        places(t == R - 1)
+        cp(T.ow[:].indirect(T.lo[:, 0:6]), T.tm[:, HID + NT * t:HID + NT * t + NT], "lo hid ow", "ow", sca(NT))
+        pick(T.oww[:], T.wp4[:], T.ow[:, 1:C + 1], "wp4 ow", "oww", cy(C))
         ts(T.xo[:], T.oww[:, 3:C:4], 4.0, Op.mult, c4, Op.add, "oww c4", "xo", cy(80))
         if t < R - 1:
-            labels(t + 1)
+            act(T.slw[:], T.ow[:].indirect(T.do[:]), "ow do", "slw", c=ga(C))
+            act(T.pib[:], e2, "e2", "pib", 1.0, 191.6)
+            act(ra, vw, "vw", "ra", 1.0, RND)
+            act(rd2, ra, "ra", "rd2", 2.0, -2 * RND)
+            act(rv, vw, "vw", "rv", 2.0)
+            tt(fr, rv, rd2, Op.subtract, "rv rd2", "fr")
+            tt(nk, fr, mv, Op.mult, "fr cw", "nk")
+            tt(kk, nk, e4, Op.subtract, "nk e4", "kk")
+            labels()
             tables()
-            grid()
         else:
-            act(T.mz[:], un, "un", "mz", -1.0, 1.5)
+            act(rev(T.mz, 0), T.tm[:].indirect(idx), tmk, "mz", c=ga(P))
             dma("y", T.oz[:], T.mz[0:128:16, :], "mz", "oz")
         add("v", lambda lis=lis, n=nl: V.wait_ge(lis, n), "r3", "lp%d" % t, 0.0, "w")
         for b in range(4):
-            tt(T.tb[:, b:4 * NT:4], T.dd[:, FL * b:FL * b + FL].indirect(lp[:, 0:6]), T.ta[:, b:4 * NT:4], Op.add,
-               "ta%d dd%d ddz%d lp%d" % (b, b, b, t), "tb%d" % b, ga(NT))
+            tt(T.tb[:, b:4 * NT:4], T.dd[:, DW * b:DW * b + C + 1].indirect(lp[:, 0:6]), T.ta[:, b:4 * NT:4], Op.add,
+               "ta%d dd%d ddz lp%d" % (b, b, t), "tb%d" % b, ga(NT))
         quant(T.qb[:], T.sb[:], T.tb[:], "tb0 tb1 tb2 tb3 tbz", "qb")
         for b in range(4):
             mm(b, 128, T.qw[:, 128 * b:128 * b + 128], T.sw[:, 128 * b:128 * b + 128], T.qb[:], T.sb[:], "qw sw qb")
+        h0 = 4 * (C + NT * t)
         for b in range(4):
-            tt(T.tmp[:, NT * b:NT * b + NT], T.ps[:, 512 * b:512 * b + NT], T.a64[:, b:4 * NT:4], Op.add, "a64 ps%d" % b, "tmp%d ps%d" % (b, b), cy(NT))
-            act(X[t][:, 4 * HB + b:XW:4], T.tmp[:, NT * b:NT * b + NT], "tmp%d" % b, "h%d%d" % (t, b), 0.015625, c=cy(NT))
-        hk = xk + " xo h%d0 h%d1 h%d2 h%d3" % (t, t, t, t)
+            tt(T.pool[:, h0 + b:h0 + 4 * NT:4], T.ps[:, 512 * b:512 * b + NT], T.a64[:, b:4 * NT:4], Op.add, "a64 ps%d" % b, "h%d%d ps%d" % (t, b, b), cy(NT))
+        pool += " h%d0 h%d1 h%d2 h%d3" % (t, t, t, t)
+        win, hk = T.pool[:, 0:h0 + 4 * NT], pool + " xo"
         a, b = XV // 4, HALF // 4
-        cp(X[t + 1][:, 0:4 * XV], X[t][:].indirect(T.xo[:, 0:a]), hk, "x%da" % (t + 1), ga(4 * XV))
-        if b > a: act(X[t + 1][:, 4 * XV:4 * HALF], X[t][:].indirect(T.xo[:, a:b]), hk, "x%db" % (t + 1), c=ga(4 * (HALF - XV)))
-        act(X[t + 1][:, 4 * HALF:4 * C], X[t][:].indirect(T.xo[:, b:80]), hk, "x%dc" % (t + 1), c=ga(4 * (C - HALF)))
+        ts(X[t + 1][:, 0:4 * XV], win.indirect(T.xo[:, 0:a]), 0.015625, Op.mult, None, None, hk, "x%da" % (t + 1), ga(4 * XV))
+        if b > a: act(X[t + 1][:, 4 * XV:4 * HALF], win.indirect(T.xo[:, a:b]), hk, "x%db" % (t + 1), 0.015625, c=ga(4 * (HALF - XV)))
+        act(X[t + 1][:, 4 * HALF:4 * C], win.indirect(T.xo[:, b:80]), hk, "x%dc" % (t + 1), 0.015625, c=ga(4 * (C - HALF)))
 
     pack(R, T.qv[:], T.sv[:], "qv", lambda a, n: T.yb[:, a:a + n], "yb")
     dma("y", T.oc[:, 0:4 * HALF], T.qx[:, 0:HALF].bitcast(dt.uint8), "qxa3", "oca")
@@ -543,5 +571,5 @@ def rank_program(g, core, T, topo):
         dma("ys"[k % 2], T.osc[4 * k:4 * k + 4, :], T.sx[32 * k:32 * k + 4, :], "qxa3 qxb3", "osc%d" % k)
     dma("y", T.y[:, 0:HALF], T.yb[:, 0:HALF], "yba", "ya")
     dma("s", T.y[:, HALF:C], T.yb[:, HALF:C], "ybb", "yb")
-    add("g", lambda: g.wait_ge(T.sem.sent, nsent[0]), "r0 r1 r2 r3", "", 0.0, "w")
+    add("g", lambda: g.wait_ge(T.sem.sent, nsent[0]), "r0 r1 r3", "", 0.0, "w")
     emit(ops, g, T)

@@ -8,7 +8,7 @@ PW = 4 * (C + R * NT)
 OFF, BIG = 1024.0, 1048576.0
 FL = 1024
 DW = 336
-GS = 724.0
+GS = 200.0
 KEY = 4097.0
 LAP = KEY * P
 NONE = C + 1 - 512.0
@@ -18,13 +18,14 @@ RND = 12582912.0
 OW = 424
 M, GW = 12, 240
 HALF = 160
-XV = 144
+GT = 144
+RJ, R512 = 192, 6442450944.0
 CYC, GATHER, SCATTER, CALL = 0.00104, 1.56, 3.8, 0.5
-CASES = [(0.15, 2.0, 3.0, 4.5, 0.5, 1.0), (0.1, 1.6, 2.2, 3.8, 0.3, 1.1), (0.2, 2.2, 3.8, 5.5, 0.7, 0.9)]
-TRIES = 120000
+CASES = [(0.2, 1.6, 2.2, 3.6, 0.3, 0.8), (0.2, 1.8, 2.8, 4.4, 0.4, 1.1), (0.14, 1.6, 2.2, 3.6, 0.3, 1.0)]
+TRIES = 200000
 LANES = {"v": 32, "s": 32, "p": 8, "g": 8}
-N20 = "e1 e2 e3 e4 e6 pit kk zz l48 k2 dq ra rd rv fr nk".split()
-N48 = "qd hh lt gg aa ab2 ea n32 c16s vq".split()
+N20 = "e3 e6 ra".split()
+N48 = "qd hh lt gg aa ab2 ea n32 vq emp mask0 gd".split()
 
 F, B16, I32, U16, Q4, U8 = "float32", "bfloat16", "int32", "uint16", "float8_e4m3fn_x4", "uint8"
 
@@ -43,18 +44,19 @@ SCRATCH = {
     "ta": _s(4 * NT, B16), "tb": _s(512, B16), "a64": _s(4 * NT),
     "ps": ("psum", [128, 4096], F), "n20": _s(24 * len(N20)), "n48": _s(P * len(N48)),
     "tm": _s(FL + DW), "ip": _s(8, I32), "col": _s(24), "j20": _s(20), "jw": _s(20),
-    "jm": _s(C, B16), "wpa": _s(C, B16), "wp4": _s(C, B16), "j4": _s(C, B16), "rst": _s(P, B16), "r12": _s(GW, B16),
+    "jm": _s(C, B16), "wpa": _s(C, B16), "wp4": _s(C, B16), "j4": _s(C, B16), "r12": _s(GW, B16),
     "base": _s(8), "t1": _s(192), "th": _s(192),
     "dum": _s(8), "upk": _s(8, U16), "qc": _s(4),
     "sw_": _s(376), "mk": _s(P), "rm": _s(P), "pc": _s(8), "pm": _s(8, U16),
-    "ga": _s(P, B16), "gs": _s(P), "idx": _s(4, U16), "tu": _s(104), "ub2": _s(56), "pww": _s(NT),
-    "gt": _s(NT), "rj": _s(192), "own": _s(8), "ei": _s(8, I32), "ek": _s(8, I32),
-    "en6": _s(8), "f6": _s(8), "l6": _s(8), "l9": _s(8), "lo": _s(8, U16), "ls": _s(4, U16),
-    "crp": _s(R * 64 + 16, B16), "cg": _s(C, B16), "cw": _s(C, B16), "val": _s(C), "vw": _s(C),
+    "ga": _s(P, B16), "idx": _s(4, U16), "tu": _s(104), "ub2": _s(56), "pww": _s(NT),
+    "gt": _s(GT), "rj": _s(RJ + 10 * GT), "rs2": _s(GT, B16), "dec": _s(32),
+    "pa": _s(12), "pb": _s(12), "l9": _s(12), "lo": _s(8, U16), "lf": _s(4, U16),
+    "ea0": _s(60), "ee": _s(60), "la": _s(80), "lb1": _s(80), "lab": _s(80),
+    "crp": _s(R * 64 + 16, B16), "cg": _s(C, B16), "cw": _s(3 * C, B16), "val": _s(C), "vw": _s(C),
     "d1": _s(GW, B16), "v1": _s(GW, B16), "ab": _s(GW, B16), "inc": _s(GW), "yg": _s(GW), "e16": _s(16),
     "wg": _s(GW, B16), "wr": _s(GW, B16), "rr": _s(GW, B16),
     "vo": _s(20, U16), "do": _s(20, U16), "ow": _s(OW), "slw": _s(C), "ao": _s(24, U16), "oww": _s(C), "xo": _s(80, U16),
-    "mw": _s(376), "mr": _s(C), "mww": _s(C), "pib": _s(20, B16), "lb": _s(20, B16), "po": _s(20, U16),
+    "mw": _s(376), "mr": _s(C), "mww": _s(C), "pib": _s(20, B16), "po": _s(20, U16),
     "es": _s(64), "sc": _s(4), "mz": _s(P), "yb": _s(C),
 }
 for _t in range(R):
@@ -135,7 +137,7 @@ def arrange(ops, deps):
     best, kept = now, order
     pos = {c: i for i, c in enumerate(order)}
     for step in range(TRIES):
-        end, start, held, fin = runs[step % len(CASES)]
+        end, start, held, fin = runs[step // 3 % len(CASES)]
         if step % 3:
             c, path = fin.index(end), []
             while c >= 0:
@@ -295,24 +297,26 @@ def rank_program(g, core, T, topo):
 
     X = [T.x0, T.x1, T.x2, T.x3]
     col = T.col
-    ci, cr, ct, c16, c4, csp, c36, cd, c161, c16m, cz, c4a, cq, cs, cf0, cf1, cl, ck = (col[:, k:k + 1] for k in range(18))
-    e1, e2, e3, e4, e6, pit, kk, zz, l48, k2, dq, ra, rd2, rv, fr, nk = (T.n20[:, 24 * k:24 * k + 20] for k in range(len(N20)))
-    qd, hh, lt, gg, aa, ab2, ea, n32, c16s, vq = (T.n48[:, P * k:P * k + P] for k in range(len(N48)))
+    ci, cm, cr, ct, c16, c4, csp, c36, cd, c161, c16m, cz, c4a, cq, cs, cf0, cf1, cl, ck = (col[:, k:k + 1] for k in range(19))
+    e3, e6, ra = (T.n20[:, 24 * k:24 * k + 20] for k in range(len(N20)))
+    qd, hh, lt, gg, aa, ab2, ea, n32, vq, emp, mask0, gd = (T.n48[:, P * k:P * k + P] for k in range(len(N48)))
+    mv, lap, k2, pit, e2 = T.cw[:, 45:3 * C:48], T.cw[:, 29:3 * C:48], T.ea0[:, 1:60:3], T.ea0[:, 2:60:3], T.ee[:, 2:60:3]
+    e4, kk, zz = T.lb1[:, 2:80:4], T.lab[:, 2:80:4], T.lab[:, 3:80:4]
     at = {k: P * i for i, k in enumerate(N48)}
     HID, T1S, RS2, T1A = DW, DW + R * NT, DW + R * NT + 80, FL - 32
-    mask, zg, hs, j48 = (T.tm[:, RS2 + NT + P * k:RS2 + NT + P * k + P] for k in range(4))
-    tmk = "tm tm2 hid t1s0 t1s1 t1s2 rs2 mask zg hs j48 t1a t1b idx"
+    c16s, zero, mask, zg, hs, j48 = (T.tm[:, RS2 + P * k:RS2 + P * k + P] for k in range(6))
+    tmk = "tm tm2 hid t1s0 t1s1 t1s2 c16s zero mask zg hs j48 t1a t1b idx"
 
     dma("y", T.szb[:, 0:3], T.sz[:], "", "szb")
     dma("s", T.ub[:], T.u[:], "", "ub")
-    dma("y", T.x0[:, 0:4 * HALF], T.x[:, 0:4 * HALF], "", "x0a x0b")
+    dma("y", T.x0[:, 0:4 * HALF], T.x[:, 0:4 * HALF], "", "x0a")
     dma("s", T.x0[:, 4 * HALF:4 * C], T.x[:, 4 * HALF:4 * C], "", "x0c")
     dma("y", T.qw[:].bitcast(dt.uint8), T.wc[:], "", "qw")
     dma("y", T.sw[:], T.ws[:], "", "sw")
     dma("y", T.vb[:], T.v[:], "", "vb")
 
     fill(T.ones[:], 1.0, "ones", cy(264))
-    iota(T.ip[:, 0:1], [[0, 1]], 0, 1, "ip", False)
+    iota(T.ip[:, 0:2], [[15, 2]], 0, 1, "ip", False)
     iota(T.tm[:, 0:DW], [[1, DW]], 0, 0, "tm")
     iota(j48, [[16, 3], [0, 16]], 0, 0, "j48")
     iota(T.j20[:], [[16, 20]], 0, 0, "j20")
@@ -333,36 +337,46 @@ def rank_program(g, core, T, topo):
     fill(T.ub2[:, 0:1], 0.0, "ubz")
     fill(T.sw_[:, C + 1:376], -1e29, "swz")
     fill(T.sw_[:, 0:1], -1e29, "swy")
-    fill(T.rst[:], 1.0, "rst")
-    fill(T.rst[:, 0:P:16], 0.0, "rst")
-    fill(T.tm[:, RS2:RS2 + NT], 0.0, "rs2", cy(NT))
-    fill(T.tm[:, RS2:RS2 + NT:32], -4 * BIG, "rs2")
+    fill(T.rs2[:], 0.0, "rs2", cy(GT // 2))
+    fill(T.rs2[:, 0:GT:P], -4 * BIG, "rs2")
     fill(T.es[:, P:64], 192.49, "esz")
+    fill(zero, 0.0, "zero")
     fill(c16s, 16.0, "c16s")
+    fill(T.cw[:, 13:3 * C:48], 0.0, "cw")
+    fill(T.ea0[:, 0:60:3], -48.0 / MV, "ea0")
+    fill(T.la[:], 1.0, "la", cy(80))
+    fill(T.la[:, 0:80:4], 0.0, "la")
+    fill(T.pa[:, 0:12:2], BIG, "pa")
+    for k, (a, v) in enumerate(((5 - P, 0.0), (5 + P, 1.0), (5 + 2 * P, 1.0), (5 + 3 * P, -1.0),
+                                (-4 * P, 1.0), (-3 * P, -161.0), (-2 * P, R512), (-P, -R512))):
+        sfill(T.rj[:, RJ + a:RJ + a + 25 * P + 1:5 * P], v, "rk%d" % k, 6)
+    fill(gd, BIG, "gd")
+    for k, v in enumerate((192.0, 192.0 + 900, 191.0, BIG)): fill(T.t1[:, P + k:192:64], v, "t1")
     fill(T.d1[:], -1.0, "d1", cy(GW // 2))
     fill(T.tm[:, T1S:T1S + 32], 0.0, "t1s0")
     fill(T.tm[:, T1S + P:T1S + 80], -1.0, "t1s2")
     for t in range(R): sfill(X[t][:, 4 * C:4 * HB], 0.0, "x%dz" % t, 16)
     sfill(T.dd[:, C:4 * DW:DW], 0.0, "ddz", 4)
-    sfill(T.mw[:], 0.0, "mw", 376)
+    sfill(T.mw[:], 1000.0, "mw", 376)
     sfill(T.tb[:, 4 * NT:512], 0.0, "tbz", 128)
     act(T.tm[:, FL:FL + DW], T.tm[:, 0:DW], "tm", "tm2", c=cy(DW))
     for k in range(4):
-        act(T.pool[:, C * k:C * k + C], T.x0[:, C * k:C * k + C], "x0a x0b x0c", "p%d" % k, 64.0, c=cy(C))
-    ts(T.ip[:, 1:2], T.ip[:, 0:1], 15, Op.bitwise_and, None, None, "ip", "ip1")
-    ts(T.ip[:, 2:3], T.ip[:, 0:1], 2, Op.arith_shift_right, 3, Op.bitwise_and, "ip", "ip2")
-    ts(T.ip[:, 3:4], T.ip[:, 0:1], 3, Op.bitwise_and, None, None, "ip", "ip3")
-    cp(ci, T.ip[:, 1:2], "ip1", "ci")
-    cp(col[:, 1:3], T.ip[:, 2:4], "ip2 ip3", "cr")
+        act(T.pool[:, C * k:C * k + C], T.x0[:, C * k:C * k + C], "x0a" if k < 2 else "x0c", "p%d" % k, 64.0, c=cy(C))
+    ts(T.ip[:, 2:4], T.ip[:, 0:2], 15, Op.bitwise_and, None, None, "ip", "ip1")
+    ts(T.ip[:, 4:5], T.ip[:, 0:1], 2, Op.arith_shift_right, 3, Op.bitwise_and, "ip", "ip2")
+    ts(T.ip[:, 5:6], T.ip[:, 0:1], 3, Op.bitwise_and, None, None, "ip", "ip3")
+    cp(col[:, 0:2], T.ip[:, 2:4], "ip1", "ci")
+    cp(col[:, 2:4], T.ip[:, 4:6], "ip2 ip3", "cr")
     for k, nm, a, b in ((c16, "c16", -OFF, 15 * OFF), (c161, "c161", -OFF, 15 * OFF + 1), (c16m, "c16m", -OFF, 15 * OFF - 1),
                         (cs, "cs", OFF, FL - 1 - 15 * OFF), (cf0, "cf0", 4096 * OFF, 2048 - 4096 * 15 * OFF),
-                        (cf1, "cf1", 4096 * OFF, 6144 - 4096 * 15 * OFF), (c36, "c36", 1.0, 36.0), (cd, "cd", 1.0, C + 1.0),
+                        (cf1, "cf1", 4096 * OFF, 6144 - 4096 * 15 * OFF), (cd, "cd", 1.0, C + 1.0),
                         (cz, "cz", sg / 48, 47.0 * flip / 48), (cq, "cq", sg, 15.0 * flip),
                         (cl, "cl", -OFF / 16, 15 * OFF / 16 + 192 - 0.31), (ck, "ck", 32 * OFF, -32 * 15 * OFF)):
         act(k, ci, "ci", nm, a, b)
     act(c4a, cr, "cr", "c4a", -4 * OFF, 12 * OFF)
     act(c4, ct, "cr c4a", "c4", 1.0, c4a)
-    ts(csp, ci, 12.0, Op.is_ge, c36, Op.mult, "ci c36", "csp")
+    act(c36, cm, "ci", "c36", 1.0, 36.0)
+    ts(csp, cm, 12.0, Op.is_ge, c36, Op.mult, "ci c36", "csp")
     ts(T.jm[:, 0:NT], T.jm[:, 0:NT], ci, Op.is_equal, BIG, Op.mult, "jm ci", "jm")
     ts(T.wpa[:, 0:NT], T.jm[:, 0:NT], -OFF, Op.add, None, None, "jm", "wpa")
     act(T.wpa[:, NT:2 * NT], T.wpa[:, 0:NT], "wpa", "wpb", c=cy(NT))
@@ -376,14 +390,14 @@ def rank_program(g, core, T, topo):
     act(T.crp[:, 0:R * 64], T.ones[:, 0:R * 64], "ones c16", "crp0 crp1 crp2", 0.0, c16, cy(R * 64))
     act(T.crp[:, R * 64:R * 64 + 16], T.crp[:, 0:16], "crp0", "crs", 1.0, MV)
     act(T.base[:], T.base[:], "base0 base1 csp", "base0 base1", 1.0, csp)
-    act(T.dum[:, 0:6], T.j20[:, 0:6], "j20 cd", "dum", 1.0, cd)
+    act(T.pb[:, 1:12:2], T.j20[:, 0:6], "j20 cd", "dum", 1.0, cd)
     act(T.jw[:], T.j20[:], "j20 ci", "jw", 1.0, ci)
     act(T.qc[:, 0:3], T.jw[:, 0:3], "jw", "qc", sg * KEY, 2049 + 47 * KEY * flip)
     act(zg, j48, "j48 cz", "zg", sg / 48, cz)
     quant(T.qu0[:], T.su0[:], T.ub[:], "ub", "qu0")
     add("s", lambda: S.activation(T.su[:], T.su0[:].indirect(T.upk[:]), Act.Copy), "qu0 upk", "su", ga(128))
     cp(T.qu[:].bitcast(dt.uint32), T.qu0[:].bitcast(dt.uint32).indirect(T.upk[:]), "qu0 upk", "qu", ga(128))
-    ts(mask, qd, ci, Op.is_equal, 3e29, Op.mult, "qd ci", "mask")
+    ts(mask, qd, cm, Op.is_equal, 3e29, Op.mult, "qd ci", "mask")
     act(mask, mask, "mask", "mask", 1.0, -2e29)
     for b in range(4):
         quant(T.qe[:, 128 * b:128 * b + 128], T.se[:, 128 * b:128 * b + 128], T.eye[:, 3 - b:515 - b], "eye", "qe%d" % b)
@@ -396,81 +410,84 @@ def rank_program(g, core, T, topo):
     endp, sizp = T.pww[:, pe:pe + 33:16], T.pww[:, pn:pn + 33:16]
 
     def sizes(first):
-        win, wk = (T.tm[:, 0:DW], "tm idx") if first else (T.tm[:], tmk)
-        act(rev(T.tu, P + 1, not first), win.indirect(idx), wk, "un", 1.0 + EPS, c=ga(P))
-        act(rev(T.ub2, 1, not first), win.indirect(idx), wk, "ub2", -EPS, c=ga(P))
+        if first:
+            act(un, T.tm[:, 0:DW].indirect(idx), "tm idx", "un", c=ga(P))
+            scan(T.tu[:, 1:P + 1], un, zero, 0.0, Op.add, Op.add, "un zero", "en")
+            return
+        act(rev(T.tu, P + 1), T.tm[:].indirect(idx), tmk, "un", 1.0 + EPS, c=ga(P))
+        act(rev(T.ub2, 1), T.tm[:].indirect(idx), tmk, "ub2", -EPS, c=ga(P))
         scan(T.tu[:, 1:P + 1], un, T.ub2[:, 0:P], 0.0, Op.add, Op.add, "un ub2 ubz", "en")
 
-    def places(last):
+    def places():
         pick(T.pww[:], T.wpa[:, 0:NT], rev(T.tu, 1, n=NT), "wpa en un", "pww", cy(NT))
-        act(T.en6[:, 0:3], endp, "pww c16", "en6a", 1.0, c16)
-        act(T.en6[:, 3:6], endp, "pww c16m", "en6b", 1.0, c16m)
-        act(T.f6[:, 0:3], sizp, "pww cf0", "f6a", -4096.0, cf0, f=Act.Relu)
-        act(T.f6[:, 3:6], sizp, "pww cf1", "f6b", -4096.0, cf1, f=Act.Relu)
-        tt(T.l6[:, 0:6], T.en6[:, 0:6], T.f6[:, 0:6], Op.add, "en6a en6b f6a f6b", "l6")
-        tt(T.l9[:, 0:6], T.l6[:, 0:6], T.dum[:, 0:6], Op.min, "l6 dum", "l9")
-        cp(T.lo[:, 0:6], T.l9[:, 0:6], "l9", "lo")
+        act(T.pb[:, 0:6:2], endp, "pww c16", "en6a", 1.0, c16)
+        act(T.pb[:, 6:12:2], endp, "pww c16m", "en6b", 1.0, c16m)
+        act(T.pa[:, 1:6:2], sizp, "pww cf0", "f6a", -4096.0, cf0, f=Act.Relu)
+        act(T.pa[:, 7:12:2], sizp, "pww cf1", "f6b", -4096.0, cf1, f=Act.Relu)
+        scan(T.l9[:], T.pa[:], T.pb[:], 0.0, Op.add, Op.min, "en6a en6b f6a f6b pa dum", "l9")
+        cp(T.lo[:, 0:6], T.l9[:, 1:12:2], "l9", "lo")
 
     def tables():
         tt(ea, T.tm[:, 0:P], un, Op.add, "tm un", "ea", cy(96))
         act(T.es[:, 0:P], ea, "ea", "es", 1.0 / 48, 191.5 + 0.3 / 48)
         act(T.sc[:, 0:3], sizp, "pww cs", "sc", -1.0, cs)
-        act(T.t1[:, P:192:64], T.sc[:, 0:3], "sc t1", "t1n", -11.0, 3060 - (FL - 1) + GS)
+        act(T.n48[:, at["gd"]:at["gd"] + P:16], T.sc[:, 0:3], "sc gd", "t1n", -11.0, 2292 - (FL - 1) - GS)
         tt(hh, T.tu[:, 0:P], hs, Op.subtract, "en enz hs", "hh", cy(96))
         for c in range(3):
             a = T1S + (16 * c if flip else 32 - 16 * c)
             act(T.t1[:, 64 * c:64 * c + P], T.tm[:, a:a + P], "sc t1s0 t1s1 t1s2 t1", "t1%d" % c, -1.0, T.sc[:, c:c + 1], f=Act.Relu)
             act(T.th[:, 64 * c:64 * c + P], hh, "hh qc th", "th%d" % c, 1.0, T.qc[:, c:c + 1])
-        tt(T.own[:, 0:6], T.en6[:, 0:6], T.f6[:, 0:6], Op.subtract, "en6a en6b f6a f6b", "own")
+        tt(T.n48[:, at["gd"] + 14:at["gd"] + P:16], T.pb[:, 0:6:2], T.pa[:, 1:6:2], Op.subtract, "en6a f6a gd", "own0")
+        tt(T.n48[:, at["gd"] + 15:at["gd"] + P:16], T.pb[:, 6:12:2], T.pa[:, 7:12:2], Op.subtract, "en6b f6b gd", "own1")
 
     def first_labels():
         act(n32, T.tm[:, 0:DW].indirect(idx), "tm idx", "n32", 1.0 / 32, c=ga(P))
         fill(vq[:, 0:1], 0.0, "vq0")
         scan(vq[:, 1:P], n32[:, 0:P - 1], c16s[:, 1:P], 0.0, Op.add, Op.add, "n32 c16s", "vq")
-        tt(e1[:, 0:3], T.l6[:, 0:3], sizp, Op.subtract, "l6 pww", "e1")
-        ts(e2[:, 0:3], e1[:, 0:3], c16, Op.subtract, 0.4, Op.add, "e1 c16", "e2")
-        tt(e3[:, 0:3], e2[:, 0:3], T.dum[:, 0:3], Op.min, "e2 dum", "e3")
-        cp(T.ls[:, 0:3], e3[:, 0:3], "e3", "ls")
-        cp(T.mw[:].indirect(T.ls[:, 0:3]), rev(T.n48, at["vq"]), "vq vq0 ls mw", "mw", sca(P))
-        scan(T.mr[:], T.mw[:, 0:C], T.mw[:, 0:C], 0.0, Op.max, Op.max, "mw", "mr", cy(C))
+        ts(T.lf[:, 0:3], endp, c16, Op.add, None, None, "pww c16", "lf")
+        act(emp, rev(T.tu, P + 1), "un", "emp", 2e29, -1e29)
+        tt(mask0, mask, emp, Op.min, "mask emp", "mask0", cy(96))
+        cp(T.mw[:].indirect(T.lo[:, 0:3]), rev(T.n48, at["vq"]), "vq vq0 lo mw", "mw", sca(P))
+        scan(T.mr[:, C - 1::-1], T.mw[:, C:0:-1], T.mw[:, C:0:-1], 1000.0, Op.min, Op.min, "mw", "mr", cy(C))
         pick(T.mww[:], T.wpa[:], T.mr[:], "wpa wpb wpc mr", "mww", cy(C))
         act(T.pib[:], T.mww[:, 15:C:16], "mww cl", "pib", 1.0 / 16, cl)
-        act(ra, T.mww[:, 15:C:16], "mww ck", "ra", -32.0, ck)
-        act(rv, T.pib[:], "pib", "rv", 512.0, -512.0 * 192)
-        tt(fr, T.jw[:], ra, Op.add, "jw ra", "fr")
-        tt(kk, fr, rv, Op.add, "fr rv", "kk")
+        act(T.lb1[:, 0:80:4], T.jw[:], "jw", "l0")
+        act(T.lb1[:, 1:80:4], T.mww[:, 15:C:16], "mww ck", "l1", -32.0, ck)
+        act(e4, T.pib[:], "pib", "e4", 512.0, -512.0 * 192)
 
-    def labels():
+    def labels(first):
+        act(T.lb1[:, 3:80:4], T.pib[:], "pib", "l3", 1.0, -192.0)
+        scan(T.lab[:], T.la[:], T.lb1[:], 0.0, Op.mult, Op.add, "la l0 l1 l2 l3 e4", "kk zz", cy(80))
         act(pit, T.pib[:], "pib", "pit", 1.0, -192.0)
         act(T.d1[:, 0:GW:M], T.pib[:], "pib d1", "d1", 0.25, 144 - 0.375)
-        cp(T.po[:], pit, "pit", "po")
-        tt(zz, kk, pit, Op.add, "kk pit", "zz")
-        act(T.lb[:], zz, "zz", "lb", 1.0 / 48, 191.5 + 1.5 / 48)
-        act(l48, T.lb[:], "lb", "l48", 48.0 / MV, -(192 * 48.0 + 1.75) / MV)
-        act(k2, kk, "kk", "k2", 1.0 / MV)
-        tt(dq, k2, l48, Op.subtract, "k2 l48", "dq")
+        ts(T.po[:], T.pib[:], -192.0, Op.add, None, None, "pib", "po")
+        act(lap, zz, "zz cw", "cw", 1.0 / 48, 191.5 + 1.5 / 48)
+        act(k2, kk, "kk", "k2", 1.0 / MV, (192 * 48.0 + 1.75) / MV)
         scan(T.v1[:], T.r12[:], T.d1[:], 0.0, Op.mult, Op.add, "r12 d1", "v1", cy(GW // 2))
-        act(T.ab[:], T.v1[:], "v1", "ab", 1.0, -191.0, cy(GW), Act.Abs)
-        act(T.inc[:], T.ab[:], "ab", "inc", -1.0, 1.0, cy(GW), Act.Relu)
+        if first: ts(T.inc[:], T.v1[:], 191.0, Op.is_equal, None, None, "v1", "inc", cy(GW))
+        else:
+            act(T.ab[:], T.v1[:], "v1", "ab", 1.0, -191.0, cy(GW), Act.Abs)
+            act(T.inc[:], T.ab[:], "ab", "inc", -1.0, 1.0, cy(GW), Act.Relu)
         act(T.inc[:, 0:GW:M], zz, "zz inc", "inc", 1.0 / 48, 1.0 / 48 - 1)
         scan(T.yg[:], T.r12[:], T.inc[:], 0.0, Op.mult, Op.add, "r12 inc", "yg", cy(GW))
 
     def pack(t, wq, ws, wk, out, ok):
         qx, sx = (T["qx%d" % t], T["sx%d" % t]) if t < R else (T.qx, T.sx)
-        for h, a, n, rd in ((0, 0, HALF, "x%da x%db" % (t, t)), (1, HALF, C - HALF, "x%dc" % t)):
+        for h, a, n, rd in ((0, 0, HALF, "x%da" % t), (1, HALF, C - HALF, "x%dc" % t)):
             nm = "ab"[h]
             quant(qx[:, a:a + n], sx[:, a:a + n], X[t][:, 4 * a:4 * a + 4 * n], rd, "qx%s%d" % (nm, t), n)
             mm(h, n, wq, ws, qx[:, a:a + n], sx[:, a:a + n], wk + " qx%s%d" % (nm, t))
-            act(out(a, n), T.ps[:, 512 * h:512 * h + n], "ps%d" % h, ok + nm + " ps%d" % h, c=cy(n))
+            if h: cp(out(a, n), T.ps[:, 512 * h:512 * h + n], "ps%d" % h, ok + nm + " ps%d" % h, cy(n))
+            else: act(out(a, n), T.ps[:, 512 * h:512 * h + n], "ps%d" % h, ok + nm + " ps%d" % h, c=cy(n))
 
     sizes(True)
-    places(False)
+    places()
     tables()
     first_labels()
-    labels()
+    labels(True)
     pool = "p0 p1 p2 p3"
     for t in range(R):
-        xk = "x%da x%db x%dc x%dz" % (t, t, t, t)
+        xk = "x%da x%dc x%dz" % (t, t, t)
         pack(t, T.qu[:], T.su[:], "qu su", lambda a, n: T.sw_[:, 1 + a:1 + a + n], "sw")
         qx, sx, ql, sl, arr = T["qx%d" % t], T["sx%d" % t], T["ql%d" % t], T["sl%d" % t], T.sem["arr%d" % t]
         na = send(ql[:].bitcast(dt.uint8), qx[:].bitcast(dt.uint8), arr, t, "qxa%d qxb%d" % (t, t), "r0", "R")
@@ -479,7 +496,8 @@ def rank_program(g, core, T, topo):
         for b in range(4):
             mm(4 + b, C, T.qe[:, 128 * b:128 * b + 128], T.se[:, 128 * b:128 * b + 128], ql[:], sl[:], "qe%d ql%d" % (b, t))
             act(T.dd[:, DW * b:DW * b + C], T.ps[:, 512 * (4 + b):512 * (4 + b) + C], "ps%d" % (4 + b), "dd%d ps%d" % (b, 4 + b), c=cy(C))
-        tt(T.mk[:], T.sw_[:].indirect(T.lo[:, 0:3]), mask, Op.min, "swa swb swz swy lo mask", "mk", ga(P))
+        if t: tt(T.mk[:], T.sw_[:].indirect(T.lo[:, 0:3]), mask, Op.min, "swa swb swz swy lo mask", "mk", ga(P))
+        else: tt(T.mk[:], T.sw_[:].indirect(T.lf[:, 0:3]), mask0, Op.min, "swa swb swz swy lf mask0", "mk", ga(P))
         scan(T.rm[:], rev(T.mk, 0), rev(T.mk, 0), -3e29, Op.max, Op.max, "mk", "rm")
         add("s", lambda: S.activation(lt, T.rm[:], Act.Sign, bias=T.rm[:, P - 1:P], scale=-1.0, accum_out=T.pc[:, 0:1]), "rm", "lt pc", 0.09)
         ts(T.pm[:], T.base[:], T.pc[:, 0:1], Op.add, None, None, "pc base0", "pm")
@@ -487,62 +505,57 @@ def rank_program(g, core, T, topo):
         cp(crp.indirect(T.pm[:, 0:1]), T.crp[:, R * 64:R * 64 + 16], "pm crs crp%d" % t, "crp%d" % t, sca(16))
         pm3, pm64 = T.pm[:, 0:3], T.pm[:, 4:7]
         tt(T.ga[:], T.es[:].indirect(pm3), zg, Op.subtract, "es esz pm zg", "ga", ga(P))
-        tt(gg, T.t1[:].indirect(pm64), T.ga[:], Op.subtract, "t1 t1n t10 t11 t12 pm ga", "gg", ga(P))
-        scan(T.gs[:], T.rst[:], gg, 0.0, Op.mult, Op.add, "rst gg", "gs")
-        ts(idx, T.gs[:, 15:P:16], -1.0, Op.mult, GS + 0.1, Op.add, "gs", "idx")
+        tt(gg, T.t1[:].indirect(pm64), T.ga[:], Op.subtract, "t1 t10 t11 t12 pm ga", "gg", ga(P))
+        scan(T.gt[:, 0:GT:3], gg, gd, 0.0, Op.add, Op.min, "gg gd t1n own0 own1", "gs")
+        ts(idx, T.gt[:, 39:GT:P], -1.0, Op.mult, 0.1 - GS, Op.add, "gs", "idx")
         ts(aa, T.ga[:], -192.0, Op.add, LAP, Op.mult, "ga", "aa")
         act(ab2, T.ga[:], "ga", "ab2", LAP, -193 * LAP)
-        tt(T.gt[:, 1:NT:2], T.th[:].indirect(pm64), aa, Op.add, "th th0 th1 th2 pm aa", "g1 g3 g4", ga(P))
-        tt(T.gt[:, 0:NT:2], T.th[:].indirect(pm64), ab2, Op.add, "th th0 th1 th2 pm ab2", "g2", ga(P))
-        tt(T.gt[:, 25:NT:32], T.own[:, 0:3], T.gs[:, 15:P:16], Op.min, "gs own", "g3")
-        tt(T.gt[:, 27:NT:32], T.own[:, 3:6], T.gs[:, 15:P:16], Op.min, "gs own", "g4")
-        scan(T.rj[:, NT - 1::-1], T.tm[:, RS2:RS2 + NT], T.gt[:, NT - 1::-1], 0.0, Op.add, Op.max, "rs2 g1 g2 g3 g4", "rj0", cy(NT))
-        scan(T.rj[:, 2 * NT - 2:NT - 1:-1], T.gt[:, NT - 2::-1], T.rj[:, NT - 1:0:-1], NONE, Op.max, Op.min, "rj0 g1 g2 g3 g4", "rj1", cy(NT))
-        cp(T.ei[:, 0:6], T.rj[:, 0:2 * NT:32], "rj0 rj1", "ei")
-        ts(T.ek[:, 0:6], T.ei[:, 0:6], 511, Op.bitwise_and, None, None, "ei", "ek")
+        tt(T.gt[:, 1:GT:3], T.th[:].indirect(pm64), aa, Op.add, "th th0 th1 th2 pm aa", "g1", ga(P))
+        tt(T.gt[:, 2:GT:3], T.th[:].indirect(pm64), ab2, Op.add, "th th0 th1 th2 pm ab2", "g2", ga(P))
+        a, b = RJ + 5 * (GT - 1), RJ + 5 * GT
+        scan(T.rj[:, a:RJ - 1:-5], T.rs2[:], T.gt[:, GT - 1::-1], 0.0, Op.add, Op.max, "rs2 g1 g2 gs", "rj0", cy(GT))
+        scan(T.rj[:, b + 5 * (GT - 2):b - 1:-5], T.gt[:, GT - 2::-1], T.rj[:, a:RJ + 4:-5], NONE, Op.max, Op.min, "rj0 g1 g2 gs", "rj1", cy(GT))
+        scan(T.dec[:, 0:30], T.rj[:, RJ + 5 - P:RJ + 6 + 28 * P:P], T.rj[:, RJ - 4 * P:RJ + 1 + 25 * P:P], 0.0, Op.mult, Op.add,
+             "rj0 rj1 rk0 rk1 rk2 rk3 rk4 rk5 rk6 rk7", "dec")
         lm, lp, lis = T["lm%d" % t], T["lp%d" % t], T.sem["lis%d" % t]
-        ts(lm[:, 0:6], T.ek[:, 0:6], -1.0, Op.add, None, None, "ek", "lm%d" % t)
+        ts(lm[:, 0:6], T.dec[:, 4:30:5], -0.9, Op.add, None, None, "dec", "lm%d" % t)
         nl = send(lp[:, 0:6], lm[:, 0:6], lis, t, "lm%d" % t, "r3", "r")
         win = X[t][:, 0:4 * HB]
         for b in range(4):
-            ts(T.ao[:, 6 * b:6 * b + 6], T.ek[:, 0:6], 4.0, Op.mult, b - 4.0, Op.add, "ek", "ao%d" % b)
+            ts(T.ao[:, 6 * b:6 * b + 6], lm[:, 0:6], 4.0, Op.mult, float(b), Op.add, "lm%d" % t, "ao%d" % b)
             act(T.ta[:, b:4 * NT:4], win.indirect(T.ao[:, 6 * b:6 * b + 6]), "ao%d %s" % (b, xk), "ta%d" % b, c=ga(NT))
         act(T.a64[:], T.ta[:], "ta0 ta1 ta2 ta3", "a64", 64.0, c=cy(384))
         sizes(False)
         act(T.cg[:], crp.indirect(T.po[:]), "crp%d po" % t, "cg", c=ga(C))
-        pick(T.cw[:], T.wpa[:], T.cg[:], "wpa wpb wpc cg", "cw", cy(C // 2))
-        mv = T.cw[:, 15:C:16]
-        tt(e1, mv, dq, Op.mult, "cw dq", "e1")
-        tt(e2, e1, pit, Op.add, "e1 pit", "e2")
-        ts(T.vo[:], e2, 0.25, Op.add, None, None, "e2", "vo")
+        pick(T.cw[:, 0:3 * C:3], T.wpa[:], T.cg[:], "wpa wpb wpc cg cw", "cw", cy(C // 2))
+        scan(T.ee[:], T.cw[:, 13:3 * C:16], T.ea0[:], 0.0, Op.mult, Op.add, "cw k2 pit ea0", "ee")
+        ts(T.vo[:], e2, 0.25, Op.add, None, None, "ee", "vo")
         act(T.val[:], T.tu[:, 0:P + 1].indirect(T.vo[:]), "en enz vo c161", "val", 1.0, c161, ga(C))
         pick(T.vw[:], T.wpa[:], T.val[:], "wpa wpb wpc val", "vw", cy(C))
         vw = T.vw[:, 15:C:16]
         act(T.e16[:], T.es[:].indirect(T.pm[:, 0:1]), "es esz pm", "e16", c=0.09)
         for m in range(M):
-            act(T.wg[:, m:GW:M], T.yg[:, m:GW:M], "yg e16", "wg%d" % m, -1.0, T.e16[:, m:m + 1])
+            act(T.wg[:, m:GW:M], T.yg[:, m:GW:M], "yg e16", "wg%d" % m, -1.0, T.e16[:, m + 1:m + 2])
         ts(T.wr[:], T.wg[:], -192.0, Op.add, 0.0, Op.max, " ".join("wg%d" % m for m in range(M)), "wr", cy(GW // 2))
-        scan(T.rr[:], T.r12[:], T.wr[:], 0.0, Op.mult, Op.add, "r12 wr", "rr", cy(GW // 2))
-        tt(e3, mv, kk, Op.subtract, "cw kk", "e3")
-        tt(e4, e3, T.rr[:, M - 1:GW:M], Op.min, "e3 rr", "e4")
-        tt(e6, vw, e4, Op.subtract, "vw e4", "e6")
+        scan(T.rr[:], T.r12[:], T.wr[:], 0.0, Op.mult, Op.subtract, "r12 wr", "rr", cy(GW // 2))
+        tt(e3, kk, mv, Op.subtract, "cw kk", "e3")
+        tt(e4, e3, T.rr[:, M - 1:GW:M], Op.max, "e3 rr", "e4")
+        tt(e6, vw, e4, Op.add, "vw e4", "e6")
         cp(T.do[:], e6, "e6", "do")
         if t == 0: cp(T.ow[:].indirect(T.do[:]), T.tm[:, 0:C], "do tm ow", "ow", sca(C))
         else: cp(T.ow[:].indirect(T.do[:]), T.slw[:], "do slw ow", "ow", sca(C))
-        places(t == R - 1)
+        places()
         cp(T.ow[:].indirect(T.lo[:, 0:6]), T.tm[:, HID + NT * t:HID + NT * t + NT], "lo hid ow", "ow", sca(NT))
         pick(T.oww[:], T.wp4[:], T.ow[:, 1:C + 1], "wp4 ow", "oww", cy(C))
         ts(T.xo[:], T.oww[:, 3:C:4], 4.0, Op.mult, c4, Op.add, "oww c4", "xo", cy(80))
         if t < R - 1:
             act(T.slw[:], T.ow[:].indirect(T.do[:]), "ow do", "slw", c=ga(C))
-            act(T.pib[:], e2, "e2", "pib", 1.0, 191.6)
+            act(T.pib[:], e2, "ee", "pib", 1.0, 191.6)
             act(ra, vw, "vw", "ra", 1.0, RND)
-            act(rd2, ra, "ra", "rd2", 2.0, -2 * RND)
-            act(rv, vw, "vw", "rv", 2.0)
-            tt(fr, rv, rd2, Op.subtract, "rv rd2", "fr")
-            tt(nk, fr, mv, Op.mult, "fr cw", "nk")
-            tt(kk, nk, e4, Op.subtract, "nk e4", "kk")
-            labels()
+            act(T.lb1[:, 0:80:4], vw, "vw", "l0", 2.0)
+            act(T.lb1[:, 1:80:4], ra, "ra", "l1", -2.0, 2 * RND)
+            act(T.la[:, 2:80:4], mv, "cw la", "l2")
+            labels(False)
             tables()
         else:
             act(rev(T.mz, 0), T.tm[:].indirect(idx), tmk, "mz", c=ga(P))
@@ -559,9 +572,8 @@ def rank_program(g, core, T, topo):
             tt(T.pool[:, h0 + b:h0 + 4 * NT:4], T.ps[:, 512 * b:512 * b + NT], T.a64[:, b:4 * NT:4], Op.add, "a64 ps%d" % b, "h%d%d ps%d" % (t, b, b), cy(NT))
         pool += " h%d0 h%d1 h%d2 h%d3" % (t, t, t, t)
         win, hk = T.pool[:, 0:h0 + 4 * NT], pool + " xo"
-        a, b = XV // 4, HALF // 4
-        ts(X[t + 1][:, 0:4 * XV], win.indirect(T.xo[:, 0:a]), 0.015625, Op.mult, None, None, hk, "x%da" % (t + 1), ga(4 * XV))
-        if b > a: act(X[t + 1][:, 4 * XV:4 * HALF], win.indirect(T.xo[:, a:b]), hk, "x%db" % (t + 1), 0.015625, c=ga(4 * (HALF - XV)))
+        b = HALF // 4
+        ts(X[t + 1][:, 0:4 * HALF], win.indirect(T.xo[:, 0:b]), 0.015625, Op.mult, None, None, hk, "x%da" % (t + 1), ga(4 * HALF))
         act(X[t + 1][:, 4 * HALF:4 * C], win.indirect(T.xo[:, b:80]), hk, "x%dc" % (t + 1), 0.015625, c=ga(4 * (C - HALF)))
 
     pack(R, T.qv[:], T.sv[:], "qv", lambda a, n: T.yb[:, a:a + n], "yb")

@@ -6,10 +6,10 @@ STEP = [1, 2, 1]
 HB = 324
 PW = 4 * (C + R * NT)
 OFF, BIG = 1024.0, 1048576.0
-FL = 1024
+FL = 928
 DW = 336
 GS = 200.0
-KEY = 4097.0
+KEY = 1025.0
 LAP = KEY * P
 NONE = C + 1 - 512.0
 EPS = 1.0 / 1024
@@ -17,15 +17,17 @@ MV = 512.0
 RND = 12582912.0
 OW = 424
 M, GW = 12, 240
+TS = 52
+XP, XN = [(0, 20), (20, 40), (40, 60), (60, 80)], "abcd"
 HALF = 160
 GT = 144
 RJ, R512 = 192, 6442450944.0
 CYC, GATHER, SCATTER, CALL = 0.00104, 1.56, 3.8, 0.5
-CASES = [(0.2, 1.6, 2.2, 3.6, 0.3, 0.8), (0.2, 1.8, 2.8, 4.4, 0.4, 1.1), (0.14, 1.6, 2.2, 3.6, 0.3, 1.0)]
-TRIES = 200000
+CASES = [(0.175, 1.6, 2.3, 3.7, 0.3, 0.9), (0.18, 1.3, 1.6, 2.9, 0.25, 0.9), (0.2, 1.8, 2.9, 4.5, 0.4, 1.1)]
+TRIES = 140000
 LANES = {"v": 32, "s": 32, "p": 8, "g": 8}
 N20 = "e3 e6 ra".split()
-N48 = "qd hh lt gg aa ab2 ea n32 vq emp mask0 gd".split()
+N48 = "hh lt gg ea n32 emp mask0".split()
 
 F, B16, I32, U16, Q4, U8 = "float32", "bfloat16", "int32", "uint16", "float8_e4m3fn_x4", "uint8"
 
@@ -41,22 +43,22 @@ SCRATCH = {
     "qw": _s(512, Q4), "sw": _s(512, U8), "qe": _s(512, Q4), "se": _s(512, U8),
     "qx": _s(C, Q4), "sx": _s(C, U8), "qb": _s(128, Q4), "sb": _s(128, U8),
     "ones": _s(528, B16), "eye": _s(528, B16), "dd": _s(4 * DW, B16),
-    "ta": _s(4 * NT, B16), "tb": _s(512, B16), "a64": _s(4 * NT),
+    "ta": _s(4 * NT, B16), "tb": _s(512, B16), "a64": _s(4 * NT, B16),
     "ps": ("psum", [128, 4096], F), "n20": _s(24 * len(N20)), "n48": _s(P * len(N48)),
     "tm": _s(FL + DW), "ip": _s(8, I32), "col": _s(24), "j20": _s(20), "jw": _s(20),
     "jm": _s(C, B16), "wpa": _s(C, B16), "wp4": _s(C, B16), "j4": _s(C, B16), "r12": _s(GW, B16),
-    "base": _s(8), "t1": _s(192), "th": _s(192),
-    "dum": _s(8), "upk": _s(8, U16), "qc": _s(4),
-    "sw_": _s(376), "mk": _s(P), "rm": _s(P), "pc": _s(8), "pm": _s(8, U16),
-    "ga": _s(P, B16), "idx": _s(4, U16), "tu": _s(104), "ub2": _s(56), "pww": _s(NT),
+    "base": _s(4), "ht": _s(3 * P, B16), "kt": _s(3 * P), "tr": _s(3 * P), "t1": _s(3 * TS), "th": _s(3 * TS),
+    "upk": _s(8, U16), "qc": _s(8),
+    "sw_": _s(376), "mk": _s(P), "rm": _s(P), "pc": _s(8), "pm": _s(4, U16),
+    "idx": _s(4, U16), "tu": _s(256), "pww": _s(NT),
     "gt": _s(GT), "rj": _s(RJ + 10 * GT), "rs2": _s(GT, B16), "dec": _s(32),
-    "pa": _s(12), "pb": _s(12), "l9": _s(12), "lo": _s(8, U16), "lf": _s(4, U16),
+    "pa": _s(64), "pb": _s(12), "l9": _s(12), "lo": _s(8, U16), "lf": _s(4, U16),
     "ea0": _s(60), "ee": _s(60), "la": _s(80), "lb1": _s(80), "lab": _s(80),
     "crp": _s(R * 64 + 16, B16), "cg": _s(C, B16), "cw": _s(3 * C, B16), "val": _s(C), "vw": _s(C),
     "d1": _s(GW, B16), "v1": _s(GW, B16), "ab": _s(GW, B16), "inc": _s(GW), "yg": _s(GW), "e16": _s(16),
     "wg": _s(GW, B16), "wr": _s(GW, B16), "rr": _s(GW, B16),
     "vo": _s(20, U16), "do": _s(20, U16), "ow": _s(OW), "slw": _s(C), "ao": _s(24, U16), "oww": _s(C), "xo": _s(80, U16),
-    "mw": _s(376), "mr": _s(C), "mww": _s(C), "pib": _s(20, B16), "po": _s(20, U16),
+    "mr": _s(C), "mww": _s(C), "pib": _s(20, B16), "po": _s(20, U16),
     "es": _s(64), "sc": _s(4), "mz": _s(P), "yb": _s(C),
 }
 for _t in range(R):
@@ -73,7 +75,7 @@ ORDER = {}
 
 def depends(ops):
     last_w, readers, deps = {}, {}, []
-    for n, (e, fn, rd, wr, kind, cost) in enumerate(ops):
+    for n, (rd, wr) in enumerate(o[2:4] for o in ops):
         d = set()
         for k in rd:
             if k in last_w: d.add(last_w[k])
@@ -98,7 +100,13 @@ def arrange(ops, deps):
     for i in range(n):
         for d in deps[i]: users[d].append(i)
     costs = [[call if o[4] in "rR" else o[5] * (f if o[4] == "c" else 1.0) for o in ops] for wake, near, far, wide, call, f in CASES]
-    lates = [[{"d": near, "r": far, "R": wide}.get(o[4], 0.0) + wake for o in ops] for wake, near, far, wide, call, f in CASES]
+    form = [0] * n
+
+    def choose(c, k):
+        form[c], eng[c] = k, "vspgy".index(ops[c][6][k][0])
+        for i in range(len(CASES)): costs[i][c] = ops[c][6][k][2] * CASES[i][5]
+
+    lates = [[{"d": near, "r": far, "R": wide, "w": -wake}.get(o[4], 0.0) + wake for o in ops] for wake, near, far, wide, call, f in CASES]
 
     def play(order, k):
         cost, late = costs[k], lates[k]
@@ -113,8 +121,10 @@ def arrange(ops, deps):
             free[e], last[e], fin[c] = s, c, s + late[c]
         return max(fin), start, held, fin
 
-    def value(order):
-        r = [play(order, k) for k in range(len(CASES))]
+    def value(order, most=1e9):
+        r = [play(order, 0)]
+        if r[0][0] > most: return 1e9, r
+        r += [play(order, k) for k in range(1, len(CASES))]
         return sum(a[0] for a in r) + sum(r[0][3]) / n, r
 
     way = [0.0] * n
@@ -134,11 +144,17 @@ def arrange(ops, deps):
             if not left[u]: pool.append(u)
     rng = np.random.RandomState(1)
     now, runs = value(order)
-    best, kept = now, order
+    best, kept = now, (order, list(form))
     pos = {c: i for i, c in enumerate(order)}
+    free_ = [i for i in range(n) if len(ops[i][6]) > 1]
     for step in range(TRIES):
-        end, start, held, fin = runs[step // 3 % len(CASES)]
-        if step % 3:
+        end, start, held, fin = runs[step // 4 % len(CASES)]
+        back = None
+        if step % 4 == 3:
+            c = free_[rng.randint(len(free_))]
+            back, new = (c, form[c]), order
+            choose(c, (form[c] + 1 + rng.randint(len(ops[c][6]) - 1)) % len(ops[c][6]))
+        elif step % 4:
             c, path = fin.index(end), []
             while c >= 0:
                 if held[c] >= 0 and held[c] not in deps[c]: path.append(c)
@@ -146,7 +162,10 @@ def arrange(ops, deps):
             if not path: continue
             c = path[rng.randint(len(path))]
             p = held[c]
-            if rng.rand() < 0.5:
+            if len(ops[p][6]) > 1 and rng.rand() < 0.3:
+                back, new = (p, form[p]), order
+                choose(p, (form[p] + 1 + rng.randint(len(ops[p][6]) - 1)) % len(ops[p][6]))
+            elif rng.rand() < 0.5:
                 lo = max([pos[d] for d in deps[c]] + [-1]) + 1
                 if lo > pos[p]: continue
                 mates = [i for i in range(lo, pos[p] + 1) if eng[order[i]] == eng[c]][-4:]
@@ -164,19 +183,26 @@ def arrange(ops, deps):
             to = rng.randint(max(lo, pos[c] - 30), min(hi, pos[c] + 30))
             new = order[:pos[c]] + order[pos[c] + 1:]
             new.insert(to, c)
-        v, r = value(new)
+        v, r = value(new, runs[0][0] + 0.25)
         if v <= now + 0.25 * (1 - step / TRIES) * rng.rand():
             order = sorted(new, key=lambda i: r[0][1][i])
             pos = {c: i for i, c in enumerate(order)}
             now, runs = v, r
-            if v < best: best, kept = v, order
-    ORDER[n] = [int(c) for c in kept]
+            if v < best: best, kept = v, (order, list(form))
+        elif back: choose(*back)
+    ORDER[n] = [int(c) for c in kept[0]], kept[1]
     return ORDER[n]
+
+
+def settle(ops):
+    deps = depends(ops)
+    order, form = arrange(ops, deps)
+    return [(o[6][k][0], o[6][k][1], o[2], o[3], o[4], o[6][k][2]) for o, k in zip(ops, form)], deps, order
 
 
 def emit(ops, g, T):
     queue = {"v": g.vector, "s": g.scalar, "p": g.tensor, "g": g, "y": g.sync}
-    deps = depends(ops)
+    ops, deps, order = settle(ops)
     known = {e: 0 for e in queue}
     after, sig, waited, place = {}, {}, set(), {}
     lanes = {e: [] for e in LANES}
@@ -187,7 +213,7 @@ def emit(ops, g, T):
         waited.add(d)
         known[e] |= after[d]
 
-    for n in arrange(ops, deps):
+    for n in order:
         e, fn, rd, wr, kind, cost = ops[n]
         place[n] = len(place)
         for d in sorted(deps[n], key=lambda d: -place[d]):
@@ -232,8 +258,8 @@ def rank_program(g, core, T, topo):
     ops = []
     nsent = [0]
 
-    def add(e, fn, rd, wr, cost, kind="c"):
-        ops.append((e, fn, rd.split(), wr.split(), kind, cost))
+    def add(e, fn, rd, wr, cost, kind="c", more=()):
+        ops.append((e, fn, rd.split(), wr.split(), kind, cost, [(e, fn, cost)] + list(more)))
 
     def cy(n): return max(64, n) * CYC
 
@@ -254,15 +280,20 @@ def rank_program(g, core, T, topo):
     def scan(out, d0, d1, init, o0, o1, rd, wr, c=0.067):
         add("v", lambda: V.tensor_tensor_scan(out, d0, d1, init, o0, o1), rd, wr, c)
 
-    def fill(ap, v, wr, c=0.067):
-        add("v", lambda: V.memset(ap, v), "", wr, c)
+    def fill(ap, v, wr, n, half=False):
+        more = [("s", lambda: S.activation(ap, T.ones[:, 0:n], Act.Copy, scale=float(v)), cy(n))]
+        if v == int(v) and abs(v) < 2 ** 24:
+            more.append(("g", lambda: g.iota(ap, [[0, n]], int(v), 0, allow_small_or_imprecise_dtypes=True), 0.13 + 2 * n * CYC))
+        add("v", lambda: V.memset(ap, v), "ones", wr, cy(n // 2 if half else n), more=more)
 
-    def act(out, a, rd, wr, scale=1.0, bias=None, c=0.067, f=None):
-        if bias is None: add("s", lambda: S.activation(out, a, Act.Copy, scale=scale), rd, wr, c)
-        else: add("s", lambda: S.activation(out, a, f or Act.Identity, bias=bias, scale=scale), rd, wr, c)
-
-    def sfill(out, v, wr, n):
-        act(out, T.ones[:, 0:n], "ones", wr, 0.0, v, cy(n))
+    def act(out, a, rd, wr, scale=1.0, bias=None, c=0.067, f=None, cv=None):
+        if f: return add("s", lambda: S.activation(out, a, f, bias=bias, scale=scale), rd, wr, c)
+        if bias is None:
+            other = (lambda: V.tensor_copy(out, a)) if scale == 1.0 else (lambda: V.tensor_scalar(out, a, scale, None, Op.mult))
+            add("s", lambda: S.activation(out, a, Act.Copy, scale=scale), rd, wr, c, more=[("v", other, cv or c)])
+        else:
+            add("s", lambda: S.activation(out, a, Act.Identity, bias=bias, scale=scale), rd, wr, c,
+                more=[("v", lambda: V.tensor_scalar(out, a, scale, bias, Op.mult, Op.add), cv or c)])
 
     def quant(q, s, a, rd, wr, n=128):
         add("v", lambda: V.quantize_mx(q, s, a), rd, wr, 0.015 + 0.0011 * n)
@@ -297,80 +328,73 @@ def rank_program(g, core, T, topo):
 
     X = [T.x0, T.x1, T.x2, T.x3]
     col = T.col
-    ci, cm, cr, ct, c16, c4, csp, c36, cd, c161, c16m, cz, c4a, cq, cs, cf0, cf1, cl, ck = (col[:, k:k + 1] for k in range(19))
+    ci, cm, cr, ct, c16, c4, csp, c36, c16m, c4a, cq, cs, cf0, cf1, cl, ck = (col[:, k:k + 1] for k in range(16))
     e3, e6, ra = (T.n20[:, 24 * k:24 * k + 20] for k in range(len(N20)))
-    qd, hh, lt, gg, aa, ab2, ea, n32, vq, emp, mask0, gd = (T.n48[:, P * k:P * k + P] for k in range(len(N48)))
+    hh, lt, gg, ea, n32, emp, mask0 = (T.n48[:, P * k:P * k + P] for k in range(len(N48)))
+    UB, VQ, GD = 104, 208, 16
+    gd = T.pa[:, GD:GD + P]
     mv, lap, k2, pit, e2 = T.cw[:, 45:3 * C:48], T.cw[:, 29:3 * C:48], T.ea0[:, 1:60:3], T.ea0[:, 2:60:3], T.ee[:, 2:60:3]
     e4, kk, zz = T.lb1[:, 2:80:4], T.lab[:, 2:80:4], T.lab[:, 3:80:4]
-    at = {k: P * i for i, k in enumerate(N48)}
-    HID, T1S, RS2, T1A = DW, DW + R * NT, DW + R * NT + 80, FL - 32
-    c16s, zero, mask, zg, hs, j48 = (T.tm[:, RS2 + P * k:RS2 + P * k + P] for k in range(6))
-    tmk = "tm tm2 hid t1s0 t1s1 t1s2 c16s zero mask zg hs j48 t1a t1b idx"
+    HID, T1S, T1A = DW, DW + R * NT + P, FL - 32
+    zero = T.tm[:, T1S - P:T1S]
+    qd, mask, hs = (T.tm[:, T1S + 80 + P * k:T1S + 80 + P * k + P] for k in range(3))
+    tmk = "tm tm2 hid zero t1s1 t1s2 qd mask hs t1a t1b idx"
 
     dma("y", T.szb[:, 0:3], T.sz[:], "", "szb")
     dma("s", T.ub[:], T.u[:], "", "ub")
-    dma("y", T.x0[:, 0:4 * HALF], T.x[:, 0:4 * HALF], "", "x0a")
-    dma("s", T.x0[:, 4 * HALF:4 * C], T.x[:, 4 * HALF:4 * C], "", "x0c")
+    dma("y", T.x0[:, 0:4 * HALF], T.x[:, 0:4 * HALF], "", "x0a x0b")
+    dma("s", T.x0[:, 4 * HALF:4 * C], T.x[:, 4 * HALF:4 * C], "", "x0c x0d")
     dma("y", T.qw[:].bitcast(dt.uint8), T.wc[:], "", "qw")
     dma("y", T.sw[:], T.ws[:], "", "sw")
     dma("y", T.vb[:], T.v[:], "", "vb")
 
-    fill(T.ones[:], 1.0, "ones", cy(264))
+    add("v", lambda: V.memset(T.ones[:], 1.0), "", "ones", cy(264))
     iota(T.ip[:, 0:2], [[15, 2]], 0, 1, "ip", False)
     iota(T.tm[:, 0:DW], [[1, DW]], 0, 0, "tm")
-    iota(j48, [[16, 3], [0, 16]], 0, 0, "j48")
     iota(T.j20[:], [[16, 20]], 0, 0, "j20")
     iota(T.jm[:, 0:NT], [[0, NT // 16], [1, 16]], 0, 0, "jm")
     iota(T.j4[:], [[0, C // 4], [1, 4]], 0, 0, "j4")
     if flip: iota(qd, [[-1, 12], [0, 4]], 11, 0, "qd")
     else: iota(qd, [[1, 12], [0, 4]], 0, 0, "qd")
-    fill(T.base[:, 0:4], 0.0, "base1")
-    iota(T.base[:, 4:8], [[64, 4]], 0, 0, "base0")
     iota(T.tm[:, HID:HID + R * NT], [[1, R * NT]], C, 0, "hid")
     iota(hs, [[int(KEY), P]], int(KEY), 0, "hs")
-    iota(T.ow[:], [[0, OW]], C, 0, "ow")
-    iota(T.th[:], [[0, 192]], int(NONE), 0, "th")
+    fill(T.ow[:], 1000.0, "ow", OW)
+    fill(T.th[:], NONE, "th", 3 * TS)
     add("g", lambda: g.affine_select(T.eye[:], T.ones[:], [[1, 528]], Op.is_equal, 0.0, -3, -4), "ones", "eye", 1.27)
     add("g", lambda: g.affine_select(T.r12[:], T.ones[:, 0:GW], [[0, 20], [1, M]], Op.not_equal, 0.0, 0, 0), "ones", "r12", 0.67)
-    fill(T.t1[:], 0.0, "t1", cy(192))
-    fill(T.tu[:, 0:1], 0.0, "enz")
-    fill(T.ub2[:, 0:1], 0.0, "ubz")
-    fill(T.sw_[:, C + 1:376], -1e29, "swz")
-    fill(T.sw_[:, 0:1], -1e29, "swy")
-    fill(T.rs2[:], 0.0, "rs2", cy(GT // 2))
-    fill(T.rs2[:, 0:GT:P], -4 * BIG, "rs2")
-    fill(T.es[:, P:64], 192.49, "esz")
-    fill(zero, 0.0, "zero")
-    fill(c16s, 16.0, "c16s")
-    fill(T.cw[:, 13:3 * C:48], 0.0, "cw")
-    fill(T.ea0[:, 0:60:3], -48.0 / MV, "ea0")
-    fill(T.la[:], 1.0, "la", cy(80))
-    fill(T.la[:, 0:80:4], 0.0, "la")
-    fill(T.pa[:, 0:12:2], BIG, "pa")
-    for k, (a, v) in enumerate(((5 - P, 0.0), (5 + P, 1.0), (5 + 2 * P, 1.0), (5 + 3 * P, -1.0),
-                                (-4 * P, 1.0), (-3 * P, -161.0), (-2 * P, R512), (-P, -R512))):
-        sfill(T.rj[:, RJ + a:RJ + a + 25 * P + 1:5 * P], v, "rk%d" % k, 6)
-    fill(gd, BIG, "gd")
-    for k, v in enumerate((192.0, 192.0 + 900, 191.0, BIG)): fill(T.t1[:, P + k:192:64], v, "t1")
-    fill(T.d1[:], -1.0, "d1", cy(GW // 2))
-    fill(T.tm[:, T1S:T1S + 32], 0.0, "t1s0")
-    fill(T.tm[:, T1S + P:T1S + 80], -1.0, "t1s2")
-    for t in range(R): sfill(X[t][:, 4 * C:4 * HB], 0.0, "x%dz" % t, 16)
-    sfill(T.dd[:, C:4 * DW:DW], 0.0, "ddz", 4)
-    sfill(T.mw[:], 1000.0, "mw", 376)
-    sfill(T.tb[:, 4 * NT:512], 0.0, "tbz", 128)
-    act(T.tm[:, FL:FL + DW], T.tm[:, 0:DW], "tm", "tm2", c=cy(DW))
+    fill(T.tu[:, 0:VQ + 1:UB], 0.0, "enz", 3)
+    fill(T.sw_[:, C + 1:376], -1e29, "swz", 375 - C)
+    fill(T.sw_[:, 0:1], -1e29, "swy", 1)
+    fill(T.rs2[:], 0.0, "rs2", GT, True)
+    fill(T.rs2[:, 0:GT:P], -4 * BIG, "rs2", 3)
+    fill(T.es[:, P:64], 192.49, "esz", 16)
+    fill(T.tm[:, T1S - P:T1S + 32], 0.0, "zero", 80)
+    fill(T.tm[:, T1S + P:T1S + 80], -1.0, "t1s2", 32)
+    fill(T.cw[:, 13:3 * C:48], 0.0, "cw", 20)
+    fill(T.ea0[:, 0:60:3], -48.0 / MV, "ea0", 20)
+    fill(T.la[:], 1.0, "la", 80)
+    fill(T.la[:, 0:80:4], 0.0, "la", 20)
+    fill(T.pa[:], BIG, "pa", 64)
+    fill(T.rj[:, RJ + 5 - P:RJ + 6 + 28 * P:P], 1.0, "rj0 rj1 rk0 rk1", 30)
+    for k, (a, v) in enumerate(((5 - P, 0.0), (5 + 3 * P, -1.0), (-4 * P, 1.0), (-3 * P, -161.0), (-2 * P, R512), (-P, -R512))):
+        fill(T.rj[:, RJ + a:RJ + a + 25 * P + 1:5 * P], v, "rk%d" % k, 6)
+    for k, v in enumerate((0.0, 900.0, -1.0, BIG)): fill(T.t1[:, P + k:3 * TS:TS], v, "t1s%d" % (k + 3), 3)
+    fill(T.d1[:], -1.0, "d1", GW, True)
+    for t in range(R): fill(X[t][:, 4 * C:4 * HB], 0.0, "x%dz" % t, 16)
+    fill(T.dd[:, C:4 * DW:DW], 0.0, "ddz", 4)
+    fill(T.tb[:, 4 * NT:512], 0.0, "tbz", 128, True)
+    dma("y", T.tm[:, FL:FL + DW], T.tm[:, 0:DW], "tm", "tm2")
     for k in range(4):
-        act(T.pool[:, C * k:C * k + C], T.x0[:, C * k:C * k + C], "x0a" if k < 2 else "x0c", "p%d" % k, 64.0, c=cy(C))
+        act(T.pool[:, C * k:C * k + C], T.x0[:, C * k:C * k + C], "x0a x0b" if k < 2 else "x0c x0d", "p%d" % k, 64.0, c=cy(C), cv=cy(C // 2))
     ts(T.ip[:, 2:4], T.ip[:, 0:2], 15, Op.bitwise_and, None, None, "ip", "ip1")
     ts(T.ip[:, 4:5], T.ip[:, 0:1], 2, Op.arith_shift_right, 3, Op.bitwise_and, "ip", "ip2")
     ts(T.ip[:, 5:6], T.ip[:, 0:1], 3, Op.bitwise_and, None, None, "ip", "ip3")
     cp(col[:, 0:2], T.ip[:, 2:4], "ip1", "ci")
     cp(col[:, 2:4], T.ip[:, 4:6], "ip2 ip3", "cr")
-    for k, nm, a, b in ((c16, "c16", -OFF, 15 * OFF), (c161, "c161", -OFF, 15 * OFF + 1), (c16m, "c16m", -OFF, 15 * OFF - 1),
+    for k, nm, a, b in ((c16, "c16", -OFF, 15 * OFF), (c16m, "c16m", -OFF, 15 * OFF - 1),
                         (cs, "cs", OFF, FL - 1 - 15 * OFF), (cf0, "cf0", 4096 * OFF, 2048 - 4096 * 15 * OFF),
-                        (cf1, "cf1", 4096 * OFF, 6144 - 4096 * 15 * OFF), (cd, "cd", 1.0, C + 1.0),
-                        (cz, "cz", sg / 48, 47.0 * flip / 48), (cq, "cq", sg, 15.0 * flip),
+                        (cf1, "cf1", 4096 * OFF, 6144 - 4096 * 15 * OFF),
+                        (cq, "cq", sg, 15.0 * flip),
                         (cl, "cl", -OFF / 16, 15 * OFF / 16 + 192 - 0.31), (ck, "ck", 32 * OFF, -32 * 15 * OFF)):
         act(k, ci, "ci", nm, a, b)
     act(c4a, cr, "cr", "c4a", -4 * OFF, 12 * OFF)
@@ -378,22 +402,22 @@ def rank_program(g, core, T, topo):
     act(c36, cm, "ci", "c36", 1.0, 36.0)
     ts(csp, cm, 12.0, Op.is_ge, c36, Op.mult, "ci c36", "csp")
     ts(T.jm[:, 0:NT], T.jm[:, 0:NT], ci, Op.is_equal, BIG, Op.mult, "jm ci", "jm")
-    ts(T.wpa[:, 0:NT], T.jm[:, 0:NT], -OFF, Op.add, None, None, "jm", "wpa")
-    act(T.wpa[:, NT:2 * NT], T.wpa[:, 0:NT], "wpa", "wpb", c=cy(NT))
-    act(T.wpa[:, 2 * NT:C], T.wpa[:, 0:C - 2 * NT], "wpa wpb", "wpc", c=cy(C - 2 * NT))
+    act(T.wpa[:, 0:NT], T.jm[:, 0:NT], "jm", "wpa", 1.0, -OFF, cy(NT), cv=cy(64))
+    act(T.wpa[:, NT:2 * NT], T.wpa[:, 0:NT], "wpa", "wpb", c=cy(NT), cv=cy(64))
+    act(T.wpa[:, 2 * NT:C], T.wpa[:, 0:C - 2 * NT], "wpa wpb", "wpc", c=cy(128), cv=cy(64))
     ts(T.j4[:], T.j4[:], cr, Op.is_equal, BIG, Op.mult, "j4 cr", "j4", cy(C // 2))
-    act(T.wp4[:], T.j4[:], "j4", "wp4", 1.0, -OFF, cy(C))
+    act(T.wp4[:], T.j4[:], "j4", "wp4", 1.0, -OFF, cy(C), cv=cy(C // 2))
     ts(T.tm[:, T1A:T1A + 16], T.tm[:, 0:16], cq, Op.is_equal, 4097.0, Op.mult, "tm cq", "t1a")
     ts(T.tm[:, T1A + 16:FL], T.tm[:, 0:16], cq, Op.is_ge, None, None, "tm cq", "t1b")
     tt(T.tm[:, T1S + 32:T1S + P], T.tm[:, T1A:T1A + 16], T.tm[:, T1A + 16:FL], Op.subtract, "t1a t1b", "t1s1")
     cp(T.upk[:], T.j20[:, 0:8], "j20", "upk")
-    act(T.crp[:, 0:R * 64], T.ones[:, 0:R * 64], "ones c16", "crp0 crp1 crp2", 0.0, c16, cy(R * 64))
-    act(T.crp[:, R * 64:R * 64 + 16], T.crp[:, 0:16], "crp0", "crs", 1.0, MV)
-    act(T.base[:], T.base[:], "base0 base1 csp", "base0 base1", 1.0, csp)
-    act(T.pb[:, 1:12:2], T.j20[:, 0:6], "j20 cd", "dum", 1.0, cd)
+    act(T.crp[:, 0:R * 64], T.ones[:, 0:R * 64], "ones c16", "crp0 crp1 crp2", 0.0, c16, cy(R * 64), cv=cy(R * 32))
+    act(T.crp[:, R * 64:R * 64 + 16], T.ones[:, 0:16], "ones c16", "crs", MV, c16)
+    act(T.base[:], T.j20[:, 0:4], "j20 csp", "base", TS / 16, csp)
     act(T.jw[:], T.j20[:], "j20 ci", "jw", 1.0, ci)
-    act(T.qc[:, 0:3], T.jw[:, 0:3], "jw", "qc", sg * KEY, 2049 + 47 * KEY * flip)
-    act(zg, j48, "j48 cz", "zg", sg / 48, cz)
+    act(T.pb[:, 1:12:2], T.jw[:, 0:6], "jw", "dum", 1.0, C + 1.0)
+    act(T.qc[:, 0:3], T.jw[:, 0:3], "jw", "qc", sg * KEY, 513 + 47 * KEY * flip - 192 * LAP)
+    act(T.qc[:, 4:7], T.jw[:, 0:3], "jw", "zq", -sg / 48, -47.0 * flip / 48)
     quant(T.qu0[:], T.su0[:], T.ub[:], "ub", "qu0")
     add("s", lambda: S.activation(T.su[:], T.su0[:].indirect(T.upk[:]), Act.Copy), "qu0 upk", "su", ga(128))
     cp(T.qu[:].bitcast(dt.uint32), T.qu0[:].bitcast(dt.uint32).indirect(T.upk[:]), "qu0 upk", "qu", ga(128))
@@ -415,40 +439,43 @@ def rank_program(g, core, T, topo):
             scan(T.tu[:, 1:P + 1], un, zero, 0.0, Op.add, Op.add, "un zero", "en")
             return
         act(rev(T.tu, P + 1), T.tm[:].indirect(idx), tmk, "un", 1.0 + EPS, c=ga(P))
-        act(rev(T.ub2, 1), T.tm[:].indirect(idx), tmk, "ub2", -EPS, c=ga(P))
-        scan(T.tu[:, 1:P + 1], un, T.ub2[:, 0:P], 0.0, Op.add, Op.add, "un ub2 ubz", "en")
+        act(rev(T.tu, UB + 1), T.tm[:].indirect(idx), tmk, "ub2", -EPS, c=ga(P))
+        scan(T.tu[:, 1:P + 1], un, T.tu[:, UB:UB + P], 0.0, Op.add, Op.add, "un ub2 enz", "en")
 
     def places():
         pick(T.pww[:], T.wpa[:, 0:NT], rev(T.tu, 1, n=NT), "wpa en un", "pww", cy(NT))
         act(T.pb[:, 0:6:2], endp, "pww c16", "en6a", 1.0, c16)
         act(T.pb[:, 6:12:2], endp, "pww c16m", "en6b", 1.0, c16m)
-        act(T.pa[:, 1:6:2], sizp, "pww cf0", "f6a", -4096.0, cf0, f=Act.Relu)
-        act(T.pa[:, 7:12:2], sizp, "pww cf1", "f6b", -4096.0, cf1, f=Act.Relu)
-        scan(T.l9[:], T.pa[:], T.pb[:], 0.0, Op.add, Op.min, "en6a en6b f6a f6b pa dum", "l9")
+        act(T.pa[:, 1:6:2], sizp, "pww cf0 pa", "f6a", -4096.0, cf0, f=Act.Relu)
+        act(T.pa[:, 7:12:2], sizp, "pww cf1 pa", "f6b", -4096.0, cf1, f=Act.Relu)
+        scan(T.l9[:], T.pa[:, 0:12], T.pb[:], 0.0, Op.add, Op.min, "en6a en6b f6a f6b pa dum", "l9")
         cp(T.lo[:, 0:6], T.l9[:, 1:12:2], "l9", "lo")
 
     def tables():
         tt(ea, T.tm[:, 0:P], un, Op.add, "tm un", "ea", cy(96))
         act(T.es[:, 0:P], ea, "ea", "es", 1.0 / 48, 191.5 + 0.3 / 48)
         act(T.sc[:, 0:3], sizp, "pww cs", "sc", -1.0, cs)
-        act(T.n48[:, at["gd"]:at["gd"] + P:16], T.sc[:, 0:3], "sc gd", "t1n", -11.0, 2292 - (FL - 1) - GS)
+        act(T.pa[:, GD:GD + P:16], T.sc[:, 0:3], "sc pa", "t1n", -11.0, 2292 - (FL - 1) - GS)
         tt(hh, T.tu[:, 0:P], hs, Op.subtract, "en enz hs", "hh", cy(96))
         for c in range(3):
             a = T1S + (16 * c if flip else 32 - 16 * c)
-            act(T.t1[:, 64 * c:64 * c + P], T.tm[:, a:a + P], "sc t1s0 t1s1 t1s2 t1", "t1%d" % c, -1.0, T.sc[:, c:c + 1], f=Act.Relu)
-            act(T.th[:, 64 * c:64 * c + P], hh, "hh qc th", "th%d" % c, 1.0, T.qc[:, c:c + 1])
-        tt(T.n48[:, at["gd"] + 14:at["gd"] + P:16], T.pb[:, 0:6:2], T.pa[:, 1:6:2], Op.subtract, "en6a f6a gd", "own0")
-        tt(T.n48[:, at["gd"] + 15:at["gd"] + P:16], T.pb[:, 6:12:2], T.pa[:, 7:12:2], Op.subtract, "en6b f6b gd", "own1")
+            ht, kt, tr = (buf[:, P * c:P * c + P] for buf in (T.ht, T.kt, T.tr))
+            act(ht, T.es[:, 0:P], "es zq", "ht%d" % c, 1.0, T.qc[:, 4 + c:5 + c])
+            act(kt, ht, "ht%d qc" % c, "kt%d" % c, LAP, T.qc[:, c:c + 1])
+            tt(T.th[:, TS * c:TS * c + P], kt, hh, Op.add, "kt%d hh th" % c, "th%d" % c, cy(96))
+            act(tr, T.tm[:, a:a + P], "sc zero t1s1 t1s2", "tr%d" % c, -1.0, T.sc[:, c:c + 1], f=Act.Relu)
+            tt(T.t1[:, TS * c:TS * c + P], tr, ht, Op.subtract, "tr%d ht%d" % (c, c), "t1%d" % c, cy(96))
+        tt(T.pa[:, GD + 14:GD + P:16], T.pb[:, 0:6:2], T.pa[:, 1:6:2], Op.subtract, "en6a f6a pa", "own0")
+        tt(T.pa[:, GD + 15:GD + P:16], T.pb[:, 6:12:2], T.pa[:, 7:12:2], Op.subtract, "en6b f6b pa", "own1")
 
     def first_labels():
-        act(n32, T.tm[:, 0:DW].indirect(idx), "tm idx", "n32", 1.0 / 32, c=ga(P))
-        fill(vq[:, 0:1], 0.0, "vq0")
-        scan(vq[:, 1:P], n32[:, 0:P - 1], c16s[:, 1:P], 0.0, Op.add, Op.add, "n32 c16s", "vq")
+        act(n32, un, "un", "n32", 1.0 / 32, 16.0)
+        scan(T.tu[:, VQ + 1:VQ + P], n32[:, 0:P - 1], zero[:, 1:P], 0.0, Op.add, Op.add, "n32 zero", "vq")
         ts(T.lf[:, 0:3], endp, c16, Op.add, None, None, "pww c16", "lf")
         act(emp, rev(T.tu, P + 1), "un", "emp", 2e29, -1e29)
         tt(mask0, mask, emp, Op.min, "mask emp", "mask0", cy(96))
-        cp(T.mw[:].indirect(T.lo[:, 0:3]), rev(T.n48, at["vq"]), "vq vq0 lo mw", "mw", sca(P))
-        scan(T.mr[:, C - 1::-1], T.mw[:, C:0:-1], T.mw[:, C:0:-1], 1000.0, Op.min, Op.min, "mw", "mr", cy(C))
+        cp(T.ow[:].indirect(T.lo[:, 0:3]), rev(T.tu, VQ), "vq enz lo ow", "ow", sca(P))
+        scan(T.mr[:, C - 1::-1], T.ow[:, C:0:-1], T.ow[:, C:0:-1], 1000.0, Op.min, Op.min, "ow", "mr", cy(C))
         pick(T.mww[:], T.wpa[:], T.mr[:], "wpa wpb wpc mr", "mww", cy(C))
         act(T.pib[:], T.mww[:, 15:C:16], "mww cl", "pib", 1.0 / 16, cl)
         act(T.lb1[:, 0:80:4], T.jw[:], "jw", "l0")
@@ -473,12 +500,11 @@ def rank_program(g, core, T, topo):
 
     def pack(t, wq, ws, wk, out, ok):
         qx, sx = (T["qx%d" % t], T["sx%d" % t]) if t < R else (T.qx, T.sx)
-        for h, a, n, rd in ((0, 0, HALF, "x%da" % t), (1, HALF, C - HALF, "x%dc" % t)):
+        for h, a, n, rd in ((0, 0, HALF, "x%da x%db" % (t, t)), (1, HALF, C - HALF, "x%dc x%dd" % (t, t))):
             nm = "ab"[h]
             quant(qx[:, a:a + n], sx[:, a:a + n], X[t][:, 4 * a:4 * a + 4 * n], rd, "qx%s%d" % (nm, t), n)
             mm(h, n, wq, ws, qx[:, a:a + n], sx[:, a:a + n], wk + " qx%s%d" % (nm, t))
-            if h: cp(out(a, n), T.ps[:, 512 * h:512 * h + n], "ps%d" % h, ok + nm + " ps%d" % h, cy(n))
-            else: act(out(a, n), T.ps[:, 512 * h:512 * h + n], "ps%d" % h, ok + nm + " ps%d" % h, c=cy(n))
+            act(out(a, n), T.ps[:, 512 * h:512 * h + n], "ps%d" % h, ok + nm + " ps%d" % h, c=cy(n))
 
     sizes(True)
     places()
@@ -487,7 +513,7 @@ def rank_program(g, core, T, topo):
     labels(True)
     pool = "p0 p1 p2 p3"
     for t in range(R):
-        xk = "x%da x%dc x%dz" % (t, t, t)
+        xk = "x%da x%db x%dc x%dd x%dz" % (t, t, t, t, t)
         pack(t, T.qu[:], T.su[:], "qu su", lambda a, n: T.sw_[:, 1 + a:1 + a + n], "sw")
         qx, sx, ql, sl, arr = T["qx%d" % t], T["sx%d" % t], T["ql%d" % t], T["sl%d" % t], T.sem["arr%d" % t]
         na = send(ql[:].bitcast(dt.uint8), qx[:].bitcast(dt.uint8), arr, t, "qxa%d qxb%d" % (t, t), "r0", "R")
@@ -500,23 +526,20 @@ def rank_program(g, core, T, topo):
         else: tt(T.mk[:], T.sw_[:].indirect(T.lf[:, 0:3]), mask0, Op.min, "swa swb swz swy lf mask0", "mk", ga(P))
         scan(T.rm[:], rev(T.mk, 0), rev(T.mk, 0), -3e29, Op.max, Op.max, "mk", "rm")
         add("s", lambda: S.activation(lt, T.rm[:], Act.Sign, bias=T.rm[:, P - 1:P], scale=-1.0, accum_out=T.pc[:, 0:1]), "rm", "lt pc", 0.09)
-        ts(T.pm[:], T.base[:], T.pc[:, 0:1], Op.add, None, None, "pc base0", "pm")
+        ts(T.pm[:], T.base[:], T.pc[:, 0:1], Op.add, None, None, "pc base", "pm")
         crp = T.crp[:, 64 * t:64 * t + 64]
         cp(crp.indirect(T.pm[:, 0:1]), T.crp[:, R * 64:R * 64 + 16], "pm crs crp%d" % t, "crp%d" % t, sca(16))
-        pm3, pm64 = T.pm[:, 0:3], T.pm[:, 4:7]
-        tt(T.ga[:], T.es[:].indirect(pm3), zg, Op.subtract, "es esz pm zg", "ga", ga(P))
-        tt(gg, T.t1[:].indirect(pm64), T.ga[:], Op.subtract, "t1 t10 t11 t12 pm ga", "gg", ga(P))
-        scan(T.gt[:, 0:GT:3], gg, gd, 0.0, Op.add, Op.min, "gg gd t1n own0 own1", "gs")
+        pm64 = T.pm[:, 0:3]
+        act(gg, T.t1[:].indirect(pm64), "t1s3 t1s4 t1s5 t1s6 t10 t11 t12 pm", "gg", c=ga(P))
+        scan(T.gt[:, 0:GT:3], gg, gd, 0.0, Op.add, Op.min, "gg pa t1n own0 own1", "gs")
         ts(idx, T.gt[:, 39:GT:P], -1.0, Op.mult, 0.1 - GS, Op.add, "gs", "idx")
-        ts(aa, T.ga[:], -192.0, Op.add, LAP, Op.mult, "ga", "aa")
-        act(ab2, T.ga[:], "ga", "ab2", LAP, -193 * LAP)
-        tt(T.gt[:, 1:GT:3], T.th[:].indirect(pm64), aa, Op.add, "th th0 th1 th2 pm aa", "g1", ga(P))
-        tt(T.gt[:, 2:GT:3], T.th[:].indirect(pm64), ab2, Op.add, "th th0 th1 th2 pm ab2", "g2", ga(P))
+        act(T.gt[:, 1:GT:3], T.th[:].indirect(pm64), "th th0 th1 th2 pm", "g1", c=ga(P))
+        act(T.gt[:, 2:GT:3], T.th[:].indirect(pm64), "th th0 th1 th2 pm", "g2", 1.0, -LAP, ga(P))
         a, b = RJ + 5 * (GT - 1), RJ + 5 * GT
         scan(T.rj[:, a:RJ - 1:-5], T.rs2[:], T.gt[:, GT - 1::-1], 0.0, Op.add, Op.max, "rs2 g1 g2 gs", "rj0", cy(GT))
         scan(T.rj[:, b + 5 * (GT - 2):b - 1:-5], T.gt[:, GT - 2::-1], T.rj[:, a:RJ + 4:-5], NONE, Op.max, Op.min, "rj0 g1 g2 gs", "rj1", cy(GT))
         scan(T.dec[:, 0:30], T.rj[:, RJ + 5 - P:RJ + 6 + 28 * P:P], T.rj[:, RJ - 4 * P:RJ + 1 + 25 * P:P], 0.0, Op.mult, Op.add,
-             "rj0 rj1 rk0 rk1 rk2 rk3 rk4 rk5 rk6 rk7", "dec")
+             "rj0 rj1 rk0 rk1 rk2 rk3 rk4 rk5", "dec")
         lm, lp, lis = T["lm%d" % t], T["lp%d" % t], T.sem["lis%d" % t]
         ts(lm[:, 0:6], T.dec[:, 4:30:5], -0.9, Op.add, None, None, "dec", "lm%d" % t)
         nl = send(lp[:, 0:6], lm[:, 0:6], lis, t, "lm%d" % t, "r3", "r")
@@ -524,14 +547,17 @@ def rank_program(g, core, T, topo):
         for b in range(4):
             ts(T.ao[:, 6 * b:6 * b + 6], lm[:, 0:6], 4.0, Op.mult, float(b), Op.add, "lm%d" % t, "ao%d" % b)
             act(T.ta[:, b:4 * NT:4], win.indirect(T.ao[:, 6 * b:6 * b + 6]), "ao%d %s" % (b, xk), "ta%d" % b, c=ga(NT))
-        act(T.a64[:], T.ta[:], "ta0 ta1 ta2 ta3", "a64", 64.0, c=cy(384))
+        act(T.a64[:], T.ta[:], "ta0 ta1 ta2 ta3", "a64", 64.0, c=cy(384), cv=cy(192))
         sizes(False)
-        act(T.cg[:], crp.indirect(T.po[:]), "crp%d po" % t, "cg", c=ga(C))
-        pick(T.cw[:, 0:3 * C:3], T.wpa[:], T.cg[:], "wpa wpb wpc cg cw", "cw", cy(C // 2))
+        for h in range(2):
+            act(T.cg[:, HALF * h:HALF * h + HALF], crp.indirect(T.po[:, 10 * h:10 * h + 10]), "crp%d po" % t, "cg%d" % h, c=ga(HALF))
+        pick(T.cw[:, 0:3 * C:3], T.wpa[:], T.cg[:], "wpa wpb wpc cg0 cg1 cw", "cw", cy(C // 2))
         scan(T.ee[:], T.cw[:, 13:3 * C:16], T.ea0[:], 0.0, Op.mult, Op.add, "cw k2 pit ea0", "ee")
         ts(T.vo[:], e2, 0.25, Op.add, None, None, "ee", "vo")
-        act(T.val[:], T.tu[:, 0:P + 1].indirect(T.vo[:]), "en enz vo c161", "val", 1.0, c161, ga(C))
-        pick(T.vw[:], T.wpa[:], T.val[:], "wpa wpb wpc val", "vw", cy(C))
+        for h in range(2):
+            a = HALF * h
+            act(T.val[:, a:a + HALF], T.tu[:, 0:P + 1].indirect(T.vo[:, 10 * h:10 * h + 10]), "en enz vo c16", "val%d" % h, 1.0, c16, ga(HALF))
+            pick(T.vw[:, a:a + HALF], T.wpa[:, 0:HALF], T.val[:, a:a + HALF], "wpa wpb val%d" % h, "vw%d" % h, cy(HALF))
         vw = T.vw[:, 15:C:16]
         act(T.e16[:], T.es[:].indirect(T.pm[:, 0:1]), "es esz pm", "e16", c=0.09)
         for m in range(M):
@@ -540,8 +566,8 @@ def rank_program(g, core, T, topo):
         scan(T.rr[:], T.r12[:], T.wr[:], 0.0, Op.mult, Op.subtract, "r12 wr", "rr", cy(GW // 2))
         tt(e3, kk, mv, Op.subtract, "cw kk", "e3")
         tt(e4, e3, T.rr[:, M - 1:GW:M], Op.max, "e3 rr", "e4")
-        tt(e6, vw, e4, Op.add, "vw e4", "e6")
-        cp(T.do[:], e6, "e6", "do")
+        tt(e6, vw, e4, Op.add, "vw0 vw1 e4", "e6")
+        ts(T.do[:], e6, 1.0, Op.add, None, None, "e6", "do")
         if t == 0: cp(T.ow[:].indirect(T.do[:]), T.tm[:, 0:C], "do tm ow", "ow", sca(C))
         else: cp(T.ow[:].indirect(T.do[:]), T.slw[:], "do slw ow", "ow", sca(C))
         places()
@@ -551,8 +577,8 @@ def rank_program(g, core, T, topo):
         if t < R - 1:
             act(T.slw[:], T.ow[:].indirect(T.do[:]), "ow do", "slw", c=ga(C))
             act(T.pib[:], e2, "ee", "pib", 1.0, 191.6)
-            act(ra, vw, "vw", "ra", 1.0, RND)
-            act(T.lb1[:, 0:80:4], vw, "vw", "l0", 2.0)
+            act(ra, vw, "vw0 vw1", "ra", 1.0, RND)
+            act(T.lb1[:, 0:80:4], vw, "vw0 vw1", "l0", 2.0)
             act(T.lb1[:, 1:80:4], ra, "ra", "l1", -2.0, 2 * RND)
             act(T.la[:, 2:80:4], mv, "cw la", "l2")
             labels(False)
@@ -572,9 +598,8 @@ def rank_program(g, core, T, topo):
             tt(T.pool[:, h0 + b:h0 + 4 * NT:4], T.ps[:, 512 * b:512 * b + NT], T.a64[:, b:4 * NT:4], Op.add, "a64 ps%d" % b, "h%d%d ps%d" % (t, b, b), cy(NT))
         pool += " h%d0 h%d1 h%d2 h%d3" % (t, t, t, t)
         win, hk = T.pool[:, 0:h0 + 4 * NT], pool + " xo"
-        b = HALF // 4
-        ts(X[t + 1][:, 0:4 * HALF], win.indirect(T.xo[:, 0:b]), 0.015625, Op.mult, None, None, hk, "x%da" % (t + 1), ga(4 * HALF))
-        act(X[t + 1][:, 4 * HALF:4 * C], win.indirect(T.xo[:, b:80]), hk, "x%dc" % (t + 1), 0.015625, c=ga(4 * (C - HALF)))
+        for k, (a, b) in enumerate(XP):
+            act(X[t + 1][:, 16 * a:16 * b], win.indirect(T.xo[:, a:b]), hk, " ".join("x%d%s" % (t + 1, n) for n in XN[k]), 0.015625, c=ga(16 * (b - a)))
 
     pack(R, T.qv[:], T.sv[:], "qv", lambda a, n: T.yb[:, a:a + n], "yb")
     dma("y", T.oc[:, 0:4 * HALF], T.qx[:, 0:HALF].bitcast(dt.uint8), "qxa3", "oca")

@@ -4,30 +4,36 @@ from concourse.mybir import dt, AluOpType as Op, ActivationFunctionType as Act
 C, P, NT, R = 320, 48, 96, 3
 STEP = [1, 2, 1]
 HB = 324
-PW = 4 * (C + R * NT)
+PW = C + R * NT
 OFF, BIG = 1024.0, 1048576.0
 FL = 928
 DW = 336
 GS = 200.0
 KEY = 1025.0
 LAP = KEY * P
+HC = KEY * 512
 NONE = C + 1 - 512.0
-EPS = 1.0 / 1024
 MV = 512.0
+EPS, MID = 1.0 / MV, 0.3125
 RND = 12582912.0
 OW = 424
 M, GW = 12, 240
 TS = 52
-XP, XN = [(0, 20), (20, 40), (40, 60), (60, 80)], "abcd"
-HALF = 160
+ANEW = (0,)
+HALF, QH = 160, 192
+XP = [(0, 0, C), (1, 0, C), (2, 0, QH), (2, QH, C), (3, 0, QH), (3, QH, C)]
 GT = 144
-RJ, R512 = 192, 6442450944.0
-CYC, GATHER, SCATTER, CALL = 0.00104, 1.56, 3.8, 0.5
-CASES = [(0.175, 1.6, 2.3, 3.7, 0.3, 0.9), (0.18, 1.3, 1.6, 2.9, 0.25, 0.9), (0.2, 1.8, 2.9, 4.5, 0.4, 1.1)]
-TRIES = 140000
+RJ, DN, R512 = 192, 11, 6442450944.0
+CYC, CALL = 0.00104, 0.5
+CASES = [(0.19, 0.9, 0.9, 2.0, 0.3, 0.92, 1.56, 3.8, 1.0), (0.22, 1.0, 1.1, 2.5, 0.4, 0.9, 1.4, 3.0, 1.4),
+         (0.17, 1.1, 1.2, 2.4, 0.4, 1.08, 1.7, 4.8, 1.0), (0.18, 1.0, 1.1, 2.4, 0.35, 1.02, 2.05, 2.1, 1.1)]
+SLOW = (1.3, 1.6, 0.9, 0.4, -0.4)
+FIRST, TRIES, SPELL, SPAN, HEAT = 30000, 800000, 6000, 80, 0.4
+NEAR, REACH, SW, AIM, SLACK = 0.1, 40, 0.3, 0.7, 0.05
+LONG = "slw val".split()
 LANES = {"v": 32, "s": 32, "p": 8, "g": 8}
-N20 = "e3 e6 ra".split()
-N48 = "hh lt gg ea n32 emp mask0".split()
+N20 = "e3 e6".split()
+N48 = "hh lt vq ea r16 iom".split()
 
 F, B16, I32, U16, Q4, U8 = "float32", "bfloat16", "int32", "uint16", "float8_e4m3fn_x4", "uint8"
 
@@ -37,38 +43,38 @@ def _s(n, d=F):
 
 
 SCRATCH = {
-    "pool": _s(PW, B16), "x0": _s(4 * HB, B16), "x1": _s(4 * HB, B16), "x2": _s(4 * HB, B16), "x3": _s(4 * C, B16),
+    "pool": _s(4 * PW, B16), "x0": _s(4 * HB, B16), "x1": _s(4 * HB, B16), "x2": _s(4 * HB, B16), "x3": _s(4 * C, B16),
     "ub": _s(512, B16), "vb": _s(512, B16), "szb": _s(4, I32),
     "qu0": _s(128, Q4), "su0": _s(128, U8), "qu": _s(128, Q4), "su": _s(128, U8), "qv": _s(128, Q4), "sv": _s(128, U8),
     "qw": _s(512, Q4), "sw": _s(512, U8), "qe": _s(512, Q4), "se": _s(512, U8),
-    "qx": _s(C, Q4), "sx": _s(C, U8), "qb": _s(128, Q4), "sb": _s(128, U8),
-    "ones": _s(528, B16), "eye": _s(528, B16), "dd": _s(4 * DW, B16),
-    "ta": _s(4 * NT, B16), "tb": _s(512, B16), "a64": _s(4 * NT, B16),
+    "qx": _s(C, Q4), "sx": _s(C, U8), "qb": _s(2 * NT, Q4), "sb": _s(2 * NT, U8),
+    "ones": _s(256, B16), "eye": _s(528, B16), "dd": _s(4 * HB, B16),
+    "ta": _s(8 * NT, B16), "tb": _s(8 * NT, B16), "odd": _s(2 * NT, B16), "a64": _s(4 * NT, B16),
     "ps": ("psum", [128, 4096], F), "n20": _s(24 * len(N20)), "n48": _s(P * len(N48)),
-    "tm": _s(FL + DW), "ip": _s(8, I32), "col": _s(24), "j20": _s(20), "jw": _s(20),
-    "jm": _s(C, B16), "wpa": _s(C, B16), "wp4": _s(C, B16), "j4": _s(C, B16), "r12": _s(GW, B16),
-    "base": _s(4), "ht": _s(3 * P, B16), "kt": _s(3 * P), "tr": _s(3 * P), "t1": _s(3 * TS), "th": _s(3 * TS),
+    "tm": _s(FL + DW), "ip": _s(8, I32), "col": _s(8), "j20": _s(20), "jw": _s(20),
+    "jm": _s(NT, B16), "wpa": _s(C, B16), "r12": _s(GW, B16),
+    "base": _s(4), "ht": _s(3 * P, B16), "kt": _s(3 * P), "tr": _s(3 * P), "t1": _s(4 * TS), "th": _s(3 * TS), "gg": _s(64),
     "upk": _s(8, U16), "qc": _s(8),
     "sw_": _s(376), "mk": _s(P), "rm": _s(P), "pc": _s(8), "pm": _s(4, U16),
-    "idx": _s(4, U16), "tu": _s(256), "pww": _s(NT),
-    "gt": _s(GT), "rj": _s(RJ + 10 * GT), "rs2": _s(GT, B16), "dec": _s(32),
-    "pa": _s(64), "pb": _s(12), "l9": _s(12), "lo": _s(8, U16), "lf": _s(4, U16),
-    "ea0": _s(60), "ee": _s(60), "la": _s(80), "lb1": _s(80), "lab": _s(80),
-    "crp": _s(R * 64 + 16, B16), "cg": _s(C, B16), "cw": _s(3 * C, B16), "val": _s(C), "vw": _s(C),
-    "d1": _s(GW, B16), "v1": _s(GW, B16), "ab": _s(GW, B16), "inc": _s(GW), "yg": _s(GW), "e16": _s(16),
+    "idx": _s(4, U16), "tu": _s(160), "pww": _s(C),
+    "gt": _s(GT), "rj": _s(RJ + 2 * DN * GT), "rs2": _s(GT, B16), "dec": _s(72),
+    "gd": _s(176), "lo": _s(8, U16), "dl": _s(80), "dlo": _s(2, U16),
+    "ee": _s(60), "lab": _s(100), "pib": _s(20, B16),
+    "crp": _s(R * 64 + 16, B16), "cg": _s(C, B16), "cw": _s(15 * C + 96, B16), "val": _s(C), "vw": _s(15 * C + 192),
+    "d1": _s(GW, B16), "v1": _s(GW, B16), "ab": _s(GW, B16), "inc": _s(GW), "yg": _s(GW),
     "wg": _s(GW, B16), "wr": _s(GW, B16), "rr": _s(GW, B16),
-    "vo": _s(20, U16), "do": _s(20, U16), "ow": _s(OW), "slw": _s(C), "ao": _s(24, U16), "oww": _s(C), "xo": _s(80, U16),
-    "mr": _s(C), "mww": _s(C), "pib": _s(20, B16), "po": _s(20, U16),
-    "es": _s(64), "sc": _s(4), "mz": _s(P), "yb": _s(C),
+    "vo": _s(20, U16), "do": _s(20, U16), "ow": _s(OW), "slw": _s(OW), "oww": _s(C), "xo": _s(20, U16),
+    "mr": _s(C), "fw": _s(2 * OW), "po": _s(20, U16),
+    "sc": _s(4), "yb": _s(C),
 }
 for _t in range(R):
     SCRATCH["qx%d" % _t] = _s(C, Q4)
     SCRATCH["sx%d" % _t] = _s(C, U8)
     SCRATCH["ql%d" % _t] = _s(C, Q4)
     SCRATCH["sl%d" % _t] = _s(C, U8)
-    SCRATCH["lm%d" % _t] = _s(8, U16)
-    SCRATCH["lp%d" % _t] = _s(8, U16)
-SEMAPHORES = (["sent", "arr0", "arr1", "arr2", "lis0", "lis1", "lis2"] + ["d%d" % i for i in range(24)]
+    SCRATCH["lm%d" % _t] = _s(32, U16)
+    SCRATCH["lp%d" % _t] = _s(24, U16)
+SEMAPHORES = (["sent", "ara0", "ara1", "ara2", "arb0", "arb1", "arb2", "lis0", "lis1", "lis2"] + ["d%d" % i for i in range(24)]
               + [e + str(i) for e in LANES for i in range(LANES[e])])
 ORDER = {}
 
@@ -91,45 +97,30 @@ def depends(ops):
     return deps
 
 
+def price(c, case):
+    return case[5] * (c.real + CYC * (c.imag * case[6] if c.imag > 0 else -c.imag * case[7]))
+
+
 def arrange(ops, deps):
     n = len(ops)
     if n in ORDER: return ORDER[n]
+    K = range(len(CASES))
     eng = ["vspgy".index(o[0]) for o in ops]
     deps = [sorted(d) for d in deps]
     users = [[] for o in ops]
     for i in range(n):
         for d in deps[i]: users[d].append(i)
-    costs = [[call if o[4] in "rR" else o[5] * (f if o[4] == "c" else 1.0) for o in ops] for wake, near, far, wide, call, f in CASES]
+    cost = [[k[4] if o[4] in "rR" else price(o[5], k) * (k[8] if o[0] == "p" else 1.0) if o[4] == "c" else o[5] for o in ops] for k in CASES]
+    late = [[{"d": k[1], "r": k[2], "R": k[3], "w": -k[0]}.get(o[4], 0.0) + k[0] + o[7] for o in ops] for k in CASES]
     form = [0] * n
 
     def choose(c, k):
         form[c], eng[c] = k, "vspgy".index(ops[c][6][k][0])
-        for i in range(len(CASES)): costs[i][c] = ops[c][6][k][2] * CASES[i][5]
-
-    lates = [[{"d": near, "r": far, "R": wide, "w": -wake}.get(o[4], 0.0) + wake for o in ops] for wake, near, far, wide, call, f in CASES]
-
-    def play(order, k):
-        cost, late = costs[k], lates[k]
-        free, last, fin, start, held = [0.0] * 5, [-1] * 5, [0.0] * n, [0.0] * n, [-1] * n
-        for c in order:
-            e = eng[c]
-            s, h = free[e], last[e]
-            for d in deps[c]:
-                if fin[d] > s: s, h = fin[d], d
-            start[c], held[c] = s, h
-            s += cost[c]
-            free[e], last[e], fin[c] = s, c, s + late[c]
-        return max(fin), start, held, fin
-
-    def value(order, most=1e9):
-        r = [play(order, 0)]
-        if r[0][0] > most: return 1e9, r
-        r += [play(order, k) for k in range(1, len(CASES))]
-        return sum(a[0] for a in r) + sum(r[0][3]) / n, r
+        for i in K: cost[i][c] = price(ops[c][6][k][2], CASES[i])
 
     way = [0.0] * n
     for i in range(n - 1, -1, -1):
-        way[i] = costs[0][i] + lates[0][i] + max([way[u] for u in users[i]] + [0.0])
+        way[i] = cost[0][i] + late[0][i] + max([way[u] for u in users[i]] + [0.0])
     left, ready, free, order = [len(d) for d in deps], [0.0] * n, [0.0] * 5, []
     pool = [i for i in range(n) if not left[i]]
     while pool:
@@ -137,67 +128,144 @@ def arrange(ops, deps):
         c = max((i for i in pool if max(ready[i], free[eng[i]]) <= t + 0.1), key=lambda i: way[i])
         pool.remove(c)
         order.append(c)
-        free[eng[c]] = max(ready[c], free[eng[c]]) + costs[0][c]
+        free[eng[c]] = max(ready[c], free[eng[c]]) + cost[0][c]
         for u in users[c]:
-            ready[u] = max(ready[u], free[eng[c]] + lates[0][c])
+            ready[u] = max(ready[u], free[eng[c]] + late[0][c])
             left[u] -= 1
             if not left[u]: pool.append(u)
+
+    fin, tail = [[0.0] * n for k in K], [[0.0] * n for k in K]
+    head, rest = [[[0.0] * 5] * (n + 1) for k in K], [[[0.0] * 5] * (n + 1) for k in K]
+    pos = [0] * n
+
+    def renew(a, b, w0, w1):
+        for i in range(a, b + 1): pos[order[i]] = i
+        for k in K:
+            co, la, f, h = cost[k], late[k], fin[k], head[k]
+            q = h[a]
+            for i in range(a, w1 + 1):
+                c = order[i]
+                e = eng[c]
+                s = q[e]
+                for d in deps[c]:
+                    if f[d] > s: s = f[d]
+                q = q[:]
+                q[e] = s = s + co[c]
+                f[c], h[i + 1] = s + la[c], q
+            f, h = tail[k], rest[k]
+            q = h[b + 1]
+            for i in range(b, w0 - 1, -1):
+                c = order[i]
+                e = eng[c]
+                s = 0.0
+                for u in users[c]:
+                    if f[u] > s: s = f[u]
+                s += la[c]
+                if q[e] > s: s = q[e]
+                q = q[:]
+                q[e] = f[c] = s + co[c]
+                h[i] = q
+
+    def through(a, b, part, ends, room):
+        worse = 0.0
+        for k in K:
+            co, la, f, t, q = cost[k], late[k], fin[k], tail[k], head[k][a][:]
+            old = max(max([f[c] - la[c] - co[c] + t[c] for c in part]), max([x + y for x, y in zip(q, rest[k][b + 1])]))
+            new, most = {}, 0.0
+            for c in part:
+                e = eng[c]
+                s = q[e]
+                for d in deps[c]:
+                    v = new.get(d) or f[d]
+                    if v > s: s = v
+                q[e] = s = s + co[c]
+                new[c] = s = s + la[c]
+                if s > most: most = s
+                for u in users[c]:
+                    if pos[u] > b and s + t[u] > most: most = s + t[u]
+            for x, y in zip(q, rest[k][b + 1]):
+                if x + y > most: most = x + y
+            worse += most - old + max(most - ends[k], 0.0)
+            if worse > room + SLACK * (len(K) - 1 - k): break
+        return worse
+
+    def longest(w0, w1):
+        return [max(fin[k][c] - late[k][c] - cost[k][c] + tail[k][c] for c in order[w0:w1 + 1]) for k in K]
+
+    def tidy(w0, w1):
+        f, la, co = fin[0], late[0], cost[0]
+        order[w0:w1 + 1] = sorted(order[w0:w1 + 1], key=lambda x: f[x] - la[x] - co[x] + 1e-9 * pos[x])
+        renew(w0, w1, w0, w1)
+
     rng = np.random.RandomState(1)
-    now, runs = value(order)
-    best, kept = now, (order, list(form))
-    pos = {c: i for i, c in enumerate(order)}
-    free_ = [i for i in range(n) if len(ops[i][6]) > 1]
-    for step in range(TRIES):
-        end, start, held, fin = runs[step // 4 % len(CASES)]
-        back = None
-        if step % 4 == 3:
-            c = free_[rng.randint(len(free_))]
-            back, new = (c, form[c]), order
-            choose(c, (form[c] + 1 + rng.randint(len(ops[c][6]) - 1)) % len(ops[c][6]))
-        elif step % 4:
-            c, path = fin.index(end), []
-            while c >= 0:
-                if held[c] >= 0 and held[c] not in deps[c]: path.append(c)
-                c = held[c]
-            if not path: continue
-            c = path[rng.randint(len(path))]
-            p = held[c]
-            if len(ops[p][6]) > 1 and rng.rand() < 0.3:
-                back, new = (p, form[p]), order
-                choose(p, (form[p] + 1 + rng.randint(len(ops[p][6]) - 1)) % len(ops[p][6]))
-            elif rng.rand() < 0.5:
-                lo = max([pos[d] for d in deps[c]] + [-1]) + 1
-                if lo > pos[p]: continue
-                mates = [i for i in range(lo, pos[p] + 1) if eng[order[i]] == eng[c]][-4:]
-                to = mates[rng.randint(len(mates))]
-                new = order[:to] + [c] + order[to:pos[c]] + order[pos[c] + 1:]
+
+    def improve(w0, w1, tries):
+        ends, m = longest(w0, w1), w1 - w0 + 1
+        best, kept = sum(ends), (order[w0:w1 + 1], list(form))
+        for step, (r0, r1, r2, r3, r4) in enumerate(rng.rand(tries, 5).tolist()):
+            x0 = int(r0 * m)
+            c = order[w0 + x0]
+            ahead, behind = AIM / 2 <= r1 < AIM, r1 < AIM / 2
+            if ahead or behind:
+                k = step % len(CASES)
+                f, la, co, t, e = fin[k], late[k], cost[k], tail[k], ends[k] - NEAR
+                for x in range(x0, x0 + 60):
+                    x = w0 + x % m
+                    c = order[x]
+                    s = f[c] - la[c] - co[c]
+                    if s + t[c] >= e and s - head[k][x][eng[c]] < 1e-9 and all(f[d] < s - 1e-9 for d in deps[c]): break
+                else: continue
+                if behind:
+                    x -= 1
+                    while x >= w0 and eng[order[x]] != eng[c]: x -= 1
+                    if x < w0: continue
+                    c = order[x]
+            i, was, many = pos[c], form[c], len(ops[c][6])
+            lo, hi = max([pos[d] + 1 for d in deps[c]] + [w0, i - REACH]), min([pos[u] - 1 for u in users[c]] + [w1, i + REACH])
+            swap = many > 1 and r3 < SW
+            if swap: j = min(hi, max(lo, i + int(r2 * 9) - 4))
             else:
-                hi = min([pos[u] for u in users[p]] + [n])
-                if hi <= pos[c]: continue
-                mates = [i for i in range(pos[c], hi) if eng[order[i]] == eng[c]][:6]
-                to = mates[rng.randint(len(mates))]
-                new = order[:pos[p]] + order[pos[p] + 1:to + 1] + [p] + order[to + 1:]
-        else:
-            c = rng.randint(n)
-            lo, hi = max([pos[d] for d in deps[c]] + [-1]) + 1, min([pos[u] for u in users[c]] + [n])
-            to = rng.randint(max(lo, pos[c] - 30), min(hi, pos[c] + 30))
-            new = order[:pos[c]] + order[pos[c] + 1:]
-            new.insert(to, c)
-        v, r = value(new, runs[0][0] + 0.25)
-        if v <= now + 0.25 * (1 - step / TRIES) * rng.rand():
-            order = sorted(new, key=lambda i: r[0][1][i])
-            pos = {c: i for i, c in enumerate(order)}
-            now, runs = v, r
-            if v < best: best, kept = v, (order, list(form))
-        elif back: choose(*back)
-    ORDER[n] = [int(c) for c in kept[0]], kept[1]
+                mates = [x for x in range(i if behind else lo, (i if ahead else hi) + 1) if eng[order[x]] == eng[c] and x != i]
+                if not mates: continue
+                if ahead or behind: mates = mates[:6] if behind else mates[-6:]
+                j = mates[int(r2 * len(mates))]
+            a, b = min(i, j), max(i, j)
+            if swap:
+                start = [fin[k][c] - cost[k][c] + tail[k][c] for k in K]
+                choose(c, (was + 1 + step % (many - 1)) % many)
+                keep = [tail[k][c] for k in K]
+                for k in K: tail[k][c] = start[k] - fin[k][c] + cost[k][c]
+            part = [c] + order[a:b] if j < i else order[a + 1:b + 1] + [c]
+            room = HEAT * (1 - step / tries) * r4
+            worse = through(a, b, part, ends, room)
+            if swap:
+                for k in K: tail[k][c] = keep[k]
+            if worse <= room:
+                order[a:b + 1] = part
+                renew(a, b, w0, w1)
+                if step % 12 == 0: tidy(w0, w1)
+                ends = longest(w0, w1)
+                if sum(ends) < best - 1e-9: best, kept = sum(ends), (order[w0:w1 + 1], list(form))
+            elif swap: choose(c, was)
+        order[w0:w1 + 1] = kept[0]
+        for c in kept[0]:
+            if form[c] != kept[1][c]: choose(c, kept[1][c])
+        renew(0, n - 1, 0, n - 1)
+        tidy(0, n - 1)
+
+    renew(0, n - 1, 0, n - 1)
+    improve(0, n - 1, FIRST)
+    for turn in range(TRIES // SPELL):
+        w0 = rng.randint(-SPAN // 2, n - SPAN // 2)
+        improve(max(w0, 0), min(w0 + SPAN, n - 1), SPELL)
+    ORDER[n] = order, form
     return ORDER[n]
 
 
 def settle(ops):
     deps = depends(ops)
     order, form = arrange(ops, deps)
-    return [(o[6][k][0], o[6][k][1], o[2], o[3], o[4], o[6][k][2]) for o, k in zip(ops, form)], deps, order
+    return [(o[6][k][0], o[6][k][1], o[2], o[3], o[4], o[6][k][2], o[7]) for o, k in zip(ops, form)], deps, order
 
 
 def emit(ops, g, T):
@@ -214,7 +282,7 @@ def emit(ops, g, T):
         known[e] |= after[d]
 
     for n in order:
-        e, fn, rd, wr, kind, cost = ops[n]
+        e, fn, rd, wr, kind = ops[n][:5]
         place[n] = len(place)
         for d in sorted(deps[n], key=lambda d: -place[d]):
             if ops[d][4] not in "rR" and not known[e] >> d & 1: wait(e, d)
@@ -258,14 +326,14 @@ def rank_program(g, core, T, topo):
     ops = []
     nsent = [0]
 
-    def add(e, fn, rd, wr, cost, kind="c", more=()):
-        ops.append((e, fn, rd.split(), wr.split(), kind, cost, [(e, fn, cost)] + list(more)))
+    def add(e, fn, rd, wr, cost, kind="c", more=(), slow=0.0):
+        ops.append((e, fn, rd.split(), wr.split(), kind, cost, [(e, fn, cost)] + list(more), slow))
 
     def cy(n): return max(64, n) * CYC
 
-    def ga(n): return 0.05 + n * GATHER * CYC
+    def ga(n): return 0.055 + n * 1j
 
-    def sca(n): return 0.05 + n * SCATTER * CYC
+    def sca(n): return 0.05 - n * 1j
 
     def ts(out, in0, s1, o0, s2, o1, rd, wr, c=0.067):
         if o1 is None: add("v", lambda: V.tensor_scalar(out, in0, s1, None, o0), rd, wr, c)
@@ -281,16 +349,16 @@ def rank_program(g, core, T, topo):
         add("v", lambda: V.tensor_tensor_scan(out, d0, d1, init, o0, o1), rd, wr, c)
 
     def fill(ap, v, wr, n, half=False):
-        more = [("s", lambda: S.activation(ap, T.ones[:, 0:n], Act.Copy, scale=float(v)), cy(n))]
+        more = [("s", lambda: S.activation(ap, T.ones[:, 0:n], Act.Copy, scale=float(v)), cy(n))] if n <= 256 else []
         if v == int(v) and abs(v) < 2 ** 24:
             more.append(("g", lambda: g.iota(ap, [[0, n]], int(v), 0, allow_small_or_imprecise_dtypes=True), 0.13 + 2 * n * CYC))
-        add("v", lambda: V.memset(ap, v), "ones", wr, cy(n // 2 if half else n), more=more)
+        add("v", lambda: V.memset(ap, v), "ones" if n <= 256 else "", wr, cy(n // 2 if half else n), more=more)
 
     def act(out, a, rd, wr, scale=1.0, bias=None, c=0.067, f=None, cv=None):
         if f: return add("s", lambda: S.activation(out, a, f, bias=bias, scale=scale), rd, wr, c)
         if bias is None:
             other = (lambda: V.tensor_copy(out, a)) if scale == 1.0 else (lambda: V.tensor_scalar(out, a, scale, None, Op.mult))
-            add("s", lambda: S.activation(out, a, Act.Copy, scale=scale), rd, wr, c, more=[("v", other, cv or c)])
+            add("s", lambda: S.activation(out, a, Act.Copy, scale=scale), rd, wr, c, more=[] if wr[:3] in LONG else [("v", other, cv or c)])
         else:
             add("s", lambda: S.activation(out, a, Act.Identity, bias=bias, scale=scale), rd, wr, c,
                 more=[("v", lambda: V.tensor_scalar(out, a, scale, bias, Op.mult, Op.add), cv or c)])
@@ -307,17 +375,21 @@ def rank_program(g, core, T, topo):
         if flt: add("g", lambda: g.iota(out, pat, base, cm, allow_small_or_imprecise_dtypes=True), "", wr, 0.13 + 2 * n * CYC)
         else: add("g", lambda: g.iota(out, pat, base, cm), "", wr, 0.13 + 2 * n * CYC)
 
-    def dma(e, out, a, rd, wr):
+    def dma(e, out, a, rd, wr, slow=0.0):
         q = {"y": g.sync, "s": S, "g": g}[e]
-        add(e, lambda: q.dma_start(out, a), rd, wr, 0.1, "d")
+        add(e, lambda: q.dma_start(out, a), rd, wr, 0.1, "d", slow=slow)
 
     def send(dst, src, arr, t, rd, wr, kind):
         mate = T.cores[rank ^ STEP[t]]
         rid, pid = topo.addr(mate)[0:2]
-        add("g", lambda: g.remote_dma(dst, src, arr, T.sem.sent, pid, rid, topo.mask(core, mate)), rd, wr, CALL, kind)
+        add("g", lambda: g.remote_dma(dst, src, arr, T.sem.sent, pid, rid, topo.mask(core, mate)), rd, wr, CALL, kind,
+            slow=(wr != "r3") * (SLOW[0] * (t == 0) + SLOW[2] * (topo.die(T.cores[0]) != topo.die(T.cores[STEP[t]])) + SLOW[3 + (kind == "R")]))
         k = len(topo.engines(core, mate))
         nsent[0] += k
         return k
+
+    def plus(out, a, b, o, rd, wr):
+        scan(out, a, b, -BIG, Op.max, o, rd, wr)
 
     def pick(out, pat, src, rd, wr, c):
         scan(out, pat, src, 0.0, Op.add, Op.min, rd, wr, c)
@@ -326,287 +398,312 @@ def rank_program(g, core, T, topo):
         if not (flip and on): return buf[:, a:a + n]
         return buf[:, a + n - 1:a - 1:-1] if a else buf[:, n - 1::-1]
 
+    def xkeys(t, a, b):
+        if t == 0: return "x0a " * (a < QH) + "x0b " * (b > QH)
+        return " ".join("x%d_%d" % (t, k) for k, (p, lo, hi) in enumerate(XP) if lo < b and a < hi)
+
     X = [T.x0, T.x1, T.x2, T.x3]
     col = T.col
-    ci, cm, cr, ct, c16, c4, csp, c36, c16m, c4a, cq, cs, cf0, cf1, cl, ck = (col[:, k:k + 1] for k in range(16))
-    e3, e6, ra = (T.n20[:, 24 * k:24 * k + 20] for k in range(len(N20)))
-    hh, lt, gg, ea, n32, emp, mask0 = (T.n48[:, P * k:P * k + P] for k in range(len(N48)))
-    UB, VQ, GD = 104, 208, 16
-    gd = T.pa[:, GD:GD + P]
-    mv, lap, k2, pit, e2 = T.cw[:, 45:3 * C:48], T.cw[:, 29:3 * C:48], T.ea0[:, 1:60:3], T.ea0[:, 2:60:3], T.ee[:, 2:60:3]
-    e4, kk, zz = T.lb1[:, 2:80:4], T.lab[:, 2:80:4], T.lab[:, 3:80:4]
+    ci, cm, c16, csp, c36, cq, c63 = (col[:, k:k + 1] for k in range(7))
+    e3, e6 = (T.n20[:, 24 * k:24 * k + 20] for k in range(len(N20)))
+    hh, lt, vq, ea, r16, iom = (T.n48[:, P * k:P * k + P] for k in range(len(N48)))
+    es = T.t1[:, 3 * TS:3 * TS + P]
+    UB = 104
+    gd = T.gd[:, 0:GT:3]
+
+    def slot(buf, a, step=240, h=0, n=20): return buf[:, a + 2400 * h:a + 2400 * h + 240 * n - step + 1:step]
+
+    mv, lap = slot(T.cw, 225), slot(T.cw, 145)
+    ra, vw, e4, np_, k2 = (slot(T.vw, a) for a in (177, 225, 321, 369, 289))
+    nk, nz = T.lab[:, 3:100:5], T.lab[:, 4:100:5]
+    e2 = T.ee[:, 2:60:3]
     HID, T1S, T1A = DW, DW + R * NT + P, FL - 32
-    zero = T.tm[:, T1S - P:T1S]
     qd, mask, hs = (T.tm[:, T1S + 80 + P * k:T1S + 80 + P * k + P] for k in range(3))
     tmk = "tm tm2 hid zero t1s1 t1s2 qd mask hs t1a t1b idx"
 
     dma("y", T.szb[:, 0:3], T.sz[:], "", "szb")
-    dma("s", T.ub[:], T.u[:], "", "ub")
-    dma("y", T.x0[:, 0:4 * HALF], T.x[:, 0:4 * HALF], "", "x0a x0b")
-    dma("s", T.x0[:, 4 * HALF:4 * C], T.x[:, 4 * HALF:4 * C], "", "x0c x0d")
-    dma("y", T.qw[:].bitcast(dt.uint8), T.wc[:], "", "qw")
-    dma("y", T.sw[:], T.ws[:], "", "sw")
-    dma("y", T.vb[:], T.v[:], "", "vb")
+    dma("s", T.ub[:], T.u[:], "", "ub", SLOW[1] * 0.45)
+    dma("y", T.x0[:, 0:4 * QH], T.x[:, 0:4 * QH], "", "x0a", SLOW[1] * 0.8)
+    dma("s", T.x0[:, 4 * QH:4 * C], T.x[:, 4 * QH:4 * C], "", "x0b", SLOW[1])
 
-    add("v", lambda: V.memset(T.ones[:], 1.0), "", "ones", cy(264))
+    add("v", lambda: V.memset(T.ones[:], 1.0), "", "ones", cy(128))
     iota(T.ip[:, 0:2], [[15, 2]], 0, 1, "ip", False)
     iota(T.tm[:, 0:DW], [[1, DW]], 0, 0, "tm")
     iota(T.j20[:], [[16, 20]], 0, 0, "j20")
     iota(T.jm[:, 0:NT], [[0, NT // 16], [1, 16]], 0, 0, "jm")
-    iota(T.j4[:], [[0, C // 4], [1, 4]], 0, 0, "j4")
     if flip: iota(qd, [[-1, 12], [0, 4]], 11, 0, "qd")
     else: iota(qd, [[1, 12], [0, 4]], 0, 0, "qd")
     iota(T.tm[:, HID:HID + R * NT], [[1, R * NT]], C, 0, "hid")
-    iota(hs, [[int(KEY), P]], int(KEY), 0, "hs")
-    fill(T.ow[:], 1000.0, "ow", OW)
-    fill(T.th[:], NONE, "th", 3 * TS)
-    add("g", lambda: g.affine_select(T.eye[:], T.ones[:], [[1, 528]], Op.is_equal, 0.0, -3, -4), "ones", "eye", 1.27)
+    iota(hs, [[int(KEY), P]], int(KEY + HC), 0, "hs")
+    iota(T.dl[:, 0:36], [[1, 6], [DN, 6]], 6, 0, "dl")
+    fill(T.ow[:, 0:C + 1], -BIG, "ow", C + 1)
+    for t in ANEW[1:]: fill(T.fw[:, OW * (t - 1):OW * (t - 1) + C + 1], -BIG, "fw%d" % t, C + 1)
+    fill(T.th[:], NONE - 100 - HC, "th", 3 * TS)
+    for h in range(2): fill(T.eye[:, 256 * h:256 * h + 256], 0.0, "ey%d" % h, 256, True)
+    fill(T.eye[:, 512:528], 0.0, "ey2", 16)
+    add("g", lambda: g.affine_select(T.eye[:, 3:515:4], T.ones[:, 0:128], [[1, 128]], Op.is_equal, 0.0, 0, -1), "ones ey0 ey1 ey2", "eye", 0.17 + 256 * CYC)
     add("g", lambda: g.affine_select(T.r12[:], T.ones[:, 0:GW], [[0, 20], [1, M]], Op.not_equal, 0.0, 0, 0), "ones", "r12", 0.67)
-    fill(T.tu[:, 0:VQ + 1:UB], 0.0, "enz", 3)
     fill(T.sw_[:, C + 1:376], -1e29, "swz", 375 - C)
     fill(T.sw_[:, 0:1], -1e29, "swy", 1)
     fill(T.rs2[:], 0.0, "rs2", GT, True)
-    fill(T.rs2[:, 0:GT:P], -4 * BIG, "rs2", 3)
-    fill(T.es[:, P:64], 192.49, "esz", 16)
+    fill(T.rs2[:, 0:GT:P], -2 * BIG, "rs2", 3)
+    fill(T.t1[:, 3 * TS + P:4 * TS], 192.49, "esz", 4)
     fill(T.tm[:, T1S - P:T1S + 32], 0.0, "zero", 80)
     fill(T.tm[:, T1S + P:T1S + 80], -1.0, "t1s2", 32)
-    fill(T.cw[:, 13:3 * C:48], 0.0, "cw", 20)
-    fill(T.ea0[:, 0:60:3], -48.0 / MV, "ea0", 20)
-    fill(T.la[:], 1.0, "la", 80)
-    fill(T.la[:, 0:80:4], 0.0, "la", 20)
-    fill(T.pa[:], BIG, "pa", 64)
-    fill(T.rj[:, RJ + 5 - P:RJ + 6 + 28 * P:P], 1.0, "rj0 rj1 rk0 rk1", 30)
-    for k, (a, v) in enumerate(((5 - P, 0.0), (5 + 3 * P, -1.0), (-4 * P, 1.0), (-3 * P, -161.0), (-2 * P, R512), (-P, -R512))):
-        fill(T.rj[:, RJ + a:RJ + a + 25 * P + 1:5 * P], v, "rk%d" % k, 6)
+    for k, (a, v) in enumerate(((65, 0.0), (81, 0.0), (129, -1.0), (177, 1.0), (273, 1.0))): fill(slot(T.cw, a), v, "cz%d" % k, 20)
+    fill(slot(T.vw, 209), 48.0 / MV, "ea0", 20)
+    fill(slot(T.vw, 273), -MID, "l1", 20)
+    fill(T.gd[:, 0:GT + 27:3], BIG, "gd", P + 9)
+    r0, r1, per = RJ + DN - P, RJ - 4 * P, DN * P
+    fill(T.rj[:, r0:r0 + 6 * per - P + 1:P], 1.0, "rj0 rj1 rk0 rk1 rk2", 6 * DN)
+    fill(T.rj[:, r1:r1 + 6 * per - P + 1:P], 1.0, "rj0 rj1 rk3 rk4 rk5 rk6 rk7 rk8", 6 * DN)
+    for k, (a, v) in enumerate(((r0, 0.0), (r0 + 4 * P, -1.0), (r0 + 7 * P, 4.0), (r1 + P, -209.0),
+                                (r1 + 2 * P, R512), (r1 + 3 * P, -R512), (r1 + 5 * P, RND), (r1 + 6 * P, -RND), (r1 + 7 * P, -4.0))):
+        fill(T.rj[:, a:a + 5 * per + 1:per], v, "rk%d" % k, 6)
     for k, v in enumerate((0.0, 900.0, -1.0, BIG)): fill(T.t1[:, P + k:3 * TS:TS], v, "t1s%d" % (k + 3), 3)
     fill(T.d1[:], -1.0, "d1", GW, True)
     for t in range(R): fill(X[t][:, 4 * C:4 * HB], 0.0, "x%dz" % t, 16)
-    fill(T.dd[:, C:4 * DW:DW], 0.0, "ddz", 4)
-    fill(T.tb[:, 4 * NT:512], 0.0, "tbz", 128, True)
-    dma("y", T.tm[:, FL:FL + DW], T.tm[:, 0:DW], "tm", "tm2")
-    for k in range(4):
-        act(T.pool[:, C * k:C * k + C], T.x0[:, C * k:C * k + C], "x0a x0b" if k < 2 else "x0c x0d", "p%d" % k, 64.0, c=cy(C), cv=cy(C // 2))
+    fill(T.dd[:, 4 * C:4 * HB], 0.0, "ddz", 16)
+    iota(T.odd[:], [[0, NT], [1, 2]], 0, 0, "odd")
+    add("g", lambda: g.iota(T.tm[:, FL:FL + DW], [[1, DW]], 0, 0, allow_small_or_imprecise_dtypes=True), "tm", "tm2", 0.13 + 2 * DW * CYC,
+        more=[("s", lambda: S.activation(T.tm[:, FL:FL + DW], T.tm[:, 0:DW], Act.Copy), cy(DW)),
+              ("v", lambda: V.tensor_copy(T.tm[:, FL:FL + DW], T.tm[:, 0:DW]), cy(DW))])
+    for b in range(4):
+        act(T.pool[:, PW * b:PW * b + C], T.x0[:, b:4 * C:4], xkeys(0, 0, C), "p%d" % b, 64.0, c=cy(C), cv=cy(C // 2))
     ts(T.ip[:, 2:4], T.ip[:, 0:2], 15, Op.bitwise_and, None, None, "ip", "ip1")
-    ts(T.ip[:, 4:5], T.ip[:, 0:1], 2, Op.arith_shift_right, 3, Op.bitwise_and, "ip", "ip2")
-    ts(T.ip[:, 5:6], T.ip[:, 0:1], 3, Op.bitwise_and, None, None, "ip", "ip3")
     cp(col[:, 0:2], T.ip[:, 2:4], "ip1", "ci")
-    cp(col[:, 2:4], T.ip[:, 4:6], "ip2 ip3", "cr")
-    for k, nm, a, b in ((c16, "c16", -OFF, 15 * OFF), (c16m, "c16m", -OFF, 15 * OFF - 1),
-                        (cs, "cs", OFF, FL - 1 - 15 * OFF), (cf0, "cf0", 4096 * OFF, 2048 - 4096 * 15 * OFF),
-                        (cf1, "cf1", 4096 * OFF, 6144 - 4096 * 15 * OFF),
-                        (cq, "cq", sg, 15.0 * flip),
-                        (cl, "cl", -OFF / 16, 15 * OFF / 16 + 192 - 0.31), (ck, "ck", 32 * OFF, -32 * 15 * OFF)):
-        act(k, ci, "ci", nm, a, b)
-    act(c4a, cr, "cr", "c4a", -4 * OFF, 12 * OFF)
-    act(c4, ct, "cr c4a", "c4", 1.0, c4a)
+    act(c16, ci, "ci", "c16", -OFF, 15 * OFF)
+    act(cq, ci, "ci", "cq", sg, 15.0 * flip)
+    act(c63, ci, "ci", "c63", -OFF * 63 / 64, 15 * OFF * 63 / 64)
     act(c36, cm, "ci", "c36", 1.0, 36.0)
     ts(csp, cm, 12.0, Op.is_ge, c36, Op.mult, "ci c36", "csp")
     ts(T.jm[:, 0:NT], T.jm[:, 0:NT], ci, Op.is_equal, BIG, Op.mult, "jm ci", "jm")
     act(T.wpa[:, 0:NT], T.jm[:, 0:NT], "jm", "wpa", 1.0, -OFF, cy(NT), cv=cy(64))
     act(T.wpa[:, NT:2 * NT], T.wpa[:, 0:NT], "wpa", "wpb", c=cy(NT), cv=cy(64))
     act(T.wpa[:, 2 * NT:C], T.wpa[:, 0:C - 2 * NT], "wpa wpb", "wpc", c=cy(128), cv=cy(64))
-    ts(T.j4[:], T.j4[:], cr, Op.is_equal, BIG, Op.mult, "j4 cr", "j4", cy(C // 2))
-    act(T.wp4[:], T.j4[:], "j4", "wp4", 1.0, -OFF, cy(C), cv=cy(C // 2))
     ts(T.tm[:, T1A:T1A + 16], T.tm[:, 0:16], cq, Op.is_equal, 4097.0, Op.mult, "tm cq", "t1a")
     ts(T.tm[:, T1A + 16:FL], T.tm[:, 0:16], cq, Op.is_ge, None, None, "tm cq", "t1b")
     tt(T.tm[:, T1S + 32:T1S + P], T.tm[:, T1A:T1A + 16], T.tm[:, T1A + 16:FL], Op.subtract, "t1a t1b", "t1s1")
     cp(T.upk[:], T.j20[:, 0:8], "j20", "upk")
     act(T.crp[:, 0:R * 64], T.ones[:, 0:R * 64], "ones c16", "crp0 crp1 crp2", 0.0, c16, cy(R * 64), cv=cy(R * 32))
     act(T.crp[:, R * 64:R * 64 + 16], T.ones[:, 0:16], "ones c16", "crs", MV, c16)
+    act(T.tu[:, 0:1], c16, "c16", "enz")
+    act(T.tu[:, UB:UB + 1], c16, "c16", "ubz", 1.0, -MID)
+    act(r16, T.ones[:, 0:P], "ones c16", "r16", 0.0, c16)
+    act(iom, T.tm[:, DW - 1:DW - 1 - P:-1], "tm c16", "iom", 1.0, c16)
     act(T.base[:], T.j20[:, 0:4], "j20 csp", "base", TS / 16, csp)
     act(T.jw[:], T.j20[:], "j20 ci", "jw", 1.0, ci)
-    act(T.pb[:, 1:12:2], T.jw[:, 0:6], "jw", "dum", 1.0, C + 1.0)
-    act(T.qc[:, 0:3], T.jw[:, 0:3], "jw", "qc", sg * KEY, 513 + 47 * KEY * flip - 192 * LAP)
+    for k in range(2): act(T.th[:, P + k:3 * TS:TS], T.jw[:, 0:3], "jw th", "thz%d" % k, 1.0, NONE + P * k - HC)
+    add("g", lambda: g.iota(T.slw[:, 1:C + 1], [[1, C]], 0, 0, allow_small_or_imprecise_dtypes=True), "tm", "slw", 0.13 + 2 * C * CYC,
+        more=[("s", lambda: S.activation(T.slw[:, 1:C + 1], T.tm[:, 0:C], Act.Copy), cy(C)),
+              ("v", lambda: V.tensor_copy(T.slw[:, 1:C + 1], T.tm[:, 0:C]), cy(C))])
+    act(T.qc[:, 0:3], T.jw[:, 0:3], "jw c16", "qc", -sg * KEY, c16)
+    act(T.qc[:, 0:3], T.qc[:, 0:3], "qc", "qc", -1.0, 513 + 47 * KEY * flip - 192 * LAP)
     act(T.qc[:, 4:7], T.jw[:, 0:3], "jw", "zq", -sg / 48, -47.0 * flip / 48)
+    pick(T.dl[:, P:80], T.wpa[:, 0:32], T.dl[:, 0:32], "wpa dl", "dl2", 0.067)
+    ts(T.dlo[:], T.dl[:, P + 15:80:16], c16, Op.add, None, None, "dl2 c16", "dlo")
     quant(T.qu0[:], T.su0[:], T.ub[:], "ub", "qu0")
     add("s", lambda: S.activation(T.su[:], T.su0[:].indirect(T.upk[:]), Act.Copy), "qu0 upk", "su", ga(128))
     cp(T.qu[:].bitcast(dt.uint32), T.qu0[:].bitcast(dt.uint32).indirect(T.upk[:]), "qu0 upk", "qu", ga(128))
-    ts(mask, qd, cm, Op.is_equal, 3e29, Op.mult, "qd ci", "mask")
-    act(mask, mask, "mask", "mask", 1.0, -2e29)
+    ts(mask, qd, cm, Op.not_equal, -2e29, Op.mult, "qd ci", "mask")
     for b in range(4):
         quant(T.qe[:, 128 * b:128 * b + 128], T.se[:, 128 * b:128 * b + 128], T.eye[:, 3 - b:515 - b], "eye", "qe%d" % b)
-    quant(T.qv[:], T.sv[:], T.vb[:], "vb", "qv")
     cp(T.idx[:, 0:3], T.szb[:, 0:3], "szb", "idx")
 
     idx = T.idx[:, 0:3]
     un = T.tu[:, P + 1:2 * P + 1]
-    pe, pn = ((P + 15, 15) if flip else (15, P + 15))
-    endp, sizp = T.pww[:, pe:pe + 33:16], T.pww[:, pn:pn + 33:16]
+    pe, pn = ((3 * P + 45, 45) if flip else (45, 3 * P + 45))
+    sizp = T.pww[:, pn:pn + 97:48]
+    act(T.pww[:, pe + 16:pe + 113:48], T.jw[:, 0:3], "jw", "dum", 1.0, C + 1.0)
+    act(T.pww[:, pe + 32:pe + 129:48], T.jw[:, 0:3], "jw", "dum2", 1.0, C + 2.0 + P)
 
-    def sizes(first):
-        if first:
-            act(un, T.tm[:, 0:DW].indirect(idx), "tm idx", "un", c=ga(P))
-            scan(T.tu[:, 1:P + 1], un, zero, 0.0, Op.add, Op.add, "un zero", "en")
-            return
-        act(rev(T.tu, P + 1), T.tm[:].indirect(idx), tmk, "un", 1.0 + EPS, c=ga(P))
-        act(rev(T.tu, UB + 1), T.tm[:].indirect(idx), tmk, "ub2", -EPS, c=ga(P))
-        scan(T.tu[:, 1:P + 1], un, T.tu[:, UB:UB + P], 0.0, Op.add, Op.add, "un ub2 enz", "en")
+    def sizes(t):
+        win, wk = (T.tm[:], tmk) if t >= 0 else (T.tm[:, 0:DW], "tm idx")
+        if t + 1 < R and t + 1 not in ANEW:
+            act(rev(T.tu, P + 1), win.indirect(idx), wk + " c16", "un", 1.0 - EPS, c16, ga(P))
+            act(rev(T.tu, UB + 1), win.indirect(idx), wk + " c16", "ub2", -EPS, c16, ga(P))
+            scan(T.tu[:, 1:P + 1], un, T.tu[:, UB:UB + P], c16, Op.add, Op.subtract, "un ub2 ubz c16", "en")
+        else:
+            act(rev(T.tu, P + 1, t >= 0), win.indirect(idx), wk + " c16", "un", 1.0, c16, ga(P))
+            scan(T.tu[:, 1:P + 1], un, r16, c16, Op.add, Op.subtract, "un r16 c16", "en")
 
-    def places():
-        pick(T.pww[:], T.wpa[:, 0:NT], rev(T.tu, 1, n=NT), "wpa en un", "pww", cy(NT))
-        act(T.pb[:, 0:6:2], endp, "pww c16", "en6a", 1.0, c16)
-        act(T.pb[:, 6:12:2], endp, "pww c16m", "en6b", 1.0, c16m)
-        act(T.pa[:, 1:6:2], sizp, "pww cf0 pa", "f6a", -4096.0, cf0, f=Act.Relu)
-        act(T.pa[:, 7:12:2], sizp, "pww cf1 pa", "f6b", -4096.0, cf1, f=Act.Relu)
-        scan(T.l9[:], T.pa[:, 0:12], T.pb[:], 0.0, Op.add, Op.min, "en6a en6b f6a f6b pa dum", "l9")
-        cp(T.lo[:, 0:6], T.l9[:, 1:12:2], "l9", "lo")
+    def places(both):
+        pick(T.pww[:, 0:3 * NT:3], T.wpa[:, 0:NT], rev(T.tu, 1, n=NT), "wpa en un", "pww", cy(NT))
+        for k in range(1 + both):
+            f6 = T.gd[:, GT + 3 + 3 * k:GT + 27:9]
+            add("s", lambda f6=f6, k=k: S.activation(f6, sizp, Act.Relu, bias=2048.0 + 4096 * k, scale=-4096.0), "pww gd", "f6" + "ab"[k], 0.067,
+                more=[("v", lambda f6=f6, k=k: V.tensor_scalar(f6, sizp, 0.5 + k, 2048.0, Op.is_lt, Op.mult), 0.067)])
+        scan(T.gd[:, 26:155:16], T.gd[:, GT:GT + 27:3], T.pww[:, pe:pe + 129:16], 0.0, Op.add, Op.min, "pww f6a f6b dum dum2 gd", "l9")
+        cp(T.lo[:, 0:3], T.gd[:, 42:GT:P], "l9", "lo")
+        if both: ts(T.lo[:, 3:6], T.gd[:, 58:155:P], -1.0, Op.add, None, None, "l9", "lo2")
 
-    def tables():
-        tt(ea, T.tm[:, 0:P], un, Op.add, "tm un", "ea", cy(96))
-        act(T.es[:, 0:P], ea, "ea", "es", 1.0 / 48, 191.5 + 0.3 / 48)
-        act(T.sc[:, 0:3], sizp, "pww cs", "sc", -1.0, cs)
-        act(T.pa[:, GD:GD + P:16], T.sc[:, 0:3], "sc pa", "t1n", -11.0, 2292 - (FL - 1) - GS)
-        tt(hh, T.tu[:, 0:P], hs, Op.subtract, "en enz hs", "hh", cy(96))
+    def tables(e):
+        plus(T.n48[:, 4 * P - 1:3 * P - 1:-1], T.n48[:, 6 * P - 1:5 * P - 1:-1], T.tu[:, 2 * P:P:-1], Op.subtract, "iom un", "ea")
+        act(es, ea, "ea", "es", -1.0 / 48, 191.5 + (DW - 0.18) / 48)
+        act(T.sc[:, 0:3], sizp, "pww", "sc", -e, FL - 1.0)
+        act(T.gd[:, 0:GT:P], sizp, "pww gd", "t1n", 11.0 * e, 2292 - 12 * (FL - 1) - GS)
+        act(T.gd[:, 45:GT:P], sizp, "pww gd", "own1", 4096.0, -6144.0)
+        plus(hh, T.tu[:, 0:P], hs, Op.subtract, "en enz hs", "hh")
         for c in range(3):
             a = T1S + (16 * c if flip else 32 - 16 * c)
             ht, kt, tr = (buf[:, P * c:P * c + P] for buf in (T.ht, T.kt, T.tr))
-            act(ht, T.es[:, 0:P], "es zq", "ht%d" % c, 1.0, T.qc[:, 4 + c:5 + c])
+            act(ht, es, "es zq", "ht%d" % c, 1.0, T.qc[:, 4 + c:5 + c])
             act(kt, ht, "ht%d qc" % c, "kt%d" % c, LAP, T.qc[:, c:c + 1])
-            tt(T.th[:, TS * c:TS * c + P], kt, hh, Op.add, "kt%d hh th" % c, "th%d" % c, cy(96))
+            plus(T.th[:, TS * c:TS * c + P], kt, hh, Op.add, "kt%d hh th" % c, "th%d" % c)
             act(tr, T.tm[:, a:a + P], "sc zero t1s1 t1s2", "tr%d" % c, -1.0, T.sc[:, c:c + 1], f=Act.Relu)
             tt(T.t1[:, TS * c:TS * c + P], tr, ht, Op.subtract, "tr%d ht%d" % (c, c), "t1%d" % c, cy(96))
-        tt(T.pa[:, GD + 14:GD + P:16], T.pb[:, 0:6:2], T.pa[:, 1:6:2], Op.subtract, "en6a f6a pa", "own0")
-        tt(T.pa[:, GD + 15:GD + P:16], T.pb[:, 6:12:2], T.pa[:, 7:12:2], Op.subtract, "en6b f6b pa", "own1")
 
-    def first_labels():
-        act(n32, un, "un", "n32", 1.0 / 32, 16.0)
-        scan(T.tu[:, VQ + 1:VQ + P], n32[:, 0:P - 1], zero[:, 1:P], 0.0, Op.add, Op.add, "n32 zero", "vq")
-        ts(T.lf[:, 0:3], endp, c16, Op.add, None, None, "pww c16", "lf")
-        act(emp, rev(T.tu, P + 1), "un", "emp", 2e29, -1e29)
-        tt(mask0, mask, emp, Op.min, "mask emp", "mask0", cy(96))
-        cp(T.ow[:].indirect(T.lo[:, 0:3]), rev(T.tu, VQ), "vq enz lo ow", "ow", sca(P))
-        scan(T.mr[:, C - 1::-1], T.ow[:, C:0:-1], T.ow[:, C:0:-1], 1000.0, Op.min, Op.min, "ow", "mr", cy(C))
-        pick(T.mww[:], T.wpa[:], T.mr[:], "wpa wpb wpc mr", "mww", cy(C))
-        act(T.pib[:], T.mww[:, 15:C:16], "mww cl", "pib", 1.0 / 16, cl)
-        act(T.lb1[:, 0:80:4], T.jw[:], "jw", "l0")
-        act(T.lb1[:, 1:80:4], T.mww[:, 15:C:16], "mww ck", "l1", -32.0, ck)
-        act(e4, T.pib[:], "pib", "e4", 512.0, -512.0 * 192)
+    def first_labels(t):
+        fw, fk = (T.fw[:, OW * (t - 1):OW * t], "fw%d" % t) if t else (T.ow[:], "ow")
+        fill(mv, 64.0, "cw0 cw1", 20)
+        act(e4, T.jw[:], "jw", "e4", -1.0, KEY + HC + 64 * MID)
+        act(vq, hh, "hh c63", "vq", 1.0 / 64, c63)
+        cp(fw.indirect(T.lo[:, 0:3]), rev(T.n48, 2 * P), "vq lo " + fk, fk, sca(P))
+        scan(T.mr[:, C - 1::-1], fw[:, C:0:-1], fw[:, C:0:-1], -BIG, Op.max, Op.max, fk, "mr", cy(C))
+        pick(T.vw[:, 0:15 * C:15], T.wpa[:], T.mr[:], "wpa wpb wpc mr", "vw0 vw1", cy(C))
+        act(T.pib[:], vw, "vw0 vw1", "pib", -64.0 / KEY, 191.15 - HC / KEY)
+        act(ra, T.pib[:], "pib", "ra", -KEY / 64, 192 * KEY / 64)
+        act(T.d1[:, 0:GW:M], vw, "vw0 vw1 d1", "d1", -16.0 / KEY, 192 - 0.586 - HC / KEY / 4)
+        ts(T.po[:], T.pib[:], -192.0, Op.add, None, None, "pib", "po")
+
+    def next_labels():
+        act(T.pib[:], e2, "ee0 ee1", "pib", -1.0, 192.0)
+        ts(ra, vw, RND, Op.add, RND, Op.subtract, "vw0 vw1", "ra")
+        act(T.d1[:, 0:GW:M], e2, "ee0 ee1 d1", "d1", -0.25, 192 - 0.425)
+        ts(T.po[:], e2, -1.0, Op.mult, None, None, "ee0 ee1", "po")
 
     def labels(first):
-        act(T.lb1[:, 3:80:4], T.pib[:], "pib", "l3", 1.0, -192.0)
-        scan(T.lab[:], T.la[:], T.lb1[:], 0.0, Op.mult, Op.add, "la l0 l1 l2 l3 e4", "kk zz", cy(80))
-        act(pit, T.pib[:], "pib", "pit", 1.0, -192.0)
-        act(T.d1[:, 0:GW:M], T.pib[:], "pib d1", "d1", 0.25, 144 - 0.375)
-        ts(T.po[:], T.pib[:], -192.0, Op.add, None, None, "pib", "po")
-        act(lap, zz, "zz cw", "cw", 1.0 / 48, 191.5 + 1.5 / 48)
-        act(k2, kk, "kk", "k2", 1.0 / MV, (192 * 48.0 + 1.75) / MV)
+        act(np_, T.pib[:], "pib", "np", -1.0, 192.0)
+        scan(T.lab[:], slot(T.cw, 81, 48), slot(T.vw, 177, 48), 0.0, Op.mult, Op.add, "cz1 cz2 cz3 cz4 cw0 cw1 l1 ra vw0 vw1 e4 np", "kk", cy(100))
+        act(lap, nz, "kk", "lap", -1.0 / 48, 191.5 + 1.5 / 48)
+        act(k2, nk, "kk", "k2", 1.0 / MV, -(192 * 48.0 + 1.4) / MV)
         scan(T.v1[:], T.r12[:], T.d1[:], 0.0, Op.mult, Op.add, "r12 d1", "v1", cy(GW // 2))
         if first: ts(T.inc[:], T.v1[:], 191.0, Op.is_equal, None, None, "v1", "inc", cy(GW))
         else:
             act(T.ab[:], T.v1[:], "v1", "ab", 1.0, -191.0, cy(GW), Act.Abs)
             act(T.inc[:], T.ab[:], "ab", "inc", -1.0, 1.0, cy(GW), Act.Relu)
-        act(T.inc[:, 0:GW:M], zz, "zz inc", "inc", 1.0 / 48, 1.0 / 48 - 1)
+        act(T.inc[:, 0:GW:M], nz, "kk inc", "inc", -1.0 / 48, 1.0 / 48 - 1)
         scan(T.yg[:], T.r12[:], T.inc[:], 0.0, Op.mult, Op.add, "r12 inc", "yg", cy(GW))
 
     def pack(t, wq, ws, wk, out, ok):
         qx, sx = (T["qx%d" % t], T["sx%d" % t]) if t < R else (T.qx, T.sx)
-        for h, a, n, rd in ((0, 0, HALF, "x%da x%db" % (t, t)), (1, HALF, C - HALF, "x%dc x%dd" % (t, t))):
+        for h, a, n in ((0, 0, QH), (1, QH, C - QH)):
             nm = "ab"[h]
-            quant(qx[:, a:a + n], sx[:, a:a + n], X[t][:, 4 * a:4 * a + 4 * n], rd, "qx%s%d" % (nm, t), n)
+            quant(qx[:, a:a + n], sx[:, a:a + n], X[t][:, 4 * a:4 * a + 4 * n], xkeys(t, a, a + n) + " qxa3" * (t == R and h), "qx%s%d" % (nm, t), n)
             mm(h, n, wq, ws, qx[:, a:a + n], sx[:, a:a + n], wk + " qx%s%d" % (nm, t))
             act(out(a, n), T.ps[:, 512 * h:512 * h + n], "ps%d" % h, ok + nm + " ps%d" % h, c=cy(n))
 
-    sizes(True)
-    places()
-    tables()
-    first_labels()
+    sizes(-1)
+    places(False)
+    tables(1.0)
+    first_labels(0)
     labels(True)
-    pool = "p0 p1 p2 p3"
+    old, new = "slw", "ow"
     for t in range(R):
-        xk = "x%da x%db x%dc x%dd x%dz" % (t, t, t, t, t)
+        xk = xkeys(t, 0, C) + " x%dz" % t
         pack(t, T.qu[:], T.su[:], "qu su", lambda a, n: T.sw_[:, 1 + a:1 + a + n], "sw")
-        qx, sx, ql, sl, arr = T["qx%d" % t], T["sx%d" % t], T["ql%d" % t], T["sl%d" % t], T.sem["arr%d" % t]
-        na = send(ql[:].bitcast(dt.uint8), qx[:].bitcast(dt.uint8), arr, t, "qxa%d qxb%d" % (t, t), "r0", "R")
-        na += send(sl[:], sx[:], arr, t, "qxa%d qxb%d" % (t, t), "r1", "R")
-        add("p", lambda arr=arr, n=na: g.tensor.wait_ge(arr, n), "r0 r1", "ql%d" % t, 0.0, "w")
-        for b in range(4):
-            mm(4 + b, C, T.qe[:, 128 * b:128 * b + 128], T.se[:, 128 * b:128 * b + 128], ql[:], sl[:], "qe%d ql%d" % (b, t))
-            act(T.dd[:, DW * b:DW * b + C], T.ps[:, 512 * (4 + b):512 * (4 + b) + C], "ps%d" % (4 + b), "dd%d ps%d" % (b, 4 + b), c=cy(C))
-        if t: tt(T.mk[:], T.sw_[:].indirect(T.lo[:, 0:3]), mask, Op.min, "swa swb swz swy lo mask", "mk", ga(P))
-        else: tt(T.mk[:], T.sw_[:].indirect(T.lf[:, 0:3]), mask0, Op.min, "swa swb swz swy lf mask0", "mk", ga(P))
-        scan(T.rm[:], rev(T.mk, 0), rev(T.mk, 0), -3e29, Op.max, Op.max, "mk", "rm")
+        qx, sx, ql, sl = T["qx%d" % t], T["sx%d" % t], T["ql%d" % t], T["sl%d" % t]
+        for h, a, z in ((0, 0, QH), (1, QH, C)):
+            arr, nm = T.sem["ar%s%d" % ("ab"[h], t)], "ab"[h]
+            na = send(ql[:, a:z].bitcast(dt.uint8), qx[:, a:z].bitcast(dt.uint8), arr, t, "qx%s%d" % (nm, t), "r0" + nm, "R")
+            if h == 0: na += send(sl[:], sx[:], arr, t, "qxa%d qxb%d" % (t, t), "r1", "r")
+            add("p", lambda arr=arr, n=na: g.tensor.wait_ge(arr, n), "r0b qla%d" % t if h else "r0a r1", "ql%s%d" % (nm, t), 0.0, "w")
+            for b in range(4):
+                k = 4 - 4 * h + b
+                mm(k, z - a, T.qe[:, 128 * b:128 * b + 128], T.se[:, 128 * b:128 * b + 128], ql[:, a:z], sl[:, a:z], "qe%d ql%s%d" % (b, nm, t))
+                act(T.dd[:, 4 * a + b:4 * z:4], T.ps[:, 512 * k:512 * k + z - a], "ps%d" % k, "dd%s%d ps%d" % (nm, b, k), c=cy(z - a))
+        tt(T.mk[:], T.sw_[:].indirect(T.lo[:, 0:3]), mask, Op.add, "swa swb swz swy lo mask", "mk", ga(P))
+        scan(T.rm[:], rev(T.mk, 0), rev(T.mk, 0), -2e29, Op.max, Op.max, "mk", "rm")
         add("s", lambda: S.activation(lt, T.rm[:], Act.Sign, bias=T.rm[:, P - 1:P], scale=-1.0, accum_out=T.pc[:, 0:1]), "rm", "lt pc", 0.09)
         ts(T.pm[:], T.base[:], T.pc[:, 0:1], Op.add, None, None, "pc base", "pm")
+        if t == 0:
+            dma("y", T.qw[:, 0:256].bitcast(dt.uint8), T.wc[:, 0:1024], "lt", "qw0", 0.8)
+            dma("y", T.sw[:], T.ws[:], "lt", "sw", 0.8)
         crp = T.crp[:, 64 * t:64 * t + 64]
         cp(crp.indirect(T.pm[:, 0:1]), T.crp[:, R * 64:R * 64 + 16], "pm crs crp%d" % t, "crp%d" % t, sca(16))
         pm64 = T.pm[:, 0:3]
-        act(gg, T.t1[:].indirect(pm64), "t1s3 t1s4 t1s5 t1s6 t10 t11 t12 pm", "gg", c=ga(P))
-        scan(T.gt[:, 0:GT:3], gg, gd, 0.0, Op.add, Op.min, "gg pa t1n own0 own1", "gs")
+        act(T.gg[:], T.t1[:].indirect(T.pm[:]), "t1s3 t1s4 t1s5 t1s6 t10 t11 t12 es esz pm", "gg", c=ga(64))
+        scan(T.gt[:, 0:GT:3], T.gg[:, 0:P], gd, 0.0, Op.add, Op.min, "gg gd t1n l9 own1", "gs")
         ts(idx, T.gt[:, 39:GT:P], -1.0, Op.mult, 0.1 - GS, Op.add, "gs", "idx")
-        act(T.gt[:, 1:GT:3], T.th[:].indirect(pm64), "th th0 th1 th2 pm", "g1", c=ga(P))
-        act(T.gt[:, 2:GT:3], T.th[:].indirect(pm64), "th th0 th1 th2 pm", "g2", 1.0, -LAP, ga(P))
-        a, b = RJ + 5 * (GT - 1), RJ + 5 * GT
-        scan(T.rj[:, a:RJ - 1:-5], T.rs2[:], T.gt[:, GT - 1::-1], 0.0, Op.add, Op.max, "rs2 g1 g2 gs", "rj0", cy(GT))
-        scan(T.rj[:, b + 5 * (GT - 2):b - 1:-5], T.gt[:, GT - 2::-1], T.rj[:, a:RJ + 4:-5], NONE, Op.max, Op.min, "rj0 g1 g2 gs", "rj1", cy(GT))
-        scan(T.dec[:, 0:30], T.rj[:, RJ + 5 - P:RJ + 6 + 28 * P:P], T.rj[:, RJ - 4 * P:RJ + 1 + 25 * P:P], 0.0, Op.mult, Op.add,
-             "rj0 rj1 rk0 rk1 rk2 rk3 rk4 rk5", "dec")
+        act(T.gt[:, 1:GT:3], T.th[:].indirect(pm64), "th thz0 thz1 th0 th1 th2 pm", "g1", 1.0, HC, ga(P))
+        act(T.gt[:, 2:GT:3], T.th[:].indirect(pm64), "th thz0 thz1 th0 th1 th2 pm", "g2", 1.0, HC - LAP, ga(P))
+        a, b = RJ + DN * (GT - 1), RJ + DN * GT
+        scan(T.rj[:, a:RJ - 1:-DN], T.rs2[:], T.gt[:, GT - 1::-1], 0.0, Op.add, Op.max, "rs2 g1 g2 gs", "rj0", cy(GT))
+        scan(T.rj[:, b + DN * (GT - 2):b - 1:-DN], T.gt[:, GT - 2::-1], T.rj[:, a:RJ + DN - 1:-DN], NONE, Op.max, Op.min, "rj0 g1 g2 gs", "rj1", cy(GT))
+        scan(T.dec[:, 0:6 * DN], T.rj[:, r0:r0 + 6 * per - P + 1:P], T.rj[:, r1:r1 + 6 * per - P + 1:P], 0.0, Op.mult, Op.add,
+             "rj0 rj1 rk0 rk1 rk2 rk3 rk4 rk5 rk6 rk7 rk8", "dec", cy(6 * DN))
         lm, lp, lis = T["lm%d" % t], T["lp%d" % t], T.sem["lis%d" % t]
-        ts(lm[:, 0:6], T.dec[:, 4:30:5], -0.9, Op.add, None, None, "dec", "lm%d" % t)
-        nl = send(lp[:, 0:6], lm[:, 0:6], lis, t, "lm%d" % t, "r3", "r")
-        win = X[t][:, 0:4 * HB]
-        for b in range(4):
-            ts(T.ao[:, 6 * b:6 * b + 6], lm[:, 0:6], 4.0, Op.mult, float(b), Op.add, "lm%d" % t, "ao%d" % b)
-            act(T.ta[:, b:4 * NT:4], win.indirect(T.ao[:, 6 * b:6 * b + 6]), "ao%d %s" % (b, xk), "ta%d" % b, c=ga(NT))
-        act(T.a64[:], T.ta[:], "ta0 ta1 ta2 ta3", "a64", 64.0, c=cy(384), cv=cy(192))
-        sizes(False)
+        ts(lm[:], T.dec[:, 0:6 * DN].indirect(T.dlo[:]), 4.0 * C + 3, Op.min, None, None, "dec dlo", "lm%d" % t, ga(32))
+        nl = send(lp[:], lm[:, 6:30], lis, t, "lm%d" % t, "r3", "r")
+        if t == 0:
+            dma("y", T.qw[:, 256:512].bitcast(dt.uint8), T.wc[:, 1024:2048], "lm0", "qw1", 0.8)
+        if t == 1:
+            dma("y", T.vb[:], T.v[:], "lm1", "vb", 0.8)
+            quant(T.qv[:], T.sv[:], T.vb[:], "vb", "qv")
         for h in range(2):
-            act(T.cg[:, HALF * h:HALF * h + HALF], crp.indirect(T.po[:, 10 * h:10 * h + 10]), "crp%d po" % t, "cg%d" % h, c=ga(HALF))
-        pick(T.cw[:, 0:3 * C:3], T.wpa[:], T.cg[:], "wpa wpb wpc cg0 cg1 cw", "cw", cy(C // 2))
-        scan(T.ee[:], T.cw[:, 13:3 * C:16], T.ea0[:], 0.0, Op.mult, Op.add, "cw k2 pit ea0", "ee")
-        ts(T.vo[:], e2, 0.25, Op.add, None, None, "ee", "vo")
+            act(T.ta[:, 4 * NT * h:4 * NT * h + 4 * NT:2], X[t][:, 0:4 * HB].indirect(lm[:, 6 + 12 * h:18 + 12 * h]), "lm%d " % t + xk, "ta%d" % h, c=ga(2 * NT))
+        act(T.a64[:], T.ta[:, 0:8 * NT:2], "ta0 ta1", "a64", 64.0, c=cy(384), cv=cy(192))
+        sizes(t)
         for h in range(2):
             a = HALF * h
-            act(T.val[:, a:a + HALF], T.tu[:, 0:P + 1].indirect(T.vo[:, 10 * h:10 * h + 10]), "en enz vo c16", "val%d" % h, 1.0, c16, ga(HALF))
-            pick(T.vw[:, a:a + HALF], T.wpa[:, 0:HALF], T.val[:, a:a + HALF], "wpa wpb val%d" % h, "vw%d" % h, cy(HALF))
-        vw = T.vw[:, 15:C:16]
-        act(T.e16[:], T.es[:].indirect(T.pm[:, 0:1]), "es esz pm", "e16", c=0.09)
+            act(T.cg[:, a:a + HALF], crp.indirect(T.po[:, 10 * h:10 * h + 10]), "crp%d po" % t, "cg%d" % h, c=ga(HALF))
+            pick(T.cw[:, 15 * a:15 * a + 15 * HALF:15], T.wpa[:, 0:HALF], T.cg[:, a:a + HALF], "wpa wpb cg%d" % h, "cw%d" % h, cy(HALF // 2))
+            scan(T.ee[:, 30 * h:30 * h + 30], slot(T.cw, 65, 80, h, 10), slot(T.vw, 209, 80, h, 10), 0.0, Op.mult, Op.add, "cw%d cz0 lap k2 np ea0" % h, "ee%d" % h)
+            ts(T.vo[:, 10 * h:10 * h + 10], T.ee[:, 30 * h + 2:30 * h + 30:3], -1.0, Op.mult, 0.3, Op.add, "ee%d" % h, "vo%d" % h)
+            act(T.val[:, a:a + HALF], T.tu[:, 0:P + 1].indirect(T.vo[:, 10 * h:10 * h + 10]), "en enz vo%d" % h, "val%d" % h, c=ga(HALF))
+            pick(T.vw[:, 15 * a:15 * a + 15 * HALF:15], T.wpa[:, 0:HALF], T.val[:, a:a + HALF], "wpa wpb val%d" % h, "vw%d" % h, cy(HALF))
         for m in range(M):
-            act(T.wg[:, m:GW:M], T.yg[:, m:GW:M], "yg e16", "wg%d" % m, -1.0, T.e16[:, m + 1:m + 2])
-        ts(T.wr[:], T.wg[:], -192.0, Op.add, 0.0, Op.max, " ".join("wg%d" % m for m in range(M)), "wr", cy(GW // 2))
-        scan(T.rr[:], T.r12[:], T.wr[:], 0.0, Op.mult, Op.subtract, "r12 wr", "rr", cy(GW // 2))
-        tt(e3, kk, mv, Op.subtract, "cw kk", "e3")
-        tt(e4, e3, T.rr[:, M - 1:GW:M], Op.max, "e3 rr", "e4")
-        tt(e6, vw, e4, Op.add, "vw0 vw1 e4", "e6")
+            act(T.wg[:, m:GW:M], T.yg[:, m:GW:M], "yg gg", "wg%d" % m, -1.0, T.gg[:, P + m + 1:P + m + 2])
+        add("v", lambda: V.tensor_scalar(T.wr[:], T.wg[:], -192.0, 0.0, Op.add, Op.max), " ".join("wg%d" % m for m in range(M)), "wr", cy(GW // 2),
+            more=[("s", lambda: S.activation(T.wr[:], T.wg[:], Act.Relu, bias=-192.0, scale=1.0), cy(GW))])
+        scan(T.rr[:], T.r12[:], T.wr[:], 0.0, Op.mult, Op.add, "r12 wr", "rr", cy(GW // 2))
+        tt(e3, nk, mv, Op.add, "cw0 cw1 kk", "e3")
+        tt(e4, e3, T.rr[:, M - 1:GW:M], Op.min, "e3 rr", "e4")
+        tt(e6, vw, e4, Op.subtract, "vw0 vw1 e4", "e6")
         ts(T.do[:], e6, 1.0, Op.add, None, None, "e6", "do")
-        if t == 0: cp(T.ow[:].indirect(T.do[:]), T.tm[:, 0:C], "do tm ow", "ow", sca(C))
-        else: cp(T.ow[:].indirect(T.do[:]), T.slw[:], "do slw ow", "ow", sca(C))
-        places()
-        cp(T.ow[:].indirect(T.lo[:, 0:6]), T.tm[:, HID + NT * t:HID + NT * t + NT], "lo hid ow", "ow", sca(NT))
-        pick(T.oww[:], T.wp4[:], T.ow[:, 1:C + 1], "wp4 ow", "oww", cy(C))
-        ts(T.xo[:], T.oww[:, 3:C:4], 4.0, Op.mult, c4, Op.add, "oww c4", "xo", cy(80))
-        if t < R - 1:
-            act(T.slw[:], T.ow[:].indirect(T.do[:]), "ow do", "slw", c=ga(C))
-            act(T.pib[:], e2, "ee", "pib", 1.0, 191.6)
-            act(ra, vw, "vw0 vw1", "ra", 1.0, RND)
-            act(T.lb1[:, 0:80:4], vw, "vw0 vw1", "l0", 2.0)
-            act(T.lb1[:, 1:80:4], ra, "ra", "l1", -2.0, 2 * RND)
-            act(T.la[:, 2:80:4], mv, "cw la", "l2")
+        hid = T.tm[:, HID + NT * t:HID + NT * t + NT]
+        if t in ANEW: cp(T[old][:].indirect(lm[:, 0:6]), hid, "lm%d hid %s" % (t, old), old, sca(NT))
+        cp(T[new][:].indirect(T.do[:]), T[old][:, 1:C + 1], "do %s %s" % (old, new), new, sca(C))
+        if t not in ANEW or t < R - 1: places(t not in ANEW)
+        if t not in ANEW: cp(T[new][:].indirect(T.lo[:, 0:6]), hid, "lo lo2 hid " + new, new, sca(NT))
+        pick(T.oww[:], T.wpa[:], T[new][:, 1:C + 1], "wpa wpb wpc " + new, "oww", cy(C))
+        ts(T.xo[:], T.oww[:, 15:C:16], c16, Op.add, None, None, "oww c16", "xo")
+        if t + 1 in ANEW:
+            tables(1.0)
+            first_labels(t + 1)
             labels(False)
-            tables()
+            old, new = new, old
+        elif t < R - 1:
+            if t not in ANEW: act(T[old][:, 1:C + 1], T[new][:, 0:C + 1].indirect(T.do[:]), "do " + new, old, c=ga(C))
+            next_labels()
+            labels(False)
+            tables(1.0 / (1.0 - EPS))
         else:
-            act(rev(T.mz, 0), T.tm[:].indirect(idx), tmk, "mz", c=ga(P))
-            dma("y", T.oz[:], T.mz[0:128:16, :], "mz", "oz")
-        add("v", lambda lis=lis, n=nl: V.wait_ge(lis, n), "r3", "lp%d" % t, 0.0, "w")
+            dma("y", T.oz[:], T.tu[15:128:16, P + 1:2 * P + 1], "un", "oz")
+        add("s", lambda lis=lis, n=nl: S.wait_ge(lis, n), "r3", "lp%d" % t, 0.0, "w")
+        for h in range(2):
+            add("s", lambda h=h, lp=lp: S.activation(T.ta[:, 4 * NT * h + 1:4 * NT * h + 4 * NT:2], T.dd[:].indirect(lp[:, 12 * h:12 + 12 * h]), Act.Copy),
+                "dda0 dda1 dda2 dda3 ddb0 ddb1 ddb2 ddb3 ddz lp%d" % t, "td%d" % h, ga(2 * NT))
         for b in range(4):
-            tt(T.tb[:, b:4 * NT:4], T.dd[:, DW * b:DW * b + C + 1].indirect(lp[:, 0:6]), T.ta[:, b:4 * NT:4], Op.add,
-               "ta%d dd%d ddz lp%d" % (b, b, t), "tb%d" % b, ga(NT))
-        quant(T.qb[:], T.sb[:], T.tb[:], "tb0 tb1 tb2 tb3 tbz", "qb")
+            scan(T.tb[:, b:8 * NT:4], T.odd[:], T.ta[:, 2 * NT * b:2 * NT * b + 2 * NT], 0.0, Op.mult, Op.add, "odd ta%d td%d" % (b // 2, b // 2), "tb%d" % b, cy(NT))
+        quant(T.qb[:], T.sb[:], T.tb[:], "tb0 tb1 tb2 tb3", "qb", 2 * NT)
         for b in range(4):
-            mm(b, 128, T.qw[:, 128 * b:128 * b + 128], T.sw[:, 128 * b:128 * b + 128], T.qb[:], T.sb[:], "qw sw qb")
-        h0 = 4 * (C + NT * t)
+            mm(b, 2 * NT, T.qw[:, 128 * b:128 * b + 128], T.sw[:, 128 * b:128 * b + 128], T.qb[:], T.sb[:], "qw%d sw qb" % (b // 2))
+        h0 = C + NT * t
         for b in range(4):
-            tt(T.pool[:, h0 + b:h0 + 4 * NT:4], T.ps[:, 512 * b:512 * b + NT], T.a64[:, b:4 * NT:4], Op.add, "a64 ps%d" % b, "h%d%d ps%d" % (t, b, b), cy(NT))
-        pool += " h%d0 h%d1 h%d2 h%d3" % (t, t, t, t)
-        win, hk = T.pool[:, 0:h0 + 4 * NT], pool + " xo"
-        for k, (a, b) in enumerate(XP):
-            act(X[t + 1][:, 16 * a:16 * b], win.indirect(T.xo[:, a:b]), hk, " ".join("x%d%s" % (t + 1, n) for n in XN[k]), 0.015625, c=ga(16 * (b - a)))
+            tt(T.pool[:, PW * b + h0:PW * b + h0 + NT], T.ps[:, 512 * b + 1:512 * b + 2 * NT:2], T.a64[:, NT * b:NT * b + NT], Op.add,
+               "a64 ps%d" % b, "h%d%d ps%d" % (t, b, b), cy(NT))
+        for k, (b, a, z) in enumerate(XP):
+            hk = "xo p%d " % b + " ".join("h%d%d" % (r, b) for r in range(t + 1))
+            act(X[t + 1][:, 4 * a + b:4 * z:4], T.pool[:, PW * b:PW * b + h0 + NT].indirect(T.xo[:, a // 16:z // 16]), hk,
+                "x%d_%d" % (t + 1, k), 0.015625, c=ga(z - a))
 
     pack(R, T.qv[:], T.sv[:], "qv", lambda a, n: T.yb[:, a:a + n], "yb")
-    dma("y", T.oc[:, 0:4 * HALF], T.qx[:, 0:HALF].bitcast(dt.uint8), "qxa3", "oca")
-    dma("y", T.oc[:, 4 * HALF:4 * C], T.qx[:, HALF:C].bitcast(dt.uint8), "qxb3", "ocb")
+    dma("y", T.oc[:, 0:4 * QH], T.qx[:, 0:QH].bitcast(dt.uint8), "qxa3", "oca", 1.0)
+    dma("y", T.oc[:, 4 * QH:4 * C], T.qx[:, QH:C].bitcast(dt.uint8), "qxb3", "ocb", 0.7)
     for k in range(4):
         dma("ys"[k % 2], T.osc[4 * k:4 * k + 4, :], T.sx[32 * k:32 * k + 4, :], "qxa3 qxb3", "osc%d" % k)
-    dma("y", T.y[:, 0:HALF], T.yb[:, 0:HALF], "yba", "ya")
-    dma("s", T.y[:, HALF:C], T.yb[:, HALF:C], "ybb", "yb")
-    add("g", lambda: g.wait_ge(T.sem.sent, nsent[0]), "r0 r1 r3", "", 0.0, "w")
+    dma("y", T.y[:, 0:QH], T.yb[:, 0:QH], "yba", "ya", 0.2)
+    dma("s", T.y[:, QH:C], T.yb[:, QH:C], "ybb", "yb")
+    add("g", lambda: g.wait_ge(T.sem.sent, nsent[0]), "r0a r0b r1 r3", "", 0.0, "w")
     emit(ops, g, T)

import numpy as np
from concourse.mybir import dt, AluOpType as Op, ActivationFunctionType as Act

C, P, NT, R = 320, 48, 96, 3
STEP = [1, 2, 1]
HB = 324
PW = C + R * NT
OFF, BIG = 1024.0, 1048576.0
FL = 928
DW = 336
GS = 200.0
KEY = 1025.0
LAP = KEY * P
HC = KEY * 512
NONE = C + 1 - 512.0
MV = 512.0
EPS, MID = 1.0 / MV, 0.3125
RND = 12582912.0
OW = 424
M, GW = 12, 240
TS = 52
ANEW = (0,)
HALF, QH = 160, 192
XP = [(0, 0, C), (1, 0, C), (2, 0, QH), (2, QH, C), (3, 0, QH), (3, QH, C)]
GT = 144
RJ, DN, R512 = 192, 11, 6442450944.0
CYC, CALL = 0.00104, 0.5
CASES = [(0.19, 0.9, 0.9, 2.0, 0.3, 0.92, 1.56, 3.8, 1.0), (0.22, 1.0, 1.1, 2.5, 0.4, 0.9, 1.4, 3.0, 1.4),
         (0.17, 1.1, 1.2, 2.4, 0.4, 1.08, 1.7, 4.8, 1.0), (0.18, 1.0, 1.1, 2.4, 0.35, 1.02, 2.05, 2.1, 1.1)]
SLOW = (1.3, 1.6, 0.9, 0.4, -0.4)
FIRST, TRIES, SPELL, SPAN, HEAT = 30000, 800000, 6000, 80, 0.4
NEAR, REACH, SW, AIM, SLACK = 0.1, 40, 0.3, 0.7, 0.05
LONG = "slw val".split()
LANES = {"v": 32, "s": 32, "p": 8, "g": 8}
N20 = "e3 e6".split()
N48 = "hh lt vq ea r16 iom".split()

F, B16, I32, U16, Q4, U8 = "float32", "bfloat16", "int32", "uint16", "float8_e4m3fn_x4", "uint8"


def _s(n, d=F):
    return ("sbuf", [128, n], d)


SCRATCH = {
    "pool": _s(4 * PW, B16), "x0": _s(4 * HB, B16), "x1": _s(4 * HB, B16), "x2": _s(4 * HB, B16), "x3": _s(4 * C, B16),
    "ub": _s(512, B16), "vb": _s(512, B16), "szb": _s(4, I32),
    "qu0": _s(128, Q4), "su0": _s(128, U8), "qu": _s(128, Q4), "su": _s(128, U8), "qv": _s(128, Q4), "sv": _s(128, U8),
    "qw": _s(512, Q4), "sw": _s(512, U8), "qe": _s(512, Q4), "se": _s(512, U8),
    "qx": _s(C, Q4), "sx": _s(C, U8), "qb": _s(2 * NT, Q4), "sb": _s(2 * NT, U8),
    "ones": _s(256, B16), "eye": _s(528, B16), "dd": _s(4 * HB, B16),
    "ta": _s(8 * NT, B16), "tb": _s(8 * NT, B16), "odd": _s(2 * NT, B16), "a64": _s(4 * NT, B16),
    "ps": ("psum", [128, 4096], F), "n20": _s(24 * len(N20)), "n48": _s(P * len(N48)),
    "tm": _s(FL + DW), "ip": _s(8, I32), "col": _s(8), "j20": _s(20), "jw": _s(20),
    "jm": _s(NT, B16), "wpa": _s(C, B16), "r12": _s(GW, B16),
    "base": _s(4), "ht": _s(3 * P, B16), "kt": _s(3 * P), "tr": _s(3 * P), "t1": _s(4 * TS), "th": _s(3 * TS), "gg": _s(64),
    "upk": _s(8, U16), "qc": _s(8),
    "sw_": _s(376), "mk": _s(P), "rm": _s(P), "pc": _s(8), "pm": _s(4, U16),
    "idx": _s(4, U16), "tu": _s(160), "pww": _s(C),
    "gt": _s(GT), "rj": _s(RJ + 2 * DN * GT), "rs2": _s(GT, B16), "dec": _s(72),
    "gd": _s(176), "lo": _s(8, U16), "dl": _s(80), "dlo": _s(2, U16),
    "ee": _s(60), "lab": _s(100), "pib": _s(20, B16),
    "crp": _s(R * 64 + 16, B16), "cg": _s(C, B16), "cw": _s(15 * C + 96, B16), "val": _s(C), "vw": _s(15 * C + 192),
    "d1": _s(GW, B16), "v1": _s(GW, B16), "ab": _s(GW, B16), "inc": _s(GW), "yg": _s(GW),
    "wg": _s(GW, B16), "wr": _s(GW, B16), "rr": _s(GW, B16),
    "vo": _s(20, U16), "do": _s(20, U16), "ow": _s(OW), "slw": _s(OW), "oww": _s(C), "xo": _s(20, U16),
    "mr": _s(C), "fw": _s(2 * OW), "po": _s(20, U16),
    "sc": _s(4), "yb": _s(C),
}
for _t in range(R):
    SCRATCH["qx%d" % _t] = _s(C, Q4)
    SCRATCH["sx%d" % _t] = _s(C, U8)
    SCRATCH["ql%d" % _t] = _s(C, Q4)
    SCRATCH["sl%d" % _t] = _s(C, U8)
    SCRATCH["lm%d" % _t] = _s(32, U16)
    SCRATCH["lp%d" % _t] = _s(24, U16)
SEMAPHORES = (["sent", "ara0", "ara1", "ara2", "arb0", "arb1", "arb2", "lis0", "lis1", "lis2"] + ["d%d" % i for i in range(24)]
              + [e + str(i) for e in LANES for i in range(LANES[e])])
ORDER = {}


def depends(ops):
    last_w, readers, deps = {}, {}, []
    for n, (rd, wr) in enumerate(o[2:4] for o in ops):
        d = set()
        for k in rd:
            if k in last_w: d.add(last_w[k])
        for k in wr:
            if k in last_w: d.add(last_w[k])
            d.update(readers.get(k, []))
        d.discard(n)
        deps.append(d)
        for k in rd: readers.setdefault(k, []).append(n)
        for k in wr:
            last_w[k] = n
            readers[k] = []
    return deps


def price(c, case):
    return case[5] * (c.real + CYC * (c.imag * case[6] if c.imag > 0 else -c.imag * case[7]))


def arrange(ops, deps):
    n = len(ops)
    if n in ORDER: return ORDER[n]
    K = range(len(CASES))
    eng = ["vspgy".index(o[0]) for o in ops]
    deps = [sorted(d) for d in deps]
    users = [[] for o in ops]
    for i in range(n):
        for d in deps[i]: users[d].append(i)
    cost = [[k[4] if o[4] in "rR" else price(o[5], k) * (k[8] if o[0] == "p" else 1.0) if o[4] == "c" else o[5] for o in ops] for k in CASES]
    late = [[{"d": k[1], "r": k[2], "R": k[3], "w": -k[0]}.get(o[4], 0.0) + k[0] + o[7] for o in ops] for k in CASES]
    form = [0] * n

    def choose(c, k):
        form[c], eng[c] = k, "vspgy".index(ops[c][6][k][0])
        for i in K: cost[i][c] = price(ops[c][6][k][2], CASES[i])

    way = [0.0] * n
    for i in range(n - 1, -1, -1):
        way[i] = cost[0][i] + late[0][i] + max([way[u] for u in users[i]] + [0.0])
    left, ready, free, order = [len(d) for d in deps], [0.0] * n, [0.0] * 5, []
    pool = [i for i in range(n) if not left[i]]
    while pool:
        t = min(max(ready[i], free[eng[i]]) for i in pool)
        c = max((i for i in pool if max(ready[i], free[eng[i]]) <= t + 0.1), key=lambda i: way[i])
        pool.remove(c)
        order.append(c)
        free[eng[c]] = max(ready[c], free[eng[c]]) + cost[0][c]
        for u in users[c]:
            ready[u] = max(ready[u], free[eng[c]] + late[0][c])
            left[u] -= 1
            if not left[u]: pool.append(u)

    fin, tail = [[0.0] * n for k in K], [[0.0] * n for k in K]
    head, rest = [[[0.0] * 5] * (n + 1) for k in K], [[[0.0] * 5] * (n + 1) for k in K]
    pos = [0] * n

    def renew(a, b, w0, w1):
        for i in range(a, b + 1): pos[order[i]] = i
        for k in K:
            co, la, f, h = cost[k], late[k], fin[k], head[k]
            q = h[a]
            for i in range(a, w1 + 1):
                c = order[i]
                e = eng[c]
                s = q[e]
                for d in deps[c]:
                    if f[d] > s: s = f[d]
                q = q[:]
                q[e] = s = s + co[c]
                f[c], h[i + 1] = s + la[c], q
            f, h = tail[k], rest[k]
            q = h[b + 1]
            for i in range(b, w0 - 1, -1):
                c = order[i]
                e = eng[c]
                s = 0.0
                for u in users[c]:
                    if f[u] > s: s = f[u]
                s += la[c]
                if q[e] > s: s = q[e]
                q = q[:]
                q[e] = f[c] = s + co[c]
                h[i] = q

    def through(a, b, part, ends, room):
        worse = 0.0
        for k in K:
            co, la, f, t, q = cost[k], late[k], fin[k], tail[k], head[k][a][:]
            old = max(max([f[c] - la[c] - co[c] + t[c] for c in part]), max([x + y for x, y in zip(q, rest[k][b + 1])]))
            new, most = {}, 0.0
            for c in part:
                e = eng[c]
                s = q[e]
                for d in deps[c]:
                    v = new.get(d) or f[d]
                    if v > s: s = v
                q[e] = s = s + co[c]
                new[c] = s = s + la[c]
                if s > most: most = s
                for u in users[c]:
                    if pos[u] > b and s + t[u] > most: most = s + t[u]
            for x, y in zip(q, rest[k][b + 1]):
                if x + y > most: most = x + y
            worse += most - old + max(most - ends[k], 0.0)
            if worse > room + SLACK * (len(K) - 1 - k): break
        return worse

    def longest(w0, w1):
        return [max(fin[k][c] - late[k][c] - cost[k][c] + tail[k][c] for c in order[w0:w1 + 1]) for k in K]

    def tidy(w0, w1):
        f, la, co = fin[0], late[0], cost[0]
        order[w0:w1 + 1] = sorted(order[w0:w1 + 1], key=lambda x: f[x] - la[x] - co[x] + 1e-9 * pos[x])
        renew(w0, w1, w0, w1)

    rng = np.random.RandomState(1)

    def improve(w0, w1, tries):
        ends, m = longest(w0, w1), w1 - w0 + 1
        best, kept = sum(ends), (order[w0:w1 + 1], list(form))
        for step, (r0, r1, r2, r3, r4) in enumerate(rng.rand(tries, 5).tolist()):
            x0 = int(r0 * m)
            c = order[w0 + x0]
            ahead, behind = AIM / 2 <= r1 < AIM, r1 < AIM / 2
            if ahead or behind:
                k = step % len(CASES)
                f, la, co, t, e = fin[k], late[k], cost[k], tail[k], ends[k] - NEAR
                for x in range(x0, x0 + 60):
                    x = w0 + x % m
                    c = order[x]
                    s = f[c] - la[c] - co[c]
                    if s + t[c] >= e and s - head[k][x][eng[c]] < 1e-9 and all(f[d] < s - 1e-9 for d in deps[c]): break
                else: continue
                if behind:
                    x -= 1
                    while x >= w0 and eng[order[x]] != eng[c]: x -= 1
                    if x < w0: continue
                    c = order[x]
            i, was, many = pos[c], form[c], len(ops[c][6])
            lo, hi = max([pos[d] + 1 for d in deps[c]] + [w0, i - REACH]), min([pos[u] - 1 for u in users[c]] + [w1, i + REACH])
            swap = many > 1 and r3 < SW
            if swap: j = min(hi, max(lo, i + int(r2 * 9) - 4))
            else:
                mates = [x for x in range(i if behind else lo, (i if ahead else hi) + 1) if eng[order[x]] == eng[c] and x != i]
                if not mates: continue
                if ahead or behind: mates = mates[:6] if behind else mates[-6:]
                j = mates[int(r2 * len(mates))]
            a, b = min(i, j), max(i, j)
            if swap:
                start = [fin[k][c] - cost[k][c] + tail[k][c] for k in K]
                choose(c, (was + 1 + step % (many - 1)) % many)
                keep = [tail[k][c] for k in K]
                for k in K: tail[k][c] = start[k] - fin[k][c] + cost[k][c]
            part = [c] + order[a:b] if j < i else order[a + 1:b + 1] + [c]
            room = HEAT * (1 - step / tries) * r4
            worse = through(a, b, part, ends, room)
            if swap:
                for k in K: tail[k][c] = keep[k]
            if worse <= room:
                order[a:b + 1] = part
                renew(a, b, w0, w1)
                if step % 12 == 0: tidy(w0, w1)
                ends = longest(w0, w1)
                if sum(ends) < best - 1e-9: best, kept = sum(ends), (order[w0:w1 + 1], list(form))
            elif swap: choose(c, was)
        order[w0:w1 + 1] = kept[0]
        for c in kept[0]:
            if form[c] != kept[1][c]: choose(c, kept[1][c])
        renew(0, n - 1, 0, n - 1)
        tidy(0, n - 1)

    renew(0, n - 1, 0, n - 1)
    improve(0, n - 1, FIRST)
    for turn in range(TRIES // SPELL):
        w0 = rng.randint(-SPAN // 2, n - SPAN // 2)
        improve(max(w0, 0), min(w0 + SPAN, n - 1), SPELL)
    ORDER[n] = order, form
    return ORDER[n]


def settle(ops):
    deps = depends(ops)
    order, form = arrange(ops, deps)
    return [(o[6][k][0], o[6][k][1], o[2], o[3], o[4], o[6][k][2], o[7]) for o, k in zip(ops, form)], deps, order


def emit(ops, g, T):
    queue = {"v": g.vector, "s": g.scalar, "p": g.tensor, "g": g, "y": g.sync}
    ops, deps, order = settle(ops)
    known = {e: 0 for e in queue}
    after, sig, waited, place = {}, {}, set(), {}
    lanes = {e: [] for e in LANES}
    ndma = 0

    def wait(e, d):
        queue[e].wait_ge(T.sem[sig[d][0]], sig[d][1])
        waited.add(d)
        known[e] |= after[d]

    for n in order:
        e, fn, rd, wr, kind = ops[n][:5]
        place[n] = len(place)
        for d in sorted(deps[n], key=lambda d: -place[d]):
            if ops[d][4] not in "rR" and not known[e] >> d & 1: wait(e, d)
        if kind == "w":
            fn()
            known[e] |= 1 << n
            after[n] = known[e]
            continue
        if kind == "c":
            ls = lanes[e]
            k = next((i for i in range(len(ls)) if known[e] >> ls[i][1] & 1), None)
            if k is None and len(ls) < LANES[e]:
                ls.append([0, n])
                k = len(ls) - 1
            elif k is None:
                k = min(range(len(ls)), key=lambda i: place[ls[i][1]])
                wait(e, ls[k][1])
            ls[k][0] += 1
            ls[k][1] = n
            sig[n] = (e + str(k), ls[k][0])
        elif kind == "d":
            sig[n] = ("d%d" % ndma, 16)
            ndma += 1
        after[n] = known[e] | 1 << n
        ins = fn()
        if kind not in "rR": ins.then_inc(T.sem[sig[n][0]], 16 if kind == "d" else 1)
    for e in lanes:
        for ln in lanes[e]:
            if ln[1] not in waited: wait(e, ln[1])
    for n in sig:
        if ops[n][4] == "d" and n not in waited: wait(ops[n][0], n)


def rank_program(g, core, T, topo):
    rank = T.rank_of(core)
    if rank is None:
        return
    flip = (rank ^ (rank >> 1)) & 1
    sg = -1.0 if flip else 1.0
    V, S = g.vector, g.scalar
    ops = []
    nsent = [0]

    def add(e, fn, rd, wr, cost, kind="c", more=(), slow=0.0):
        ops.append((e, fn, rd.split(), wr.split(), kind, cost, [(e, fn, cost)] + list(more), slow))

    def cy(n): return max(64, n) * CYC

    def ga(n): return 0.055 + n * 1j

    def sca(n): return 0.05 - n * 1j

    def ts(out, in0, s1, o0, s2, o1, rd, wr, c=0.067):
        if o1 is None: add("v", lambda: V.tensor_scalar(out, in0, s1, None, o0), rd, wr, c)
        else: add("v", lambda: V.tensor_scalar(out, in0, s1, s2, o0, o1), rd, wr, c)

    def tt(out, a, b, o, rd, wr, c=0.067):
        add("v", lambda: V.tensor_tensor(out, a, b, o), rd, wr, c)

    def cp(out, a, rd, wr, c=0.067):
        add("v", lambda: V.tensor_copy(out, a), rd, wr, c)

    def scan(out, d0, d1, init, o0, o1, rd, wr, c=0.067):
        add("v", lambda: V.tensor_tensor_scan(out, d0, d1, init, o0, o1), rd, wr, c)

    def fill(ap, v, wr, n, half=False):
        more = [("s", lambda: S.activation(ap, T.ones[:, 0:n], Act.Copy, scale=float(v)), cy(n))] if n <= 256 else []
        if v == int(v) and abs(v) < 2 ** 24:
            more.append(("g", lambda: g.iota(ap, [[0, n]], int(v), 0, allow_small_or_imprecise_dtypes=True), 0.13 + 2 * n * CYC))
        add("v", lambda: V.memset(ap, v), "ones" if n <= 256 else "", wr, cy(n // 2 if half else n), more=more)

    def act(out, a, rd, wr, scale=1.0, bias=None, c=0.067, f=None, cv=None):
        if f: return add("s", lambda: S.activation(out, a, f, bias=bias, scale=scale), rd, wr, c)
        if bias is None:
            other = (lambda: V.tensor_copy(out, a)) if scale == 1.0 else (lambda: V.tensor_scalar(out, a, scale, None, Op.mult))
            add("s", lambda: S.activation(out, a, Act.Copy, scale=scale), rd, wr, c, more=[] if wr[:3] in LONG else [("v", other, cv or c)])
        else:
            add("s", lambda: S.activation(out, a, Act.Identity, bias=bias, scale=scale), rd, wr, c,
                more=[("v", lambda: V.tensor_scalar(out, a, scale, bias, Op.mult, Op.add), cv or c)])

    def quant(q, s, a, rd, wr, n=128):
        add("v", lambda: V.quantize_mx(q, s, a), rd, wr, 0.015 + 0.0011 * n)

    def mm(bank, n, wq, ws, xq, xs, rd):
        add("p", lambda: g.tensor.matmul_mx(T.ps[:, 512 * bank:512 * bank + n], wq, ws, xq, xs, True, True), rd, "ps%d" % bank, (n + 16) * 0.001)

    def iota(out, pat, base, cm, wr, flt=True):
        n = 1
        for a in pat: n *= a[1]
        if flt: add("g", lambda: g.iota(out, pat, base, cm, allow_small_or_imprecise_dtypes=True), "", wr, 0.13 + 2 * n * CYC)
        else: add("g", lambda: g.iota(out, pat, base, cm), "", wr, 0.13 + 2 * n * CYC)

    def dma(e, out, a, rd, wr, slow=0.0):
        q = {"y": g.sync, "s": S, "g": g}[e]
        add(e, lambda: q.dma_start(out, a), rd, wr, 0.1, "d", slow=slow)

    def send(dst, src, arr, t, rd, wr, kind):
        mate = T.cores[rank ^ STEP[t]]
        rid, pid = topo.addr(mate)[0:2]
        add("g", lambda: g.remote_dma(dst, src, arr, T.sem.sent, pid, rid, topo.mask(core, mate)), rd, wr, CALL, kind,
            slow=(wr != "r3") * (SLOW[0] * (t == 0) + SLOW[2] * (topo.die(T.cores[0]) != topo.die(T.cores[STEP[t]])) + SLOW[3 + (kind == "R")]))
        k = len(topo.engines(core, mate))
        nsent[0] += k
        return k

    def plus(out, a, b, o, rd, wr):
        scan(out, a, b, -BIG, Op.max, o, rd, wr)

    def pick(out, pat, src, rd, wr, c):
        scan(out, pat, src, 0.0, Op.add, Op.min, rd, wr, c)

    def rev(buf, a, on=True, n=P):
        if not (flip and on): return buf[:, a:a + n]
        return buf[:, a + n - 1:a - 1:-1] if a else buf[:, n - 1::-1]

    def xkeys(t, a, b):
        if t == 0: return "x0a " * (a < QH) + "x0b " * (b > QH)
        return " ".join("x%d_%d" % (t, k) for k, (p, lo, hi) in enumerate(XP) if lo < b and a < hi)

    X = [T.x0, T.x1, T.x2, T.x3]
    col = T.col
    ci, cm, c16, csp, c36, cq, c63 = (col[:, k:k + 1] for k in range(7))
    e3, e6 = (T.n20[:, 24 * k:24 * k + 20] for k in range(len(N20)))
    hh, lt, vq, ea, r16, iom = (T.n48[:, P * k:P * k + P] for k in range(len(N48)))
    es = T.t1[:, 3 * TS:3 * TS + P]
    UB = 104
    gd = T.gd[:, 0:GT:3]

    def slot(buf, a, step=240, h=0, n=20): return buf[:, a + 2400 * h:a + 2400 * h + 240 * n - step + 1:step]

    mv, lap = slot(T.cw, 225), slot(T.cw, 145)
    ra, vw, e4, np_, k2 = (slot(T.vw, a) for a in (177, 225, 321, 369, 289))
    nk, nz = T.lab[:, 3:100:5], T.lab[:, 4:100:5]
    e2 = T.ee[:, 2:60:3]
    HID, T1S, T1A = DW, DW + R * NT + P, FL - 32
    qd, mask, hs = (T.tm[:, T1S + 80 + P * k:T1S + 80 + P * k + P] for k in range(3))
    tmk = "tm tm2 hid zero t1s1 t1s2 qd mask hs t1a t1b idx"

    dma("y", T.szb[:, 0:3], T.sz[:], "", "szb")
    dma("s", T.ub[:], T.u[:], "", "ub", SLOW[1] * 0.45)
    dma("y", T.x0[:, 0:4 * QH], T.x[:, 0:4 * QH], "", "x0a", SLOW[1] * 0.8)
    dma("s", T.x0[:, 4 * QH:4 * C], T.x[:, 4 * QH:4 * C], "", "x0b", SLOW[1])

    add("v", lambda: V.memset(T.ones[:], 1.0), "", "ones", cy(128))
    iota(T.ip[:, 0:2], [[15, 2]], 0, 1, "ip", False)
    iota(T.tm[:, 0:DW], [[1, DW]], 0, 0, "tm")
    iota(T.j20[:], [[16, 20]], 0, 0, "j20")
    iota(T.jm[:, 0:NT], [[0, NT // 16], [1, 16]], 0, 0, "jm")
    if flip: iota(qd, [[-1, 12], [0, 4]], 11, 0, "qd")
    else: iota(qd, [[1, 12], [0, 4]], 0, 0, "qd")
    iota(T.tm[:, HID:HID + R * NT], [[1, R * NT]], C, 0, "hid")
    iota(hs, [[int(KEY), P]], int(KEY + HC), 0, "hs")
    iota(T.dl[:, 0:36], [[1, 6], [DN, 6]], 6, 0, "dl")
    fill(T.ow[:, 0:C + 1], -BIG, "ow", C + 1)
    for t in ANEW[1:]: fill(T.fw[:, OW * (t - 1):OW * (t - 1) + C + 1], -BIG, "fw%d" % t, C + 1)
    fill(T.th[:], NONE - 100 - HC, "th", 3 * TS)
    for h in range(2): fill(T.eye[:, 256 * h:256 * h + 256], 0.0, "ey%d" % h, 256, True)
    fill(T.eye[:, 512:528], 0.0, "ey2", 16)
    add("g", lambda: g.affine_select(T.eye[:, 3:515:4], T.ones[:, 0:128], [[1, 128]], Op.is_equal, 0.0, 0, -1), "ones ey0 ey1 ey2", "eye", 0.17 + 256 * CYC)
    add("g", lambda: g.affine_select(T.r12[:], T.ones[:, 0:GW], [[0, 20], [1, M]], Op.not_equal, 0.0, 0, 0), "ones", "r12", 0.67)
    fill(T.sw_[:, C + 1:376], -1e29, "swz", 375 - C)
    fill(T.sw_[:, 0:1], -1e29, "swy", 1)
    fill(T.rs2[:], 0.0, "rs2", GT, True)
    fill(T.rs2[:, 0:GT:P], -2 * BIG, "rs2", 3)
    fill(T.t1[:, 3 * TS + P:4 * TS], 192.49, "esz", 4)
    fill(T.tm[:, T1S - P:T1S + 32], 0.0, "zero", 80)
    fill(T.tm[:, T1S + P:T1S + 80], -1.0, "t1s2", 32)
    for k, (a, v) in enumerate(((65, 0.0), (81, 0.0), (129, -1.0), (177, 1.0), (273, 1.0))): fill(slot(T.cw, a), v, "cz%d" % k, 20)
    fill(slot(T.vw, 209), 48.0 / MV, "ea0", 20)
    fill(slot(T.vw, 273), -MID, "l1", 20)
    fill(T.gd[:, 0:GT + 27:3], BIG, "gd", P + 9)
    r0, r1, per = RJ + DN - P, RJ - 4 * P, DN * P
    fill(T.rj[:, r0:r0 + 6 * per - P + 1:P], 1.0, "rj0 rj1 rk0 rk1 rk2", 6 * DN)
    fill(T.rj[:, r1:r1 + 6 * per - P + 1:P], 1.0, "rj0 rj1 rk3 rk4 rk5 rk6 rk7 rk8", 6 * DN)
    for k, (a, v) in enumerate(((r0, 0.0), (r0 + 4 * P, -1.0), (r0 + 7 * P, 4.0), (r1 + P, -209.0),
                                (r1 + 2 * P, R512), (r1 + 3 * P, -R512), (r1 + 5 * P, RND), (r1 + 6 * P, -RND), (r1 + 7 * P, -4.0))):
        fill(T.rj[:, a:a + 5 * per + 1:per], v, "rk%d" % k, 6)
    for k, v in enumerate((0.0, 900.0, -1.0, BIG)): fill(T.t1[:, P + k:3 * TS:TS], v, "t1s%d" % (k + 3), 3)
    fill(T.d1[:], -1.0, "d1", GW, True)
    for t in range(R): fill(X[t][:, 4 * C:4 * HB], 0.0, "x%dz" % t, 16)
    fill(T.dd[:, 4 * C:4 * HB], 0.0, "ddz", 16)
    iota(T.odd[:], [[0, NT], [1, 2]], 0, 0, "odd")
    add("g", lambda: g.iota(T.tm[:, FL:FL + DW], [[1, DW]], 0, 0, allow_small_or_imprecise_dtypes=True), "tm", "tm2", 0.13 + 2 * DW * CYC,
        more=[("s", lambda: S.activation(T.tm[:, FL:FL + DW], T.tm[:, 0:DW], Act.Copy), cy(DW)),
              ("v", lambda: V.tensor_copy(T.tm[:, FL:FL + DW], T.tm[:, 0:DW]), cy(DW))])
    for b in range(4):
        act(T.pool[:, PW * b:PW * b + C], T.x0[:, b:4 * C:4], xkeys(0, 0, C), "p%d" % b, 64.0, c=cy(C), cv=cy(C // 2))
    ts(T.ip[:, 2:4], T.ip[:, 0:2], 15, Op.bitwise_and, None, None, "ip", "ip1")
    cp(col[:, 0:2], T.ip[:, 2:4], "ip1", "ci")
    act(c16, ci, "ci", "c16", -OFF, 15 * OFF)
    act(cq, ci, "ci", "cq", sg, 15.0 * flip)
    act(c63, ci, "ci", "c63", -OFF * 63 / 64, 15 * OFF * 63 / 64)
    act(c36, cm, "ci", "c36", 1.0, 36.0)
    ts(csp, cm, 12.0, Op.is_ge, c36, Op.mult, "ci c36", "csp")
    ts(T.jm[:, 0:NT], T.jm[:, 0:NT], ci, Op.is_equal, BIG, Op.mult, "jm ci", "jm")
    act(T.wpa[:, 0:NT], T.jm[:, 0:NT], "jm", "wpa", 1.0, -OFF, cy(NT), cv=cy(64))
    act(T.wpa[:, NT:2 * NT], T.wpa[:, 0:NT], "wpa", "wpb", c=cy(NT), cv=cy(64))
    act(T.wpa[:, 2 * NT:C], T.wpa[:, 0:C - 2 * NT], "wpa wpb", "wpc", c=cy(128), cv=cy(64))
    ts(T.tm[:, T1A:T1A + 16], T.tm[:, 0:16], cq, Op.is_equal, 4097.0, Op.mult, "tm cq", "t1a")
    ts(T.tm[:, T1A + 16:FL], T.tm[:, 0:16], cq, Op.is_ge, None, None, "tm cq", "t1b")
    tt(T.tm[:, T1S + 32:T1S + P], T.tm[:, T1A:T1A + 16], T.tm[:, T1A + 16:FL], Op.subtract, "t1a t1b", "t1s1")
    cp(T.upk[:], T.j20[:, 0:8], "j20", "upk")
    act(T.crp[:, 0:R * 64], T.ones[:, 0:R * 64], "ones c16", "crp0 crp1 crp2", 0.0, c16, cy(R * 64), cv=cy(R * 32))
    act(T.crp[:, R * 64:R * 64 + 16], T.ones[:, 0:16], "ones c16", "crs", MV, c16)
    act(T.tu[:, 0:1], c16, "c16", "enz")
    act(T.tu[:, UB:UB + 1], c16, "c16", "ubz", 1.0, -MID)
    act(r16, T.ones[:, 0:P], "ones c16", "r16", 0.0, c16)
    act(iom, T.tm[:, DW - 1:DW - 1 - P:-1], "tm c16", "iom", 1.0, c16)
    act(T.base[:], T.j20[:, 0:4], "j20 csp", "base", TS / 16, csp)
    act(T.jw[:], T.j20[:], "j20 ci", "jw", 1.0, ci)
    for k in range(2): act(T.th[:, P + k:3 * TS:TS], T.jw[:, 0:3], "jw th", "thz%d" % k, 1.0, NONE + P * k - HC)
    add("g", lambda: g.iota(T.slw[:, 1:C + 1], [[1, C]], 0, 0, allow_small_or_imprecise_dtypes=True), "tm", "slw", 0.13 + 2 * C * CYC,
        more=[("s", lambda: S.activation(T.slw[:, 1:C + 1], T.tm[:, 0:C], Act.Copy), cy(C)),
              ("v", lambda: V.tensor_copy(T.slw[:, 1:C + 1], T.tm[:, 0:C]), cy(C))])
    act(T.qc[:, 0:3], T.jw[:, 0:3], "jw c16", "qc", -sg * KEY, c16)
    act(T.qc[:, 0:3], T.qc[:, 0:3], "qc", "qc", -1.0, 513 + 47 * KEY * flip - 192 * LAP)
    act(T.qc[:, 4:7], T.jw[:, 0:3], "jw", "zq", -sg / 48, -47.0 * flip / 48)
    pick(T.dl[:, P:80], T.wpa[:, 0:32], T.dl[:, 0:32], "wpa dl", "dl2", 0.067)
    ts(T.dlo[:], T.dl[:, P + 15:80:16], c16, Op.add, None, None, "dl2 c16", "dlo")
    quant(T.qu0[:], T.su0[:], T.ub[:], "ub", "qu0")
    add("s", lambda: S.activation(T.su[:], T.su0[:].indirect(T.upk[:]), Act.Copy), "qu0 upk", "su", ga(128))
    cp(T.qu[:].bitcast(dt.uint32), T.qu0[:].bitcast(dt.uint32).indirect(T.upk[:]), "qu0 upk", "qu", ga(128))
    ts(mask, qd, cm, Op.not_equal, -2e29, Op.mult, "qd ci", "mask")
    for b in range(4):
        quant(T.qe[:, 128 * b:128 * b + 128], T.se[:, 128 * b:128 * b + 128], T.eye[:, 3 - b:515 - b], "eye", "qe%d" % b)
    cp(T.idx[:, 0:3], T.szb[:, 0:3], "szb", "idx")

    idx = T.idx[:, 0:3]
    un = T.tu[:, P + 1:2 * P + 1]
    pe, pn = ((3 * P + 45, 45) if flip else (45, 3 * P + 45))
    sizp = T.pww[:, pn:pn + 97:48]
    act(T.pww[:, pe + 16:pe + 113:48], T.jw[:, 0:3], "jw", "dum", 1.0, C + 1.0)
    act(T.pww[:, pe + 32:pe + 129:48], T.jw[:, 0:3], "jw", "dum2", 1.0, C + 2.0 + P)

    def sizes(t):
        win, wk = (T.tm[:], tmk) if t >= 0 else (T.tm[:, 0:DW], "tm idx")
        if t + 1 < R and t + 1 not in ANEW:
            act(rev(T.tu, P + 1), win.indirect(idx), wk + " c16", "un", 1.0 - EPS, c16, ga(P))
            act(rev(T.tu, UB + 1), win.indirect(idx), wk + " c16", "ub2", -EPS, c16, ga(P))
            scan(T.tu[:, 1:P + 1], un, T.tu[:, UB:UB + P], c16, Op.add, Op.subtract, "un ub2 ubz c16", "en")
        else:
            act(rev(T.tu, P + 1, t >= 0), win.indirect(idx), wk + " c16", "un", 1.0, c16, ga(P))
            scan(T.tu[:, 1:P + 1], un, r16, c16, Op.add, Op.subtract, "un r16 c16", "en")

    def places(both):
        pick(T.pww[:, 0:3 * NT:3], T.wpa[:, 0:NT], rev(T.tu, 1, n=NT), "wpa en un", "pww", cy(NT))
        for k in range(1 + both):
            f6 = T.gd[:, GT + 3 + 3 * k:GT + 27:9]
            add("s", lambda f6=f6, k=k: S.activation(f6, sizp, Act.Relu, bias=2048.0 + 4096 * k, scale=-4096.0), "pww gd", "f6" + "ab"[k], 0.067,
                more=[("v", lambda f6=f6, k=k: V.tensor_scalar(f6, sizp, 0.5 + k, 2048.0, Op.is_lt, Op.mult), 0.067)])
        scan(T.gd[:, 26:155:16], T.gd[:, GT:GT + 27:3], T.pww[:, pe:pe + 129:16], 0.0, Op.add, Op.min, "pww f6a f6b dum dum2 gd", "l9")
        cp(T.lo[:, 0:3], T.gd[:, 42:GT:P], "l9", "lo")
        if both: ts(T.lo[:, 3:6], T.gd[:, 58:155:P], -1.0, Op.add, None, None, "l9", "lo2")

    def tables(e):
        plus(T.n48[:, 4 * P - 1:3 * P - 1:-1], T.n48[:, 6 * P - 1:5 * P - 1:-1], T.tu[:, 2 * P:P:-1], Op.subtract, "iom un", "ea")
        act(es, ea, "ea", "es", -1.0 / 48, 191.5 + (DW - 0.18) / 48)
        act(T.sc[:, 0:3], sizp, "pww", "sc", -e, FL - 1.0)
        act(T.gd[:, 0:GT:P], sizp, "pww gd", "t1n", 11.0 * e, 2292 - 12 * (FL - 1) - GS)
        act(T.gd[:, 45:GT:P], sizp, "pww gd", "own1", 4096.0, -6144.0)
        plus(hh, T.tu[:, 0:P], hs, Op.subtract, "en enz hs", "hh")
        for c in range(3):
            a = T1S + (16 * c if flip else 32 - 16 * c)
            ht, kt, tr = (buf[:, P * c:P * c + P] for buf in (T.ht, T.kt, T.tr))
            act(ht, es, "es zq", "ht%d" % c, 1.0, T.qc[:, 4 + c:5 + c])
            act(kt, ht, "ht%d qc" % c, "kt%d" % c, LAP, T.qc[:, c:c + 1])
            plus(T.th[:, TS * c:TS * c + P], kt, hh, Op.add, "kt%d hh th" % c, "th%d" % c)
            act(tr, T.tm[:, a:a + P], "sc zero t1s1 t1s2", "tr%d" % c, -1.0, T.sc[:, c:c + 1], f=Act.Relu)
            tt(T.t1[:, TS * c:TS * c + P], tr, ht, Op.subtract, "tr%d ht%d" % (c, c), "t1%d" % c, cy(96))

    def first_labels(t):
        fw, fk = (T.fw[:, OW * (t - 1):OW * t], "fw%d" % t) if t else (T.ow[:], "ow")
        fill(mv, 64.0, "cw0 cw1", 20)
        act(e4, T.jw[:], "jw", "e4", -1.0, KEY + HC + 64 * MID)
        act(vq, hh, "hh c63", "vq", 1.0 / 64, c63)
        cp(fw.indirect(T.lo[:, 0:3]), rev(T.n48, 2 * P), "vq lo " + fk, fk, sca(P))
        scan(T.mr[:, C - 1::-1], fw[:, C:0:-1], fw[:, C:0:-1], -BIG, Op.max, Op.max, fk, "mr", cy(C))
        pick(T.vw[:, 0:15 * C:15], T.wpa[:], T.mr[:], "wpa wpb wpc mr", "vw0 vw1", cy(C))
        act(T.pib[:], vw, "vw0 vw1", "pib", -64.0 / KEY, 191.15 - HC / KEY)
        act(ra, T.pib[:], "pib", "ra", -KEY / 64, 192 * KEY / 64)
        act(T.d1[:, 0:GW:M], vw, "vw0 vw1 d1", "d1", -16.0 / KEY, 192 - 0.586 - HC / KEY / 4)
        ts(T.po[:], T.pib[:], -192.0, Op.add, None, None, "pib", "po")

    def next_labels():
        act(T.pib[:], e2, "ee0 ee1", "pib", -1.0, 192.0)
        ts(ra, vw, RND, Op.add, RND, Op.subtract, "vw0 vw1", "ra")
        act(T.d1[:, 0:GW:M], e2, "ee0 ee1 d1", "d1", -0.25, 192 - 0.425)
        ts(T.po[:], e2, -1.0, Op.mult, None, None, "ee0 ee1", "po")

    def labels(first):
        act(np_, T.pib[:], "pib", "np", -1.0, 192.0)
        scan(T.lab[:], slot(T.cw, 81, 48), slot(T.vw, 177, 48), 0.0, Op.mult, Op.add, "cz1 cz2 cz3 cz4 cw0 cw1 l1 ra vw0 vw1 e4 np", "kk", cy(100))
        act(lap, nz, "kk", "lap", -1.0 / 48, 191.5 + 1.5 / 48)
        act(k2, nk, "kk", "k2", 1.0 / MV, -(192 * 48.0 + 1.4) / MV)
        scan(T.v1[:], T.r12[:], T.d1[:], 0.0, Op.mult, Op.add, "r12 d1", "v1", cy(GW // 2))
        if first: ts(T.inc[:], T.v1[:], 191.0, Op.is_equal, None, None, "v1", "inc", cy(GW))
        else:
            act(T.ab[:], T.v1[:], "v1", "ab", 1.0, -191.0, cy(GW), Act.Abs)
            act(T.inc[:], T.ab[:], "ab", "inc", -1.0, 1.0, cy(GW), Act.Relu)
        act(T.inc[:, 0:GW:M], nz, "kk inc", "inc", -1.0 / 48, 1.0 / 48 - 1)
        scan(T.yg[:], T.r12[:], T.inc[:], 0.0, Op.mult, Op.add, "r12 inc", "yg", cy(GW))

    def pack(t, wq, ws, wk, out, ok):
        qx, sx = (T["qx%d" % t], T["sx%d" % t]) if t < R else (T.qx, T.sx)
        for h, a, n in ((0, 0, QH), (1, QH, C - QH)):
            nm = "ab"[h]
            quant(qx[:, a:a + n], sx[:, a:a + n], X[t][:, 4 * a:4 * a + 4 * n], xkeys(t, a, a + n) + " qxa3" * (t == R and h), "qx%s%d" % (nm, t), n)
            mm(h, n, wq, ws, qx[:, a:a + n], sx[:, a:a + n], wk + " qx%s%d" % (nm, t))
            act(out(a, n), T.ps[:, 512 * h:512 * h + n], "ps%d" % h, ok + nm + " ps%d" % h, c=cy(n))

    sizes(-1)
    places(False)
    tables(1.0)
    first_labels(0)
    labels(True)
    old, new = "slw", "ow"
    for t in range(R):
        xk = xkeys(t, 0, C) + " x%dz" % t
        pack(t, T.qu[:], T.su[:], "qu su", lambda a, n: T.sw_[:, 1 + a:1 + a + n], "sw")
        qx, sx, ql, sl = T["qx%d" % t], T["sx%d" % t], T["ql%d" % t], T["sl%d" % t]
        for h, a, z in ((0, 0, QH), (1, QH, C)):
            arr, nm = T.sem["ar%s%d" % ("ab"[h], t)], "ab"[h]
            na = send(ql[:, a:z].bitcast(dt.uint8), qx[:, a:z].bitcast(dt.uint8), arr, t, "qx%s%d" % (nm, t), "r0" + nm, "R")
            if h == 0: na += send(sl[:], sx[:], arr, t, "qxa%d qxb%d" % (t, t), "r1", "r")
            add("p", lambda arr=arr, n=na: g.tensor.wait_ge(arr, n), "r0b qla%d" % t if h else "r0a r1", "ql%s%d" % (nm, t), 0.0, "w")
            for b in range(4):
                k = 4 - 4 * h + b
                mm(k, z - a, T.qe[:, 128 * b:128 * b + 128], T.se[:, 128 * b:128 * b + 128], ql[:, a:z], sl[:, a:z], "qe%d ql%s%d" % (b, nm, t))
                act(T.dd[:, 4 * a + b:4 * z:4], T.ps[:, 512 * k:512 * k + z - a], "ps%d" % k, "dd%s%d ps%d" % (nm, b, k), c=cy(z - a))
        tt(T.mk[:], T.sw_[:].indirect(T.lo[:, 0:3]), mask, Op.add, "swa swb swz swy lo mask", "mk", ga(P))
        scan(T.rm[:], rev(T.mk, 0), rev(T.mk, 0), -2e29, Op.max, Op.max, "mk", "rm")
        add("s", lambda: S.activation(lt, T.rm[:], Act.Sign, bias=T.rm[:, P - 1:P], scale=-1.0, accum_out=T.pc[:, 0:1]), "rm", "lt pc", 0.09)
        ts(T.pm[:], T.base[:], T.pc[:, 0:1], Op.add, None, None, "pc base", "pm")
        if t == 0:
            dma("y", T.qw[:, 0:256].bitcast(dt.uint8), T.wc[:, 0:1024], "lt", "qw0", 0.8)
            dma("y", T.sw[:], T.ws[:], "lt", "sw", 0.8)
        crp = T.crp[:, 64 * t:64 * t + 64]
        cp(crp.indirect(T.pm[:, 0:1]), T.crp[:, R * 64:R * 64 + 16], "pm crs crp%d" % t, "crp%d" % t, sca(16))
        pm64 = T.pm[:, 0:3]
        act(T.gg[:], T.t1[:].indirect(T.pm[:]), "t1s3 t1s4 t1s5 t1s6 t10 t11 t12 es esz pm", "gg", c=ga(64))
        scan(T.gt[:, 0:GT:3], T.gg[:, 0:P], gd, 0.0, Op.add, Op.min, "gg gd t1n l9 own1", "gs")
        ts(idx, T.gt[:, 39:GT:P], -1.0, Op.mult, 0.1 - GS, Op.add, "gs", "idx")
        act(T.gt[:, 1:GT:3], T.th[:].indirect(pm64), "th thz0 thz1 th0 th1 th2 pm", "g1", 1.0, HC, ga(P))
        act(T.gt[:, 2:GT:3], T.th[:].indirect(pm64), "th thz0 thz1 th0 th1 th2 pm", "g2", 1.0, HC - LAP, ga(P))
        a, b = RJ + DN * (GT - 1), RJ + DN * GT
        scan(T.rj[:, a:RJ - 1:-DN], T.rs2[:], T.gt[:, GT - 1::-1], 0.0, Op.add, Op.max, "rs2 g1 g2 gs", "rj0", cy(GT))
        scan(T.rj[:, b + DN * (GT - 2):b - 1:-DN], T.gt[:, GT - 2::-1], T.rj[:, a:RJ + DN - 1:-DN], NONE, Op.max, Op.min, "rj0 g1 g2 gs", "rj1", cy(GT))
        scan(T.dec[:, 0:6 * DN], T.rj[:, r0:r0 + 6 * per - P + 1:P], T.rj[:, r1:r1 + 6 * per - P + 1:P], 0.0, Op.mult, Op.add,
             "rj0 rj1 rk0 rk1 rk2 rk3 rk4 rk5 rk6 rk7 rk8", "dec", cy(6 * DN))
        lm, lp, lis = T["lm%d" % t], T["lp%d" % t], T.sem["lis%d" % t]
        ts(lm[:], T.dec[:, 0:6 * DN].indirect(T.dlo[:]), 4.0 * C + 3, Op.min, None, None, "dec dlo", "lm%d" % t, ga(32))
        nl = send(lp[:], lm[:, 6:30], lis, t, "lm%d" % t, "r3", "r")
        if t == 0:
            dma("y", T.qw[:, 256:512].bitcast(dt.uint8), T.wc[:, 1024:2048], "lm0", "qw1", 0.8)
        if t == 1:
            dma("y", T.vb[:], T.v[:], "lm1", "vb", 0.8)
            quant(T.qv[:], T.sv[:], T.vb[:], "vb", "qv")
        for h in range(2):
            act(T.ta[:, 4 * NT * h:4 * NT * h + 4 * NT:2], X[t][:, 0:4 * HB].indirect(lm[:, 6 + 12 * h:18 + 12 * h]), "lm%d " % t + xk, "ta%d" % h, c=ga(2 * NT))
        act(T.a64[:], T.ta[:, 0:8 * NT:2], "ta0 ta1", "a64", 64.0, c=cy(384), cv=cy(192))
        sizes(t)
        for h in range(2):
            a = HALF * h
            act(T.cg[:, a:a + HALF], crp.indirect(T.po[:, 10 * h:10 * h + 10]), "crp%d po" % t, "cg%d" % h, c=ga(HALF))
            pick(T.cw[:, 15 * a:15 * a + 15 * HALF:15], T.wpa[:, 0:HALF], T.cg[:, a:a + HALF], "wpa wpb cg%d" % h, "cw%d" % h, cy(HALF // 2))
            scan(T.ee[:, 30 * h:30 * h + 30], slot(T.cw, 65, 80, h, 10), slot(T.vw, 209, 80, h, 10), 0.0, Op.mult, Op.add, "cw%d cz0 lap k2 np ea0" % h, "ee%d" % h)
            ts(T.vo[:, 10 * h:10 * h + 10], T.ee[:, 30 * h + 2:30 * h + 30:3], -1.0, Op.mult, 0.3, Op.add, "ee%d" % h, "vo%d" % h)
            act(T.val[:, a:a + HALF], T.tu[:, 0:P + 1].indirect(T.vo[:, 10 * h:10 * h + 10]), "en enz vo%d" % h, "val%d" % h, c=ga(HALF))
            pick(T.vw[:, 15 * a:15 * a + 15 * HALF:15], T.wpa[:, 0:HALF], T.val[:, a:a + HALF], "wpa wpb val%d" % h, "vw%d" % h, cy(HALF))
        for m in range(M):
            act(T.wg[:, m:GW:M], T.yg[:, m:GW:M], "yg gg", "wg%d" % m, -1.0, T.gg[:, P + m + 1:P + m + 2])
        add("v", lambda: V.tensor_scalar(T.wr[:], T.wg[:], -192.0, 0.0, Op.add, Op.max), " ".join("wg%d" % m for m in range(M)), "wr", cy(GW // 2),
            more=[("s", lambda: S.activation(T.wr[:], T.wg[:], Act.Relu, bias=-192.0, scale=1.0), cy(GW))])
        scan(T.rr[:], T.r12[:], T.wr[:], 0.0, Op.mult, Op.add, "r12 wr", "rr", cy(GW // 2))
        tt(e3, nk, mv, Op.add, "cw0 cw1 kk", "e3")
        tt(e4, e3, T.rr[:, M - 1:GW:M], Op.min, "e3 rr", "e4")
        tt(e6, vw, e4, Op.subtract, "vw0 vw1 e4", "e6")
        ts(T.do[:], e6, 1.0, Op.add, None, None, "e6", "do")
        hid = T.tm[:, HID + NT * t:HID + NT * t + NT]
        if t in ANEW: cp(T[old][:].indirect(lm[:, 0:6]), hid, "lm%d hid %s" % (t, old), old, sca(NT))
        cp(T[new][:].indirect(T.do[:]), T[old][:, 1:C + 1], "do %s %s" % (old, new), new, sca(C))
        if t not in ANEW or t < R - 1: places(t not in ANEW)
        if t not in ANEW: cp(T[new][:].indirect(T.lo[:, 0:6]), hid, "lo lo2 hid " + new, new, sca(NT))
        pick(T.oww[:], T.wpa[:], T[new][:, 1:C + 1], "wpa wpb wpc " + new, "oww", cy(C))
        ts(T.xo[:], T.oww[:, 15:C:16], c16, Op.add, None, None, "oww c16", "xo")
        if t + 1 in ANEW:
            tables(1.0)
            first_labels(t + 1)
            labels(False)
            old, new = new, old
        elif t < R - 1:
            if t not in ANEW: act(T[old][:, 1:C + 1], T[new][:, 0:C + 1].indirect(T.do[:]), "do " + new, old, c=ga(C))
            next_labels()
            labels(False)
            tables(1.0 / (1.0 - EPS))
        else:
            dma("y", T.oz[:], T.tu[15:128:16, P + 1:2 * P + 1], "un", "oz")
        add("s", lambda lis=lis, n=nl: S.wait_ge(lis, n), "r3", "lp%d" % t, 0.0, "w")
        for h in range(2):
            add("s", lambda h=h, lp=lp: S.activation(T.ta[:, 4 * NT * h + 1:4 * NT * h + 4 * NT:2], T.dd[:].indirect(lp[:, 12 * h:12 + 12 * h]), Act.Copy),
                "dda0 dda1 dda2 dda3 ddb0 ddb1 ddb2 ddb3 ddz lp%d" % t, "td%d" % h, ga(2 * NT))
        for b in range(4):
            scan(T.tb[:, b:8 * NT:4], T.odd[:], T.ta[:, 2 * NT * b:2 * NT * b + 2 * NT], 0.0, Op.mult, Op.add, "odd ta%d td%d" % (b // 2, b // 2), "tb%d" % b, cy(NT))
        quant(T.qb[:], T.sb[:], T.tb[:], "tb0 tb1 tb2 tb3", "qb", 2 * NT)
        for b in range(4):
            mm(b, 2 * NT, T.qw[:, 128 * b:128 * b + 128], T.sw[:, 128 * b:128 * b + 128], T.qb[:], T.sb[:], "qw%d sw qb" % (b // 2))
        h0 = C + NT * t
        for b in range(4):
            tt(T.pool[:, PW * b + h0:PW * b + h0 + NT], T.ps[:, 512 * b + 1:512 * b + 2 * NT:2], T.a64[:, NT * b:NT * b + NT], Op.add,
               "a64 ps%d" % b, "h%d%d ps%d" % (t, b, b), cy(NT))
        for k, (b, a, z) in enumerate(XP):
            hk = "xo p%d " % b + " ".join("h%d%d" % (r, b) for r in range(t + 1))
            act(X[t + 1][:, 4 * a + b:4 * z:4], T.pool[:, PW * b:PW * b + h0 + NT].indirect(T.xo[:, a // 16:z // 16]), hk,
                "x%d_%d" % (t + 1, k), 0.015625, c=ga(z - a))

    pack(R, T.qv[:], T.sv[:], "qv", lambda a, n: T.yb[:, a:a + n], "yb")
    dma("y", T.oc[:, 0:4 * QH], T.qx[:, 0:QH].bitcast(dt.uint8), "qxa3", "oca", 1.0)
    dma("y", T.oc[:, 4 * QH:4 * C], T.qx[:, QH:C].bitcast(dt.uint8), "qxb3", "ocb", 0.7)
    for k in range(4):
        dma("ys"[k % 2], T.osc[4 * k:4 * k + 4, :], T.sx[32 * k:32 * k + 4, :], "qxa3 qxb3", "osc%d" % k)
    dma("y", T.y[:, 0:QH], T.yb[:, 0:QH], "yba", "ya", 0.2)
    dma("s", T.y[:, QH:C], T.yb[:, QH:C], "ybb", "yb")
    add("g", lambda: g.wait_ge(T.sem.sent, nsent[0]), "r0a r0b r1 r3", "", 0.0, "w")
    emit(ops, g, T)
